import numpy as np
import ml_dtypes


def mxq(x, axis, fmt="e4m3"):
    dtype, down = {"e4m3": (ml_dtypes.float8_e4m3fn, 7), "e5m2": (ml_dtypes.float8_e5m2, 14)}[fmt]
    v = np.moveaxis(np.asarray(x, np.float32).astype(ml_dtypes.bfloat16).astype(np.float64), axis, -1)
    blocks = v.reshape(v.shape[:-1] + (-1, 32))
    amax = np.abs(blocks).max(-1, keepdims=True)
    byte = np.maximum(np.where(amax > 0, np.frexp(amax)[1] - 1 + 127, 0) - down, 1)
    scale = np.exp2(byte - 127.0)
    codes = (blocks / scale).astype(np.float32).astype(dtype).astype(np.float64)
    return np.moveaxis((codes * scale).reshape(v.shape), -1, axis)


WIDE = False


def mx_kscale(k):
    if not WIDE:
        return np.ones(k)
    levels = np.array([18, -18])
    if k % 512:
        return np.exp2(np.random.permutation(np.resize(levels, k // 32))).repeat(32)
    a = np.empty((k // 512, 16))
    for p in range(k // 512):
        a[p, :8] = np.random.permutation(np.resize(levels, 8))
        for g in range(8):
            far = levels[np.abs(levels - a[p, g]) >= 10]
            a[p, g + 8] = far[np.random.randint(len(far))]
    return np.exp2(a.ravel()).repeat(32)


def f64(x):
    return np.asarray(x).astype(np.float64)


def striped(idx):
    return np.tile(np.asarray(idx).reshape(-1, 16).T, (8, 1)).astype(np.uint16)


def unstriped(offs):
    return offs[:16].T.reshape(-1).astype(np.int64)


E2M1 = np.array([0.0, 0.5, 1.0, 1.5, 2.0, 3.0, 4.0, 6.0, -0.0, -0.5, -1.0, -1.5, -2.0, -3.0, -4.0, -6.0])


def pack_weight(w, fmt):
    k, n = w.shape
    w = f64(np.asarray(w, np.float32).astype(ml_dtypes.bfloat16)).reshape(k // 32, 32, n)
    amax = np.abs(w).max(1)
    if fmt == "e4m3":
        byte = np.frexp(amax)[1] - 1 + 127 - 7
    else:
        mant, ex = np.frexp(amax / 6.0)
        byte = np.where(mant > 0.5, ex, ex - 1) + 127
    byte = np.clip(np.where(amax > 0, byte, 1), 1, 254)
    scaled = (w * np.exp2(127.0 - byte)[:, None, :]).reshape(k, n).astype(np.float32)
    by_word = np.ascontiguousarray(scaled.reshape(k // 512, 128, 4, n).transpose(0, 1, 3, 2))
    if fmt == "e4m3":
        words = by_word.astype(ml_dtypes.float8_e4m3fn).view(np.uint8)
    else:
        c = by_word.astype(ml_dtypes.float4_e2m1fn).view(np.uint8) & 0xF
        words = (c[..., 0::2] | (c[..., 1::2] << 4)).reshape(k // 512, 128, 2 * n)
    return np.ascontiguousarray(words), np.ascontiguousarray(byte.astype(np.uint8).reshape(k // 512, 16, n))


def unpack_weight(words, scales, fmt):
    g, _, n = scales.shape
    words = np.ascontiguousarray(words).reshape(g, 128, n, -1)
    if fmt == "e4m3":
        vals = words.view(ml_dtypes.float8_e4m3fn).astype(np.float64)
    else:
        nib = np.empty((g, 128, n, 4), np.uint8)
        nib[..., 0::2] = words & 0xF
        nib[..., 1::2] = words >> 4
        vals = E2M1[nib]
    vals = vals * np.repeat(np.exp2(scales.astype(np.float64) - 127.0), 8, axis=1)[..., None]
    return vals.transpose(0, 1, 3, 2).reshape(g * 512, n)


B, N, T, D, R = 1, 512, 2048, 1024, 512


def setup_inputs():
    n = np.random.standard_normal
    idx = np.random.permutation(T)[:B * N]
    s = mx_kscale(D)[:, None]
    z = mx_kscale(R)[:, None]
    x = n((B, D, R))
    wp = pack_weight(n((D, T)) * (1.00 / np.sqrt(D)) / s, "e2m1")
    return {
        "xT": (x * s).astype(np.float32),
        "w_words": np.ascontiguousarray(wp[0].reshape(1, 2, 128, T, 2).transpose(0, 2, 3, 1, 4)).reshape(1, 128, T, 4),
        "w_scales": wp[1],
        "y": (2 * np.random.randint(0, 2, (B, R, N)) - 1).astype(np.float32),
        "wt": (np.random.uniform(0.5, 1.5, (B, R, 1)) * 1.0 / np.sqrt(R) * z).astype(np.float32),
        "xm": (x.transpose(0, 2, 1) / z).astype(np.float32),
        "offs": striped(idx),
    }


def reference(xT, w_words, w_scales, y, wt, xm, offs):
    idx = unstriped(offs)
    w = unpack_weight(w_words.reshape(1, 128, T, 2, 2).transpose(0, 3, 1, 2, 4).reshape(2, 128, 2 * T), w_scales, "e2m1")
    pick = lambda x: x[:, idx].reshape(x.shape[0], B, N).transpose(1, 0, 2)
    a = mxq(f64(xT), 1, "e4m3").transpose(0, 2, 1) @ pick(w)
    g = -f64(wt) * f64(y) / (1.0 + np.exp(f64(y) * a))
    dw = mxq(f64(xm), 1, "e4m3").transpose(0, 2, 1) @ mxq(g, 1, "e5m2")
    gw = np.zeros((D, T))
    gw[:, idx] = dw.transpose(1, 0, 2).reshape(D, B * N)
    return gw

@@ -1,0 +1,193 @@
+from contextlib import ExitStack
+
+import concourse.mybir as mybir
+
+N, T, D, R = 512, 2048, 1024, 512
+FLOPS = 2 * 2 * N * D * R
+
+F32 = mybir.dt.float32
+BF16 = mybir.dt.bfloat16
+I32 = mybir.dt.int32
+U32 = mybir.dt.uint32
+U16 = mybir.dt.uint16
+U8 = mybir.dt.uint8
+E4M3 = mybir.dt.float8_e4m3fn_x4
+E5M2 = mybir.dt.float8_e5m2_x4
+E2M1 = mybir.dt.float4_e2m1fn_x4
+MULT = mybir.AluOpType.mult
+SIGMOID = mybir.ActivationFunctionType.Sigmoid
+
+P = 128
+PACK = 4
+K_PASS = P * PACK
+PASSES = D // K_PASS
+LINE = 4
+D_TILES = D // P
+WINDOWS = 3
+
+
+def tile_attend_gsig_w_kernel(tc, xT, w_words, w_scales, y, wt, xm, offs, out):
+    nc = tc.nc
+    with ExitStack() as ctx:
+        keep = ctx.enter_context(tc.tile_pool(name="keep", bufs=1))
+        ring = ctx.enter_context(tc.tile_pool(name="ring", bufs=3))
+        score_psum = ctx.enter_context(tc.psum_pool(name="score_psum", bufs=1))
+        grad_psum = ctx.enter_context(tc.psum_pool(name="grad_psum", bufs=4))
+
+        offsets = keep.tile([P, N // 16], U16, name="offsets")
+        nc.sync.dma_start(offsets[:], offs)
+
+        warm_in = keep.tile([P, 1], F32, name="warm_in")
+        warm_out = keep.tile([P, 1], F32, name="warm_out")
+        nc.gpsimd.memset(warm_in[:], 0.0)
+        nc.scalar.activation(warm_out[:], warm_in[:], SIGMOID)
+
+        table_scales = keep.tile([P, PASSES * T], U8, name="table_scales")
+        nc.vector.memset(table_scales[:].bitcast(I32), 0)
+        table_words = keep.tile([P, T], I32, name="table_words")
+        nc.sync.dma_start(table_words[:], w_words[0].rearrange("p t b -> p (t b)").bitcast(I32))
+        for q in range(4):
+            nc.scalar.dma_start(
+                table_scales[32 * q : 32 * q + 4, :].bitcast(I32).rearrange("f (o t) -> f o t", o=PASSES),
+                w_scales[:, 4 * q : 4 * q + 4, :].rearrange("o f t -> f o t").bitcast(I32),
+            )
+
+        half_r = R // 2
+        x_raw = {}
+        for o in range(PASSES):
+            for h in range(2):
+                x_raw[o, h] = keep.tile([P, PACK, half_r], F32, name="x_raw%d%d" % (o, h))
+                nc.sync.dma_start(
+                    x_raw[o, h][:],
+                    xT[0, o * K_PASS : (o + 1) * K_PASS, h * half_r : (h + 1) * half_r].rearrange("(p t) r -> p t r", t=PACK),
+                )
+        xm_rows = xm[0].rearrange("(p t) d -> p t d", t=PACK)
+        xm_cuts = [0, 128, 512, 1024]
+        xm_raw = []
+
+        def load_xm(piece):
+            lo, hi = xm_cuts[piece], xm_cuts[piece + 1]
+            raw = keep.tile([P, PACK, hi - lo], F32, name="xm_raw%d" % piece)
+            nc.sync.dma_start(raw[:], xm_rows[:, :, lo:hi])
+            xm_raw.extend(raw[:, :, c : c + P] for c in range(0, hi - lo, P))
+
+        load_xm(0)
+        weights = keep.tile([P, PACK], F32, name="weights")
+        nc.sync.dma_start(weights[:], wt[0].rearrange("(p j) o -> p (j o)", j=PACK))
+        y_rows = y[0].rearrange("(p j) n -> p j n", j=PACK)
+        signs = []
+        for jj in range(2):
+            pair = keep.tile([P, 2, N], F32, name="signs%d" % jj)
+            nc.sync.dma_start(pair[:], y_rows[:, 2 * jj : 2 * jj + 2, :])
+            signs.extend([pair[:, 0, :], pair[:, 1, :]])
+        load_xm(1)
+        load_xm(2)
+
+        windows = []
+        for w in range(WINDOWS):
+            window = keep.tile([P, T], F32, name="window%d" % w)
+            nc.vector.memset(window[:].bitcast(I32), 0)
+            windows.append(window)
+
+        picked_words = keep.tile([P, N], U32, name="picked_words")
+        nc.vector.tensor_copy(picked_words[:], table_words[:].bitcast(U32).indirect(offsets[:]))
+        w_codes = keep.tile([P, PASSES, N], U16, name="w_codes", align_bytes=64)
+        nc.vector.tensor_copy(w_codes[:], picked_words[:].bitcast(U16).rearrange("p (n o) -> p o n", o=PASSES))
+        w_planes = []
+        for o in range(PASSES):
+            plane = keep.tile([P, N], U8, name="w_plane%d" % o, align_bytes=64)
+            nc.vector.tensor_copy(plane[:], table_scales[:, o * T : (o + 1) * T].indirect(offsets[:]))
+            w_planes.append(plane)
+
+        x_codes, x_planes = [], []
+        half_s = P // 2
+        for o in range(PASSES):
+            woven = keep.tile([P, PACK, P, PACK], BF16, name="x_woven%d" % o, align_bytes=64)
+            for h in range(2):
+                dst = woven[:, :, h * half_s : (h + 1) * half_s, :].rearrange("p j s t -> p s t j")
+                src = x_raw[o, h][:].rearrange("p t (s j) -> p s t j", j=PACK)
+                if h == 0:
+                    nc.scalar.copy(dst, src)
+                else:
+                    nc.vector.tensor_copy(dst, src)
+            codes = keep.tile([P, R], U32, name="x_codes%d" % o, align_bytes=64)
+            plane = keep.tile([P, R], U8, name="x_plane%d" % o, align_bytes=64)
+            flat = woven[:].rearrange("p j s t -> p (j s t)")
+            for jj in range(o + 1):
+                width = R // (o + 1)
+                cols = slice(jj * width, (jj + 1) * width)
+                nc.vector.quantize_mx(codes[:, cols].bitcast(E4M3), plane[:, cols], flat[:, jj * width * PACK : (jj + 1) * width * PACK])
+            x_codes.append(codes)
+            x_planes.append(plane)
+
+        banks = [score_psum.tile([P, N], F32, name="scores%d" % j) for j in range(PACK)]
+        for o in range(PASSES):
+            for j in range(PACK):
+                cols = slice(j * P, (j + 1) * P)
+                nc.tensor.matmul_mx(
+                    banks[j][:],
+                    lhsT=x_codes[o][:, cols].bitcast(E4M3),
+                    lhsT_scale=x_planes[o][:, cols],
+                    rhs=w_codes[:, o, :].bitcast(E2M1),
+                    rhs_scale=w_planes[o][:],
+                    start=(o == 0),
+                    stop=(o == PASSES - 1),
+                )
+
+        xm_codes = keep.tile([P, D], U32, name="xm_codes", align_bytes=64)
+        xm_plane = keep.tile([P, D], U8, name="xm_plane", align_bytes=64)
+
+        def quantise_xm(m):
+            woven = ring.tile([P, P, PACK], BF16, name="xm_woven", align_bytes=64)
+            nc.scalar.copy(
+                woven[:].rearrange("p (c i) t -> p c t i", i=LINE),
+                xm_raw[m].rearrange("p t (c i) -> p c t i", i=LINE),
+            )
+            cols = slice(m * P, (m + 1) * P)
+            nc.vector.quantize_mx(xm_codes[:, cols].bitcast(E4M3), xm_plane[:, cols], woven[:].rearrange("p c t -> p (c t)"))
+
+        quantise_xm(0)
+
+        margins = keep.tile([P, PACK, N], F32, name="margins")
+        sigmoids = keep.tile([P, PACK, N], F32, name="sigmoids")
+        factors = keep.tile([P, PACK, N], F32, name="factors")
+        half_n = N // 2
+        halves = [slice(0, half_n), slice(half_n, N)]
+        for j in range(PACK):
+            nc.gpsimd.tensor_scalar(factors[:, j, :], signs[j], weights[:, j : j + 1], -1.0, MULT, MULT)
+            for cols in halves if j == PACK - 1 else [slice(0, N)]:
+                nc.vector.tensor_tensor(margins[:, j, cols], banks[j][:, cols], signs[j][:, cols], MULT)
+                nc.scalar.activation(sigmoids[:, j, cols], margins[:, j, cols], SIGMOID, scale=-1.0)
+
+        g_woven = keep.tile([P, N, PACK], BF16, name="g_woven", align_bytes=64)
+        g_codes = keep.tile([P, N], U32, name="g_codes", align_bytes=64)
+        g_plane = keep.tile([P, N], U8, name="g_plane", align_bytes=64)
+        for cols in halves:
+            nc.vector.tensor_tensor(
+                g_woven[:, cols, :].rearrange("p (c i) j -> p c j i", i=LINE),
+                sigmoids[:, :, cols].rearrange("p j (c i) -> p c j i", i=LINE),
+                factors[:, :, cols].rearrange("p j (c i) -> p c j i", i=LINE),
+                MULT,
+            )
+        for cols in halves:
+            nc.vector.quantize_mx(g_codes[:, cols].bitcast(E5M2), g_plane[:, cols], g_woven[:, cols, :].rearrange("p n j -> p (n j)"))
+
+        for m in range(D_TILES):
+            cols = slice(m * P, (m + 1) * P)
+            bank = grad_psum.tile([P, N], F32, name="grad")
+            nc.tensor.matmul_mx(
+                bank[:],
+                lhsT=xm_codes[:, cols].bitcast(E4M3),
+                lhsT_scale=xm_plane[:, cols],
+                rhs=g_codes[:].bitcast(E5M2),
+                rhs_scale=g_plane[:],
+                start=True,
+                stop=True,
+            )
+            columns = ring.tile([P, N], F32, name="columns")
+            nc.scalar.copy(columns[:], bank[:])
+            if m + 1 < D_TILES:
+                quantise_xm(m + 1)
+            window = windows[m % WINDOWS]
+            nc.vector.tensor_copy(window[:].indirect(offsets[:]), columns[:])
+            nc.sync.dma_start(out[cols, :], window[:])

@@ -15,13 +15,14 @@ E4M3 = mybir.dt.float8_e4m3fn_x4
 E5M2 = mybir.dt.float8_e5m2_x4
 E2M1 = mybir.dt.float4_e2m1fn_x4
 MULT = mybir.AluOpType.mult
+ADD = mybir.AluOpType.add
 SIGMOID = mybir.ActivationFunctionType.Sigmoid
 
 P = 128
 PACK = 4
 K_PASS = P * PACK
 PASSES = D // K_PASS
-LINE = 4
+PAIR = 2
 D_TILES = D // P
 WINDOWS = 3
 
@@ -37,51 +38,33 @@ def tile_attend_gsig_w_kernel(tc, xT, w_words, w_scales, y, wt, xm, offs, out):
         offsets = keep.tile([P, N // 16], U16, name="offsets")
         nc.sync.dma_start(offsets[:], offs)
 
-        warm_in = keep.tile([P, 1], F32, name="warm_in")
-        warm_out = keep.tile([P, 1], F32, name="warm_out")
-        nc.gpsimd.memset(warm_in[:], 0.0)
-        nc.scalar.activation(warm_out[:], warm_in[:], SIGMOID)
-
-        table_scales = keep.tile([P, PASSES * T], U8, name="table_scales")
-        nc.vector.memset(table_scales[:].bitcast(I32), 0)
-        table_words = keep.tile([P, T], I32, name="table_words")
-        nc.sync.dma_start(table_words[:], w_words[0].rearrange("p t b -> p (t b)").bitcast(I32))
-        for q in range(4):
-            nc.scalar.dma_start(
-                table_scales[32 * q : 32 * q + 4, :].bitcast(I32).rearrange("f (o t) -> f o t", o=PASSES),
-                w_scales[:, 4 * q : 4 * q + 4, :].rearrange("o f t -> f o t").bitcast(I32),
-            )
-
-        half_r = R // 2
-        x_raw = {}
-        for o in range(PASSES):
-            for h in range(2):
-                x_raw[o, h] = keep.tile([P, PACK, half_r], F32, name="x_raw%d%d" % (o, h))
-                nc.sync.dma_start(
-                    x_raw[o, h][:],
-                    xT[0, o * K_PASS : (o + 1) * K_PASS, h * half_r : (h + 1) * half_r].rearrange("(p t) r -> p t r", t=PACK),
-                )
-        xm_rows = xm[0].rearrange("(p t) d -> p t d", t=PACK)
-        xm_cuts = [0, 128, 512, 1024]
-        xm_raw = []
-
-        def load_xm(piece):
-            lo, hi = xm_cuts[piece], xm_cuts[piece + 1]
-            raw = keep.tile([P, PACK, hi - lo], F32, name="xm_raw%d" % piece)
-            nc.sync.dma_start(raw[:], xm_rows[:, :, lo:hi])
-            xm_raw.extend(raw[:, :, c : c + P] for c in range(0, hi - lo, P))
-
-        load_xm(0)
         weights = keep.tile([P, PACK], F32, name="weights")
         nc.sync.dma_start(weights[:], wt[0].rearrange("(p j) o -> p (j o)", j=PACK))
+        table_words = keep.tile([P, T], I32, name="table_words")
+        nc.sync.dma_start(table_words[:], w_words[0].rearrange("p t b -> p (t b)").bitcast(I32))
+        table_scales = keep.tile([P, T], U8, name="table_scales")
+        nc.gpsimd.memset(table_scales[:].bitcast(I32), 0)
+        for f in range(4):
+            nc.sync.dma_start(table_scales[f:P:32, :].bitcast(I32), w_scales[0, f:16:4, :].bitcast(I32))
+        nc.sync.dma_start(table_scales[4:P:8, :].bitcast(I32), w_scales[1].bitcast(I32))
+        moved_plane = keep.tile([P, N], U8, name="moved_plane", align_bytes=64)
+        nc.gpsimd.memset(moved_plane[:].bitcast(I32), 0)
+
+        def load_rows(rows, name):
+            raw = keep.tile([P, PACK, rows.shape[1]], F32, name=name)
+            nc.sync.dma_start(raw[:], rows.rearrange("(p t) c -> p t c", t=PACK))
+            return raw
+
+        x_raw = [load_rows(xT[0, o * K_PASS : (o + 1) * K_PASS, :], "x_raw%d" % o) for o in range(PASSES)]
         y_rows = y[0].rearrange("(p j) n -> p j n", j=PACK)
         signs = []
-        for jj in range(2):
-            pair = keep.tile([P, 2, N], F32, name="signs%d" % jj)
-            nc.sync.dma_start(pair[:], y_rows[:, 2 * jj : 2 * jj + 2, :])
-            signs.extend([pair[:, 0, :], pair[:, 1, :]])
-        load_xm(1)
-        load_xm(2)
+        for first in range(0, PACK, PAIR):
+            two = keep.tile([P, PAIR, N], F32, name="signs%d" % first)
+            nc.sync.dma_start(two[:], y_rows[:, first : first + PAIR, :])
+            signs.extend(two[:, e, :] for e in range(PAIR))
+
+        negated = keep.tile([P, PACK], F32, name="negated")
+        nc.gpsimd.tensor_scalar(negated[:], weights[:], -1.0, 0.0, MULT, ADD)
 
         windows = []
         for w in range(WINDOWS):
@@ -91,34 +74,36 @@ def tile_attend_gsig_w_kernel(tc, xT, w_words, w_scales, y, wt, xm, offs, out):
 
         picked_words = keep.tile([P, N], U32, name="picked_words")
         nc.vector.tensor_copy(picked_words[:], table_words[:].bitcast(U32).indirect(offsets[:]))
+        picked_scales = keep.tile([P, N], U8, name="picked_scales", align_bytes=64)
+        nc.vector.tensor_copy(picked_scales[:], table_scales[:].indirect(offsets[:]))
+        for f in range(4):
+            nc.scalar.dma_start(moved_plane[f:P:32, :].bitcast(I32), picked_scales[4 + 8 * f : P : 32, :].bitcast(I32))
+        w_planes = [picked_scales, moved_plane]
         w_codes = keep.tile([P, PASSES, N], U16, name="w_codes", align_bytes=64)
         nc.vector.tensor_copy(w_codes[:], picked_words[:].bitcast(U16).rearrange("p (n o) -> p o n", o=PASSES))
-        w_planes = []
-        for o in range(PASSES):
-            plane = keep.tile([P, N], U8, name="w_plane%d" % o, align_bytes=64)
-            nc.vector.tensor_copy(plane[:], table_scales[:, o * T : (o + 1) * T].indirect(offsets[:]))
-            w_planes.append(plane)
 
-        x_codes, x_planes = [], []
-        half_s = P // 2
-        for o in range(PASSES):
+        x_codes = [keep.tile([P, R], U32, name="x_codes%d" % o, align_bytes=64) for o in range(PASSES)]
+        x_planes = [keep.tile([P, R], U8, name="x_plane%d" % o, align_bytes=64) for o in range(PASSES)]
+
+        def quantise_x(o, cuts):
             woven = keep.tile([P, PACK, P, PACK], BF16, name="x_woven%d" % o, align_bytes=64)
-            for h in range(2):
-                dst = woven[:, :, h * half_s : (h + 1) * half_s, :].rearrange("p j s t -> p s t j")
-                src = x_raw[o, h][:].rearrange("p t (s j) -> p s t j", j=PACK)
-                if h == 0:
-                    nc.scalar.copy(dst, src)
-                else:
-                    nc.vector.tensor_copy(dst, src)
-            codes = keep.tile([P, R], U32, name="x_codes%d" % o, align_bytes=64)
-            plane = keep.tile([P, R], U8, name="x_plane%d" % o, align_bytes=64)
-            flat = woven[:].rearrange("p j s t -> p (j s t)")
-            for jj in range(o + 1):
-                width = R // (o + 1)
-                cols = slice(jj * width, (jj + 1) * width)
-                nc.vector.quantize_mx(codes[:, cols].bitcast(E4M3), plane[:, cols], flat[:, jj * width * PACK : (jj + 1) * width * PACK])
-            x_codes.append(codes)
-            x_planes.append(plane)
+            for copy, first in ((nc.vector.tensor_copy, 0), (nc.scalar.copy, PAIR)):
+                copy(
+                    woven[:, first : first + PAIR, :, :].rearrange("p j s t -> p s t j"),
+                    x_raw[o][:].rearrange("p t (s j) -> p s t j", j=PACK)[:, :, :, first : first + PAIR],
+                )
+            for lo, hi in zip(cuts[:-1], cuts[1:]):
+                cols = slice(lo * P, hi * P)
+                nc.vector.quantize_mx(
+                    x_codes[o][:, cols].bitcast(E4M3),
+                    x_planes[o][:, cols],
+                    woven[:, lo:hi, :, :].rearrange("p j s t -> p (j s t)"),
+                )
+
+        quantise_x(0, (0, 2, 4))
+        xm_raw = [load_rows(xm[0, :, : D // 2], "x_raw0")]
+        quantise_x(1, (0, 1, 2, 4))
+        xm_raw.append(load_rows(xm[0, :, D // 2 :], "x_raw1"))
 
         banks = [score_psum.tile([P, N], F32, name="scores%d" % j) for j in range(PACK)]
         for o in range(PASSES):
@@ -134,50 +119,66 @@ def tile_attend_gsig_w_kernel(tc, xT, w_words, w_scales, y, wt, xm, offs, out):
                     stop=(o == PASSES - 1),
                 )
 
-        xm_codes = keep.tile([P, D], U32, name="xm_codes", align_bytes=64)
-        xm_plane = keep.tile([P, D], U8, name="xm_plane", align_bytes=64)
-
-        def quantise_xm(m):
-            woven = ring.tile([P, P, PACK], BF16, name="xm_woven", align_bytes=64)
-            nc.scalar.copy(
-                woven[:].rearrange("p (c i) t -> p c t i", i=LINE),
-                xm_raw[m].rearrange("p t (c i) -> p c t i", i=LINE),
-            )
-            cols = slice(m * P, (m + 1) * P)
-            nc.vector.quantize_mx(xm_codes[:, cols].bitcast(E4M3), xm_plane[:, cols], woven[:].rearrange("p c t -> p (c t)"))
-
-        quantise_xm(0)
-
-        margins = keep.tile([P, PACK, N], F32, name="margins")
+        margins = keep.tile([P, PACK, N], F32, name="margins", align_bytes=64)
         sigmoids = keep.tile([P, PACK, N], F32, name="sigmoids")
-        factors = keep.tile([P, PACK, N], F32, name="factors")
+        factors = keep.tile([P, PACK, N], F32, name="factors", align_bytes=64)
         half_n = N // 2
         halves = [slice(0, half_n), slice(half_n, N)]
         for j in range(PACK):
-            nc.gpsimd.tensor_scalar(factors[:, j, :], signs[j], weights[:, j : j + 1], -1.0, MULT, MULT)
+            nc.gpsimd.tensor_scalar(factors[:, j, :], signs[j], negated[:, j : j + 1], 0.0, MULT, ADD)
+        for j in range(PACK):
             for cols in halves if j == PACK - 1 else [slice(0, N)]:
                 nc.vector.tensor_tensor(margins[:, j, cols], banks[j][:, cols], signs[j][:, cols], MULT)
                 nc.scalar.activation(sigmoids[:, j, cols], margins[:, j, cols], SIGMOID, scale=-1.0)
+
+        xm_plane = keep.tile([P, D], U8, name="xm_plane", align_bytes=64)
+
+        def weave_xm(woven, m):
+            cols = slice(m % 4 * P, (m % 4 + 1) * P)
+            nc.scalar.copy(
+                woven[:, cols, :].rearrange("p (c i) t -> p c t i", i=PAIR),
+                xm_raw[m // 4][:, :, cols].rearrange("p t (c i) -> p c t i", i=PAIR),
+            )
+
+        xm_codes = {}
+
+        def quantise_xm(codes, woven, first, count):
+            lo = first % 4 * P
+            nc.vector.quantize_mx(
+                codes.bitcast(E4M3),
+                xm_plane[:, first * P : (first + count) * P],
+                woven[:, lo : lo + count * P, :].rearrange("p c t -> p (c t)"),
+            )
+            for c in range(count):
+                xm_codes[first + c] = codes[:, c * P : (c + 1) * P]
+
+        xm_low = keep.tile([P, D // 2, PACK], BF16, name="xm_low", tag="margins", align_bytes=64)
+        first_codes = keep.tile([P, P], U32, name="first_codes", align_bytes=64)
+        weave_xm(xm_low, 0)
+        quantise_xm(first_codes[:], xm_low, 0, 1)
 
         g_woven = keep.tile([P, N, PACK], BF16, name="g_woven", align_bytes=64)
         g_codes = keep.tile([P, N], U32, name="g_codes", align_bytes=64)
         g_plane = keep.tile([P, N], U8, name="g_plane", align_bytes=64)
         for cols in halves:
             nc.vector.tensor_tensor(
-                g_woven[:, cols, :].rearrange("p (c i) j -> p c j i", i=LINE),
-                sigmoids[:, :, cols].rearrange("p j (c i) -> p c j i", i=LINE),
-                factors[:, :, cols].rearrange("p j (c i) -> p c j i", i=LINE),
+                g_woven[:, cols, :].rearrange("p (c i) j -> p c j i", i=PAIR),
+                sigmoids[:, :, cols].rearrange("p j (c i) -> p c j i", i=PAIR),
+                factors[:, :, cols].rearrange("p j (c i) -> p c j i", i=PAIR),
                 MULT,
             )
         for cols in halves:
             nc.vector.quantize_mx(g_codes[:, cols].bitcast(E5M2), g_plane[:, cols], g_woven[:, cols, :].rearrange("p n j -> p (n j)"))
+
+        later_codes = keep.tile([P, D - P], U32, name="later_codes", tag="factors", align_bytes=64)
+        xm_high = keep.tile([P, D // 2, PACK], BF16, name="xm_high", tag="g_woven", align_bytes=64)
 
         for m in range(D_TILES):
             cols = slice(m * P, (m + 1) * P)
             bank = grad_psum.tile([P, N], F32, name="grad")
             nc.tensor.matmul_mx(
                 bank[:],
-                lhsT=xm_codes[:, cols].bitcast(E4M3),
+                lhsT=xm_codes[m].bitcast(E4M3),
                 lhsT_scale=xm_plane[:, cols],
                 rhs=g_codes[:].bitcast(E5M2),
                 rhs_scale=g_plane[:],
@@ -186,8 +187,15 @@ def tile_attend_gsig_w_kernel(tc, xT, w_words, w_scales, y, wt, xm, offs, out):
             )
             columns = ring.tile([P, N], F32, name="columns")
             nc.scalar.copy(columns[:], bank[:])
-            if m + 1 < D_TILES:
-                quantise_xm(m + 1)
+            if m == 0:
+                for k in range(1, 4):
+                    weave_xm(xm_low, k)
+                    quantise_xm(later_codes[:, (k - 1) * P : k * P], xm_low, k, 1)
+            if m == 1:
+                for k in range(4, D_TILES):
+                    weave_xm(xm_high, k)
+            if m == 2:
+                quantise_xm(later_codes[:, 3 * P :], xm_high, 4, 4)
             window = windows[m % WINDOWS]
             nc.vector.tensor_copy(window[:].indirect(offsets[:]), columns[:])
             nc.sync.dma_start(out[cols, :], window[:])

@@ -25,6 +25,7 @@ PASSES = D // K_PASS
 PAIR = 2
 D_TILES = D // P
 WINDOWS = 3
+SHIFTED = 112
 
 
 def tile_attend_gsig_w_kernel(tc, xT, w_words, w_scales, y, wt, xm, offs, out):
@@ -34,34 +35,43 @@ def tile_attend_gsig_w_kernel(tc, xT, w_words, w_scales, y, wt, xm, offs, out):
         ring = ctx.enter_context(tc.tile_pool(name="ring", bufs=3))
         score_psum = ctx.enter_context(tc.psum_pool(name="score_psum", bufs=1))
         grad_psum = ctx.enter_context(tc.psum_pool(name="grad_psum", bufs=4))
+        half_n = N // 2
+        halves = [slice(0, half_n), slice(half_n, N)]
+        half_r = R // 2
 
         offsets = keep.tile([P, N // 16], U16, name="offsets")
         nc.sync.dma_start(offsets[:], offs)
-
         weights = keep.tile([P, PACK], F32, name="weights")
-        nc.sync.dma_start(weights[:], wt[0].rearrange("(p j) o -> p (j o)", j=PACK))
+        nc.scalar.dma_start(weights[:], wt[0].rearrange("(p j) o -> p (j o)", j=PACK))
         table_words = keep.tile([P, T], I32, name="table_words")
         nc.sync.dma_start(table_words[:], w_words[0].rearrange("p t b -> p (t b)").bitcast(I32))
+
         table_scales = keep.tile([P, T], U8, name="table_scales")
-        nc.gpsimd.memset(table_scales[:].bitcast(I32), 0)
-        for f in range(4):
-            nc.sync.dma_start(table_scales[f:P:32, :].bitcast(I32), w_scales[0, f:16:4, :].bitcast(I32))
-        nc.sync.dma_start(table_scales[4:P:8, :].bitcast(I32), w_scales[1].bitcast(I32))
+        nc.vector.memset(table_scales[:].bitcast(I32), 0)
+        for q in range(4):
+            nc.sync.dma_start(
+                table_scales[32 * q : 32 * q + 8, :].bitcast(I32), w_scales[:, 4 * q : 4 * q + 4, :].bitcast(I32)
+            )
         moved_plane = keep.tile([P, N], U8, name="moved_plane", align_bytes=64)
-        nc.gpsimd.memset(moved_plane[:].bitcast(I32), 0)
+        nc.vector.memset(moved_plane[:].bitcast(I32), 0)
+        g_codes = keep.tile([P, N], U32, name="g_codes", align_bytes=64)
+        g_plane = keep.tile([P, N], U8, name="g_plane", align_bytes=64)
+        nc.vector.memset(g_codes[:, halves[1]].bitcast(I32), 0)
+        nc.vector.memset(g_plane[:, halves[1]].bitcast(I32), 0)
+        warm = keep.tile([P, 2], F32, name="warm")
+        nc.vector.memset(warm[:, 0:1], 0.0)
+        nc.scalar.activation(warm[:, 1:2], warm[:, 0:1], SIGMOID)
 
-        def load_rows(rows, name):
-            raw = keep.tile([P, PACK, rows.shape[1]], F32, name=name)
-            nc.sync.dma_start(raw[:], rows.rearrange("(p t) c -> p t c", t=PACK))
-            return raw
+        def load_rows(tile, rows):
+            nc.sync.dma_start(tile, rows.rearrange("(p t) c -> p t c", t=PACK))
 
-        x_raw = [load_rows(xT[0, o * K_PASS : (o + 1) * K_PASS, :], "x_raw%d" % o) for o in range(PASSES)]
-        y_rows = y[0].rearrange("(p j) n -> p j n", j=PACK)
-        signs = []
-        for first in range(0, PACK, PAIR):
-            two = keep.tile([P, PAIR, N], F32, name="signs%d" % first)
-            nc.sync.dma_start(two[:], y_rows[:, first : first + PAIR, :])
-            signs.extend(two[:, e, :] for e in range(PAIR))
+        x_first = keep.tile([P, PACK, R], F32, name="x_first")
+        load_rows(x_first[:], xT[0, :K_PASS, :])
+        x_second = []
+        for h in range(2):
+            part = keep.tile([P, PACK, half_r], F32, name="x_second%d" % h)
+            load_rows(part[:], xT[0, K_PASS:, h * half_r : (h + 1) * half_r])
+            x_second.append(part)
 
         negated = keep.tile([P, PACK], F32, name="negated")
         nc.gpsimd.tensor_scalar(negated[:], weights[:], -1.0, 0.0, MULT, ADD)
@@ -72,38 +82,54 @@ def tile_attend_gsig_w_kernel(tc, xT, w_words, w_scales, y, wt, xm, offs, out):
             nc.vector.memset(window[:].bitcast(I32), 0)
             windows.append(window)
 
-        picked_words = keep.tile([P, N], U32, name="picked_words")
-        nc.vector.tensor_copy(picked_words[:], table_words[:].bitcast(U32).indirect(offsets[:]))
         picked_scales = keep.tile([P, N], U8, name="picked_scales", align_bytes=64)
         nc.vector.tensor_copy(picked_scales[:], table_scales[:].indirect(offsets[:]))
-        for f in range(4):
-            nc.scalar.dma_start(moved_plane[f:P:32, :].bitcast(I32), picked_scales[4 + 8 * f : P : 32, :].bitcast(I32))
+        nc.scalar.dma_start(moved_plane[0:SHIFTED, :].bitcast(I32), picked_scales[4 : 4 + SHIFTED, :].bitcast(I32))
         w_planes = [picked_scales, moved_plane]
+        picked_words = keep.tile([P, N], U32, name="picked_words")
+        nc.vector.tensor_copy(picked_words[:], table_words[:].bitcast(U32).indirect(offsets[:]))
         w_codes = keep.tile([P, PASSES, N], U16, name="w_codes", align_bytes=64)
         nc.vector.tensor_copy(w_codes[:], picked_words[:].bitcast(U16).rearrange("p (n o) -> p o n", o=PASSES))
 
+        signs = keep.tile([P, PACK, N], F32, name="signs", tag="table_words")
+        y_rows = y[0].rearrange("(p j) n -> p j n", j=PACK)
+        for first in range(0, PACK, PAIR):
+            nc.sync.dma_start(signs[:, first : first + PAIR, :], y_rows[:, first : first + PAIR, :])
+
         x_codes = [keep.tile([P, R], U32, name="x_codes%d" % o, align_bytes=64) for o in range(PASSES)]
         x_planes = [keep.tile([P, R], U8, name="x_plane%d" % o, align_bytes=64) for o in range(PASSES)]
+        x_woven = [keep.tile([P, PACK, P, PACK], BF16, name="x_woven%d" % o, align_bytes=64) for o in range(PASSES)]
 
-        def quantise_x(o, cuts):
-            woven = keep.tile([P, PACK, P, PACK], BF16, name="x_woven%d" % o, align_bytes=64)
+        def weave_x(o, raw, places):
             for copy, first in ((nc.vector.tensor_copy, 0), (nc.scalar.copy, PAIR)):
                 copy(
-                    woven[:, first : first + PAIR, :, :].rearrange("p j s t -> p s t j"),
-                    x_raw[o][:].rearrange("p t (s j) -> p s t j", j=PACK)[:, :, :, first : first + PAIR],
+                    x_woven[o][:, first : first + PAIR, places, :].rearrange("p j s t -> p s t j"),
+                    raw[:].rearrange("p t (s j) -> p s t j", j=PACK)[:, :, :, first : first + PAIR],
                 )
+
+        def quantise_x(o, cuts):
             for lo, hi in zip(cuts[:-1], cuts[1:]):
                 cols = slice(lo * P, hi * P)
                 nc.vector.quantize_mx(
                     x_codes[o][:, cols].bitcast(E4M3),
                     x_planes[o][:, cols],
-                    woven[:, lo:hi, :, :].rearrange("p j s t -> p (j s t)"),
+                    x_woven[o][:, lo:hi, :, :].rearrange("p j s t -> p (j s t)"),
                 )
 
+        weave_x(0, x_first, slice(0, P))
         quantise_x(0, (0, 2, 4))
-        xm_raw = [load_rows(xm[0, :, : D // 2], "x_raw0")]
+        for h in range(2):
+            weave_x(1, x_second[h], slice(h * P // 2, (h + 1) * P // 2))
         quantise_x(1, (0, 1, 2, 4))
-        xm_raw.append(load_rows(xm[0, :, D // 2 :], "x_raw1"))
+
+        quarter = D // 4
+        xm_first = keep.tile([P, 2, PACK, quarter], F32, name="xm_first", tag="x_first")
+        xm_raw = [xm_first[:, 0], xm_first[:, 1]]
+        for h in range(2):
+            part = keep.tile([P, PACK, quarter], F32, name="xm_second%d" % h, tag="x_second%d" % h)
+            xm_raw.append(part[:])
+        for c in range(4):
+            load_rows(xm_raw[c], xm[0, :, c * quarter : (c + 1) * quarter])
 
         banks = [score_psum.tile([P, N], F32, name="scores%d" % j) for j in range(PACK)]
         for o in range(PASSES):
@@ -122,63 +148,48 @@ def tile_attend_gsig_w_kernel(tc, xT, w_words, w_scales, y, wt, xm, offs, out):
         margins = keep.tile([P, PACK, N], F32, name="margins", align_bytes=64)
         sigmoids = keep.tile([P, PACK, N], F32, name="sigmoids")
         factors = keep.tile([P, PACK, N], F32, name="factors", align_bytes=64)
-        half_n = N // 2
-        halves = [slice(0, half_n), slice(half_n, N)]
         for j in range(PACK):
-            nc.gpsimd.tensor_scalar(factors[:, j, :], signs[j], negated[:, j : j + 1], 0.0, MULT, ADD)
+            nc.gpsimd.tensor_scalar(factors[:, j, :], signs[:, j, :], negated[:, j : j + 1], 0.0, MULT, ADD)
         for j in range(PACK):
             for cols in halves if j == PACK - 1 else [slice(0, N)]:
-                nc.vector.tensor_tensor(margins[:, j, cols], banks[j][:, cols], signs[j][:, cols], MULT)
+                nc.vector.tensor_tensor(margins[:, j, cols], banks[j][:, cols], signs[:, j, cols], MULT)
                 nc.scalar.activation(sigmoids[:, j, cols], margins[:, j, cols], SIGMOID, scale=-1.0)
 
+        xm_woven = keep.tile([P, D, PACK], BF16, name="xm_woven", align_bytes=64)
+        xm_codes = keep.tile([P, D], U32, name="xm_codes", align_bytes=64)
         xm_plane = keep.tile([P, D], U8, name="xm_plane", align_bytes=64)
 
-        def weave_xm(woven, m):
-            cols = slice(m % 4 * P, (m % 4 + 1) * P)
-            nc.scalar.copy(
-                woven[:, cols, :].rearrange("p (c i) t -> p c t i", i=PAIR),
-                xm_raw[m // 4][:, :, cols].rearrange("p t (c i) -> p c t i", i=PAIR),
+        def weave_xm(copy, m):
+            copy(
+                xm_woven[:, m * P : (m + 1) * P, :].rearrange("p (c i) t -> p c t i", i=PAIR),
+                xm_raw[m // 2][:, :, m % 2 * P : (m % 2 + 1) * P].rearrange("p t (c i) -> p c t i", i=PAIR),
             )
 
-        xm_codes = {}
-
-        def quantise_xm(codes, woven, first, count):
-            lo = first % 4 * P
+        def quantise_xm(first, count):
+            cols = slice(first * P, (first + count) * P)
             nc.vector.quantize_mx(
-                codes.bitcast(E4M3),
-                xm_plane[:, first * P : (first + count) * P],
-                woven[:, lo : lo + count * P, :].rearrange("p c t -> p (c t)"),
+                xm_codes[:, cols].bitcast(E4M3), xm_plane[:, cols], xm_woven[:, cols, :].rearrange("p c t -> p (c t)")
             )
-            for c in range(count):
-                xm_codes[first + c] = codes[:, c * P : (c + 1) * P]
-
-        xm_low = keep.tile([P, D // 2, PACK], BF16, name="xm_low", tag="margins", align_bytes=64)
-        first_codes = keep.tile([P, P], U32, name="first_codes", align_bytes=64)
-        weave_xm(xm_low, 0)
-        quantise_xm(first_codes[:], xm_low, 0, 1)
 
         g_woven = keep.tile([P, N, PACK], BF16, name="g_woven", align_bytes=64)
-        g_codes = keep.tile([P, N], U32, name="g_codes", align_bytes=64)
-        g_plane = keep.tile([P, N], U8, name="g_plane", align_bytes=64)
-        for cols in halves:
+
+        def form_g(cols):
             nc.vector.tensor_tensor(
                 g_woven[:, cols, :].rearrange("p (c i) j -> p c j i", i=PAIR),
                 sigmoids[:, :, cols].rearrange("p j (c i) -> p c j i", i=PAIR),
                 factors[:, :, cols].rearrange("p j (c i) -> p c j i", i=PAIR),
                 MULT,
             )
-        for cols in halves:
+
+        def quantise_g(cols):
             nc.vector.quantize_mx(g_codes[:, cols].bitcast(E5M2), g_plane[:, cols], g_woven[:, cols, :].rearrange("p n j -> p (n j)"))
 
-        later_codes = keep.tile([P, D - P], U32, name="later_codes", tag="factors", align_bytes=64)
-        xm_high = keep.tile([P, D // 2, PACK], BF16, name="xm_high", tag="g_woven", align_bytes=64)
-
-        for m in range(D_TILES):
+        def multiply(m, slots):
             cols = slice(m * P, (m + 1) * P)
             bank = grad_psum.tile([P, N], F32, name="grad")
             nc.tensor.matmul_mx(
                 bank[:],
-                lhsT=xm_codes[m].bitcast(E4M3),
+                lhsT=xm_codes[:, cols].bitcast(E4M3),
                 lhsT_scale=xm_plane[:, cols],
                 rhs=g_codes[:].bitcast(E5M2),
                 rhs_scale=g_plane[:],
@@ -186,16 +197,27 @@ def tile_attend_gsig_w_kernel(tc, xT, w_words, w_scales, y, wt, xm, offs, out):
                 stop=True,
             )
             columns = ring.tile([P, N], F32, name="columns")
-            nc.scalar.copy(columns[:], bank[:])
-            if m == 0:
-                for k in range(1, 4):
-                    weave_xm(xm_low, k)
-                    quantise_xm(later_codes[:, (k - 1) * P : k * P], xm_low, k, 1)
-            if m == 1:
-                for k in range(4, D_TILES):
-                    weave_xm(xm_high, k)
-            if m == 2:
-                quantise_xm(later_codes[:, 3 * P :], xm_high, 4, 4)
-            window = windows[m % WINDOWS]
-            nc.vector.tensor_copy(window[:].indirect(offsets[:]), columns[:])
-            nc.sync.dma_start(out[cols, :], window[:])
+            nc.scalar.copy(columns[:, slots], bank[:, slots])
+            return columns
+
+        def scatter(m, columns, slots):
+            listed = offsets[:, slots.start // 16 : slots.stop // 16]
+            nc.vector.tensor_copy(windows[m % WINDOWS][:].indirect(listed), columns[:, slots])
+
+        form_g(halves[0])
+        weave_xm(nc.vector.tensor_copy, 0)
+        quantise_g(halves[0])
+        quantise_xm(0, 1)
+        early = multiply(0, halves[0])
+        form_g(halves[1])
+        quantise_g(halves[1])
+        scatter(0, early, halves[0])
+        groups = {1: 1, 2: 2, 4: 4}
+        for m in range(D_TILES):
+            slots = halves[1] if m == 0 else slice(0, N)
+            if m in groups:
+                for k in range(m, m + groups[m]):
+                    weave_xm(nc.scalar.copy, k)
+                quantise_xm(m, groups[m])
+            scatter(m, multiply(m, slots), slots)
+            nc.sync.dma_start(out[m * P : (m + 1) * P, :], windows[m % WINDOWS][:])

@@ -26,13 +26,14 @@ PAIR = 2
 D_TILES = D // P
 WINDOWS = 3
 SHIFTED = 112
+EARLY = 2
 
 
 def tile_attend_gsig_w_kernel(tc, xT, w_words, w_scales, y, wt, xm, offs, out):
     nc = tc.nc
     with ExitStack() as ctx:
         keep = ctx.enter_context(tc.tile_pool(name="keep", bufs=1))
-        ring = ctx.enter_context(tc.tile_pool(name="ring", bufs=3))
+        ring = ctx.enter_context(tc.tile_pool(name="ring", bufs=4))
         score_psum = ctx.enter_context(tc.psum_pool(name="score_psum", bufs=1))
         grad_psum = ctx.enter_context(tc.psum_pool(name="grad_psum", bufs=4))
         half_n = N // 2
@@ -91,7 +92,7 @@ def tile_attend_gsig_w_kernel(tc, xT, w_words, w_scales, y, wt, xm, offs, out):
         w_codes = keep.tile([P, PASSES, N], U16, name="w_codes", align_bytes=64)
         nc.vector.tensor_copy(w_codes[:], picked_words[:].bitcast(U16).rearrange("p (n o) -> p o n", o=PASSES))
 
-        signs = keep.tile([P, PACK, N], F32, name="signs", tag="table_words")
+        signs = keep.tile([P, PACK, N], F32, name="signs", tag="table_scales")
         y_rows = y[0].rearrange("(p j) n -> p j n", j=PACK)
         for first in range(0, PACK, PAIR):
             nc.sync.dma_start(signs[:, first : first + PAIR, :], y_rows[:, first : first + PAIR, :])
@@ -155,20 +156,22 @@ def tile_attend_gsig_w_kernel(tc, xT, w_words, w_scales, y, wt, xm, offs, out):
                 nc.vector.tensor_tensor(margins[:, j, cols], banks[j][:, cols], signs[:, j, cols], MULT)
                 nc.scalar.activation(sigmoids[:, j, cols], margins[:, j, cols], SIGMOID, scale=-1.0)
 
-        xm_woven = keep.tile([P, D, PACK], BF16, name="xm_woven", align_bytes=64)
         xm_codes = keep.tile([P, D], U32, name="xm_codes", align_bytes=64)
         xm_plane = keep.tile([P, D], U8, name="xm_plane", align_bytes=64)
 
-        def weave_xm(copy, m):
-            copy(
-                xm_woven[:, m * P : (m + 1) * P, :].rearrange("p (c i) t -> p c t i", i=PAIR),
-                xm_raw[m // 2][:, :, m % 2 * P : (m % 2 + 1) * P].rearrange("p t (c i) -> p c t i", i=PAIR),
+        def weave_xm(woven, m):
+            nc.scalar.copy(
+                woven[:, m % 4 * P : (m % 4 + 1) * P, :].rearrange("p (c i) t -> p c t i", i=PACK),
+                xm_raw[m // 2][:, :, m % 2 * P : (m % 2 + 1) * P].rearrange("p t (c i) -> p c t i", i=PACK),
             )
 
-        def quantise_xm(first, count):
+        def quantise_xm(woven, first, count):
             cols = slice(first * P, (first + count) * P)
+            lo = first % 4 * P
             nc.vector.quantize_mx(
-                xm_codes[:, cols].bitcast(E4M3), xm_plane[:, cols], xm_woven[:, cols, :].rearrange("p c t -> p (c t)")
+                xm_codes[:, cols].bitcast(E4M3),
+                xm_plane[:, cols],
+                woven[:, lo : lo + count * P, :].rearrange("p c t -> p (c t)"),
             )
 
         g_woven = keep.tile([P, N, PACK], BF16, name="g_woven", align_bytes=64)
@@ -204,20 +207,27 @@ def tile_attend_gsig_w_kernel(tc, xT, w_words, w_scales, y, wt, xm, offs, out):
             listed = offsets[:, slots.start // 16 : slots.stop // 16]
             nc.vector.tensor_copy(windows[m % WINDOWS][:].indirect(listed), columns[:, slots])
 
+        xm_low = keep.tile([P, D // 2, PACK], BF16, name="xm_low", tag="margins", align_bytes=64)
         form_g(halves[0])
-        weave_xm(nc.vector.tensor_copy, 0)
+        weave_xm(xm_low, 0)
+        quantise_xm(xm_low, 0, 1)
         quantise_g(halves[0])
-        quantise_xm(0, 1)
-        early = multiply(0, halves[0])
+        early = [multiply(0, halves[0])]
         form_g(halves[1])
+        weave_xm(xm_low, 1)
+        quantise_xm(xm_low, 1, 1)
+        early.append(multiply(1, halves[0]))
+        scatter(0, early[0], halves[0])
         quantise_g(halves[1])
-        scatter(0, early, halves[0])
-        groups = {1: 1, 2: 2, 4: 4}
+        scatter(1, early[1], halves[0])
+        xm_high = keep.tile([P, D // 2, PACK], BF16, name="xm_high", tag="g_woven", align_bytes=64)
+        groups = {2: (xm_low, 2), 4: (xm_high, 4)}
         for m in range(D_TILES):
-            slots = halves[1] if m == 0 else slice(0, N)
+            slots = halves[1] if m < EARLY else slice(0, N)
             if m in groups:
-                for k in range(m, m + groups[m]):
-                    weave_xm(nc.scalar.copy, k)
-                quantise_xm(m, groups[m])
+                woven, count = groups[m]
+                for k in range(m, m + count):
+                    weave_xm(woven, k)
+                quantise_xm(woven, m, count)
             scatter(m, multiply(m, slots), slots)
             nc.sync.dma_start(out[m * P : (m + 1) * P, :], windows[m % WINDOWS][:])

@@ -33,7 +33,7 @@ def tile_attend_gsig_w_kernel(tc, xT, w_words, w_scales, y, wt, xm, offs, out):
     nc = tc.nc
     with ExitStack() as ctx:
         keep = ctx.enter_context(tc.tile_pool(name="keep", bufs=1))
-        ring = ctx.enter_context(tc.tile_pool(name="ring", bufs=4))
+        ring = ctx.enter_context(tc.tile_pool(name="ring", bufs=6))
         score_psum = ctx.enter_context(tc.psum_pool(name="score_psum", bufs=1))
         grad_psum = ctx.enter_context(tc.psum_pool(name="grad_psum", bufs=4))
         half_n = N // 2
@@ -41,11 +41,11 @@ def tile_attend_gsig_w_kernel(tc, xT, w_words, w_scales, y, wt, xm, offs, out):
         half_r = R // 2
 
         offsets = keep.tile([P, N // 16], U16, name="offsets")
-        nc.sync.dma_start(offsets[:], offs)
         weights = keep.tile([P, PACK], F32, name="weights")
         nc.scalar.dma_start(weights[:], wt[0].rearrange("(p j) o -> p (j o)", j=PACK))
         table_words = keep.tile([P, T], I32, name="table_words")
         nc.sync.dma_start(table_words[:], w_words[0].rearrange("p t b -> p (t b)").bitcast(I32))
+        nc.sync.dma_start(offsets[:], offs)
 
         table_scales = keep.tile([P, T], U8, name="table_scales")
         nc.vector.memset(table_scales[:].bitcast(I32), 0)
@@ -77,11 +77,12 @@ def tile_attend_gsig_w_kernel(tc, xT, w_words, w_scales, y, wt, xm, offs, out):
         negated = keep.tile([P, PACK], F32, name="negated")
         nc.gpsimd.tensor_scalar(negated[:], weights[:], -1.0, 0.0, MULT, ADD)
 
-        windows = []
-        for w in range(WINDOWS):
-            window = keep.tile([P, T], F32, name="window%d" % w)
-            nc.vector.memset(window[:].bitcast(I32), 0)
-            windows.append(window)
+        def zeroed_window(engine, tag):
+            window = keep.tile([P, T], F32, name="window", tag=tag)
+            engine.memset(window[:].bitcast(I32), 0)
+            return window
+
+        windows = [zeroed_window(nc.vector, "window0"), zeroed_window(nc.gpsimd, "weights")]
 
         picked_scales = keep.tile([P, N], U8, name="picked_scales", align_bytes=64)
         nc.vector.tensor_copy(picked_scales[:], table_scales[:].indirect(offsets[:]))
@@ -92,19 +93,22 @@ def tile_attend_gsig_w_kernel(tc, xT, w_words, w_scales, y, wt, xm, offs, out):
         w_codes = keep.tile([P, PASSES, N], U16, name="w_codes", align_bytes=64)
         nc.vector.tensor_copy(w_codes[:], picked_words[:].bitcast(U16).rearrange("p (n o) -> p o n", o=PASSES))
 
-        signs = keep.tile([P, PACK, N], F32, name="signs", tag="table_scales")
+        signs = keep.tile([P, PACK, N], F32, name="signs", tag="table_words")
         y_rows = y[0].rearrange("(p j) n -> p j n", j=PACK)
         for first in range(0, PACK, PAIR):
             nc.sync.dma_start(signs[:, first : first + PAIR, :], y_rows[:, first : first + PAIR, :])
 
         x_codes = [keep.tile([P, R], U32, name="x_codes%d" % o, align_bytes=64) for o in range(PASSES)]
         x_planes = [keep.tile([P, R], U8, name="x_plane%d" % o, align_bytes=64) for o in range(PASSES)]
-        x_woven = [keep.tile([P, PACK, P, PACK], BF16, name="x_woven%d" % o, align_bytes=64) for o in range(PASSES)]
+        x_woven = [
+            [keep.tile([P, PAIR, P, PACK], BF16, name="x_woven%d_%d" % (o, e), align_bytes=64) for e in range(2)]
+            for o in range(PASSES)
+        ]
 
         def weave_x(o, raw, places):
             for copy, first in ((nc.vector.tensor_copy, 0), (nc.scalar.copy, PAIR)):
                 copy(
-                    x_woven[o][:, first : first + PAIR, places, :].rearrange("p j s t -> p s t j"),
+                    x_woven[o][first // PAIR][:, :, places, :].rearrange("p j s t -> p s t j"),
                     raw[:].rearrange("p t (s j) -> p s t j", j=PACK)[:, :, :, first : first + PAIR],
                 )
 
@@ -114,7 +118,7 @@ def tile_attend_gsig_w_kernel(tc, xT, w_words, w_scales, y, wt, xm, offs, out):
                 nc.vector.quantize_mx(
                     x_codes[o][:, cols].bitcast(E4M3),
                     x_planes[o][:, cols],
-                    x_woven[o][:, lo:hi, :, :].rearrange("p j s t -> p (j s t)"),
+                    x_woven[o][lo // PAIR][:, lo % PAIR : lo % PAIR + hi - lo, :, :].rearrange("p j s t -> p (j s t)"),
                 )
 
         weave_x(0, x_first, slice(0, P))
@@ -147,45 +151,51 @@ def tile_attend_gsig_w_kernel(tc, xT, w_words, w_scales, y, wt, xm, offs, out):
                 )
 
         margins = keep.tile([P, PACK, N], F32, name="margins", align_bytes=64)
-        sigmoids = keep.tile([P, PACK, N], F32, name="sigmoids")
+        sigmoids = keep.tile([P, PACK, N], F32, name="sigmoids", align_bytes=64)
         factors = keep.tile([P, PACK, N], F32, name="factors", align_bytes=64)
         for j in range(PACK):
             nc.gpsimd.tensor_scalar(factors[:, j, :], signs[:, j, :], negated[:, j : j + 1], 0.0, MULT, ADD)
+        windows.append(zeroed_window(nc.gpsimd, "negated"))
+
+        def margin(j, cols):
+            nc.vector.tensor_tensor(margins[:, j, cols], banks[j][:, cols], signs[:, j, cols], MULT)
+
+        def sigmoid(j, cols):
+            nc.scalar.activation(sigmoids[:, j, cols], margins[:, j, cols], SIGMOID, scale=-1.0)
+
         for j in range(PACK):
-            for cols in halves if j == PACK - 1 else [slice(0, N)]:
-                nc.vector.tensor_tensor(margins[:, j, cols], banks[j][:, cols], signs[:, j, cols], MULT)
-                nc.scalar.activation(sigmoids[:, j, cols], margins[:, j, cols], SIGMOID, scale=-1.0)
+            margin(j, slice(0, N) if j < PAIR else halves[0])
+            sigmoid(j, halves[0])
+        for j in range(PAIR, PACK):
+            margin(j, halves[1])
 
         xm_codes = keep.tile([P, D], U32, name="xm_codes", align_bytes=64)
         xm_plane = keep.tile([P, D], U8, name="xm_plane", align_bytes=64)
 
-        def weave_xm(woven, m):
+        woven = {}
+
+        def weave_xm(m):
             nc.scalar.copy(
-                woven[:, m % 4 * P : (m % 4 + 1) * P, :].rearrange("p (c i) t -> p c t i", i=PACK),
+                woven[m].rearrange("p (c i) t -> p c t i", i=PACK),
                 xm_raw[m // 2][:, :, m % 2 * P : (m % 2 + 1) * P].rearrange("p t (c i) -> p c t i", i=PACK),
             )
 
-        def quantise_xm(woven, first, count):
+        def quantise_xm(first, count, source):
             cols = slice(first * P, (first + count) * P)
-            lo = first % 4 * P
-            nc.vector.quantize_mx(
-                xm_codes[:, cols].bitcast(E4M3),
-                xm_plane[:, cols],
-                woven[:, lo : lo + count * P, :].rearrange("p c t -> p (c t)"),
-            )
-
-        g_woven = keep.tile([P, N, PACK], BF16, name="g_woven", align_bytes=64)
+            nc.vector.quantize_mx(xm_codes[:, cols].bitcast(E4M3), xm_plane[:, cols], source.rearrange("p c t -> p (c t)"))
 
         def form_g(cols):
+            g_woven = keep.tile([P, half_n, PACK], BF16, name="g_woven", align_bytes=64)
             nc.vector.tensor_tensor(
-                g_woven[:, cols, :].rearrange("p (c i) j -> p c j i", i=PAIR),
+                g_woven[:].rearrange("p (c i) j -> p c j i", i=PAIR),
                 sigmoids[:, :, cols].rearrange("p j (c i) -> p c j i", i=PAIR),
                 factors[:, :, cols].rearrange("p j (c i) -> p c j i", i=PAIR),
                 MULT,
             )
+            return g_woven
 
-        def quantise_g(cols):
-            nc.vector.quantize_mx(g_codes[:, cols].bitcast(E5M2), g_plane[:, cols], g_woven[:, cols, :].rearrange("p n j -> p (n j)"))
+        def quantise_g(cols, g_woven):
+            nc.vector.quantize_mx(g_codes[:, cols].bitcast(E5M2), g_plane[:, cols], g_woven[:].rearrange("p n j -> p (n j)"))
 
         def multiply(m, slots):
             cols = slice(m * P, (m + 1) * P)
@@ -207,27 +217,36 @@ def tile_attend_gsig_w_kernel(tc, xT, w_words, w_scales, y, wt, xm, offs, out):
             listed = offsets[:, slots.start // 16 : slots.stop // 16]
             nc.vector.tensor_copy(windows[m % WINDOWS][:].indirect(listed), columns[:, slots])
 
-        xm_low = keep.tile([P, D // 2, PACK], BF16, name="xm_low", tag="margins", align_bytes=64)
-        form_g(halves[0])
-        weave_xm(xm_low, 0)
-        quantise_xm(xm_low, 0, 1)
-        quantise_g(halves[0])
-        early = [multiply(0, halves[0])]
-        form_g(halves[1])
-        weave_xm(xm_low, 1)
-        quantise_xm(xm_low, 1, 1)
-        early.append(multiply(1, halves[0]))
-        scatter(0, early[0], halves[0])
-        quantise_g(halves[1])
-        scatter(1, early[1], halves[0])
-        xm_high = keep.tile([P, D // 2, PACK], BF16, name="xm_high", tag="g_woven", align_bytes=64)
-        groups = {2: (xm_low, 2), 4: (xm_high, 4)}
+        def spent(j, cols):
+            return margins[:, j, cols].bitcast(BF16).rearrange("p (c t) -> p c t", t=PACK)
+
+        woven[0], woven[1] = spent(3, halves[0]), spent(3, halves[1])
+        woven[2], woven[3] = spent(2, halves[0]), spent(2, halves[1])
+        weave_xm(0)
+        for j in range(PACK):
+            sigmoid(j, halves[1])
+        weave_xm(1)
+        quantise_g(halves[0], form_g(halves[0]))
+        quantise_xm(0, 1, woven[0])
+        early = multiply(0, halves[0])
+        quantise_g(halves[1], form_g(halves[1]))
+        quantise_xm(1, 1, woven[1])
+        scatter(0, early, halves[0])
+        later = keep.tile([P, D // 2, PACK], BF16, name="later", tag="sigmoids", align_bytes=64)
+        for m in range(4, D_TILES):
+            woven[m] = later[:, (m - 4) * P : (m - 3) * P, :]
+        ahead = {0: (2, 2, spent(2, slice(0, N))), 2: (4, 4, later[:])}
         for m in range(D_TILES):
-            slots = halves[1] if m < EARLY else slice(0, N)
-            if m in groups:
-                woven, count = groups[m]
-                for k in range(m, m + count):
-                    weave_xm(woven, k)
-                quantise_xm(woven, m, count)
-            scatter(m, multiply(m, slots), slots)
-            nc.sync.dma_start(out[m * P : (m + 1) * P, :], windows[m % WINDOWS][:])
+            slots = halves[1] if m == 0 else slice(0, N)
+            columns = multiply(m, slots)
+            if m in ahead:
+                first, count, source = ahead[m]
+                for k in range(first, first + count):
+                    weave_xm(k)
+                quantise_xm(first, count, source)
+            scatter(m, columns, slots)
+            if m < D_TILES - 1:
+                nc.sync.dma_start(out[m * P : (m + 1) * P, :], windows[m % WINDOWS][:])
+            else:
+                for queue, cols in ((nc.sync, slice(0, T // 2)), (nc.scalar, slice(T // 2, T))):
+                    queue.dma_start(out[m * P : (m + 1) * P, cols], windows[m % WINDOWS][:, cols])

@@ -66,13 +66,9 @@ def tile_attend_gsig_w_kernel(tc, xT, w_words, w_scales, y, wt, xm, offs, out):
         def load_rows(tile, rows):
             nc.sync.dma_start(tile, rows.rearrange("(p t) c -> p t c", t=PACK))
 
-        x_first = keep.tile([P, PACK, R], F32, name="x_first")
-        load_rows(x_first[:], xT[0, :K_PASS, :])
-        x_second = []
-        for h in range(2):
-            part = keep.tile([P, PACK, half_r], F32, name="x_second%d" % h)
-            load_rows(part[:], xT[0, K_PASS:, h * half_r : (h + 1) * half_r])
-            x_second.append(part)
+        x_raw = [keep.tile([P, PACK, R], F32, name="x_raw%d" % o) for o in range(PASSES)]
+        for o in range(PASSES):
+            load_rows(x_raw[o][:], xT[0, o * K_PASS : (o + 1) * K_PASS, :])
 
         negated = keep.tile([P, PACK], F32, name="negated")
         nc.gpsimd.tensor_scalar(negated[:], weights[:], -1.0, 0.0, MULT, ADD)
@@ -82,7 +78,7 @@ def tile_attend_gsig_w_kernel(tc, xT, w_words, w_scales, y, wt, xm, offs, out):
             engine.memset(window[:].bitcast(I32), 0)
             return window
 
-        windows = [zeroed_window(nc.vector, "window0"), zeroed_window(nc.gpsimd, "weights")]
+        windows = [zeroed_window(nc.vector, "window%d" % w) for w in range(3)] + [zeroed_window(nc.gpsimd, "weights")]
 
         picked_scales = keep.tile([P, N], U8, name="picked_scales", align_bytes=64)
         nc.vector.tensor_copy(picked_scales[:], table_scales[:].indirect(offsets[:]))
@@ -121,20 +117,18 @@ def tile_attend_gsig_w_kernel(tc, xT, w_words, w_scales, y, wt, xm, offs, out):
                     x_woven[o][lo // PAIR][:, lo % PAIR : lo % PAIR + hi - lo, :, :].rearrange("p j s t -> p (j s t)"),
                 )
 
-        weave_x(0, x_first, slice(0, P))
-        quantise_x(0, (0, 2, 4))
-        for h in range(2):
-            weave_x(1, x_second[h], slice(h * P // 2, (h + 1) * P // 2))
-        quantise_x(1, (0, 1, 2, 4))
+        for o, cuts in enumerate(((0, 2, 4), (0, 1, 2, 4))):
+            weave_x(o, x_raw[o], slice(0, P))
+            quantise_x(o, cuts)
 
         quarter = D // 4
-        xm_first = keep.tile([P, 2, PACK, quarter], F32, name="xm_first", tag="x_first")
-        xm_raw = [xm_first[:, 0], xm_first[:, 1]]
-        for h in range(2):
-            part = keep.tile([P, PACK, quarter], F32, name="xm_second%d" % h, tag="x_second%d" % h)
-            xm_raw.append(part[:])
-        for c in range(4):
-            load_rows(xm_raw[c], xm[0, :, c * quarter : (c + 1) * quarter])
+        xm_low = keep.tile([P, 2, PACK, quarter], F32, name="xm_low", tag="x_raw0")
+        xm_high = keep.tile([P, PACK, D // 2], F32, name="xm_high", tag="x_raw1")
+        for c in range(2):
+            load_rows(xm_low[:, c], xm[0, :, c * quarter : (c + 1) * quarter])
+        load_rows(xm_high[:], xm[0, :, D // 2 :])
+        xm_raw = [xm_low[:, m // 2, :, m % 2 * P : (m % 2 + 1) * P] for m in range(4)]
+        xm_raw.extend(xm_high[:, :, m * P : (m + 1) * P] for m in range(4))
 
         banks = [score_psum.tile([P, N], F32, name="scores%d" % j) for j in range(PACK)]
         for o in range(PASSES):
@@ -155,7 +149,6 @@ def tile_attend_gsig_w_kernel(tc, xT, w_words, w_scales, y, wt, xm, offs, out):
         factors = keep.tile([P, PACK, N], F32, name="factors", align_bytes=64)
         for j in range(PACK):
             nc.gpsimd.tensor_scalar(factors[:, j, :], signs[:, j, :], negated[:, j : j + 1], 0.0, MULT, ADD)
-        windows.append(zeroed_window(nc.gpsimd, "negated"))
 
         def margin(j, cols):
             nc.vector.tensor_tensor(margins[:, j, cols], banks[j][:, cols], signs[:, j, cols], MULT)
@@ -177,7 +170,7 @@ def tile_attend_gsig_w_kernel(tc, xT, w_words, w_scales, y, wt, xm, offs, out):
         def weave_xm(m):
             nc.scalar.copy(
                 woven[m].rearrange("p (c i) t -> p c t i", i=PACK),
-                xm_raw[m // 2][:, :, m % 2 * P : (m % 2 + 1) * P].rearrange("p t (c i) -> p c t i", i=PACK),
+                xm_raw[m].rearrange("p t (c i) -> p c t i", i=PACK),
             )
 
         def quantise_xm(first, count, source):
@@ -197,6 +190,8 @@ def tile_attend_gsig_w_kernel(tc, xT, w_words, w_scales, y, wt, xm, offs, out):
         def quantise_g(cols, g_woven):
             nc.vector.quantize_mx(g_codes[:, cols].bitcast(E5M2), g_plane[:, cols], g_woven[:].rearrange("p n j -> p (n j)"))
 
+        spent_loads = {1: "x_raw0", 3: "x_raw1"}
+
         def multiply(m, slots):
             cols = slice(m * P, (m + 1) * P)
             bank = grad_psum.tile([P, N], F32, name="grad")
@@ -209,35 +204,41 @@ def tile_attend_gsig_w_kernel(tc, xT, w_words, w_scales, y, wt, xm, offs, out):
                 start=True,
                 stop=True,
             )
-            columns = ring.tile([P, N], F32, name="columns")
+            if slots.stop == N and m in spent_loads:
+                columns = keep.tile([P, N], F32, name="columns%d" % m, tag=spent_loads[m])
+            else:
+                columns = ring.tile([P, N], F32, name="columns")
             nc.scalar.copy(columns[:, slots], bank[:, slots])
             return columns
 
         def scatter(m, columns, slots):
             listed = offsets[:, slots.start // 16 : slots.stop // 16]
-            nc.vector.tensor_copy(windows[m % WINDOWS][:].indirect(listed), columns[:, slots])
+            nc.vector.tensor_copy(windows[m % len(windows)][:].indirect(listed), columns[:, slots])
 
         def spent(j, cols):
             return margins[:, j, cols].bitcast(BF16).rearrange("p (c t) -> p c t", t=PACK)
 
-        woven[0], woven[1] = spent(3, halves[0]), spent(3, halves[1])
+        woven[0] = woven[1] = spent(3, halves[0])
         woven[2], woven[3] = spent(2, halves[0]), spent(2, halves[1])
         weave_xm(0)
         for j in range(PACK):
             sigmoid(j, halves[1])
-        weave_xm(1)
         quantise_g(halves[0], form_g(halves[0]))
         quantise_xm(0, 1, woven[0])
-        early = multiply(0, halves[0])
-        quantise_g(halves[1], form_g(halves[1]))
+        early = [multiply(0, halves[0])]
+        weave_xm(1)
+        g_second = form_g(halves[1])
         quantise_xm(1, 1, woven[1])
-        scatter(0, early, halves[0])
+        early.append(multiply(1, halves[0]))
+        scatter(0, early[0], halves[0])
+        quantise_g(halves[1], g_second)
+        scatter(1, early[1], halves[0])
         later = keep.tile([P, D // 2, PACK], BF16, name="later", tag="sigmoids", align_bytes=64)
         for m in range(4, D_TILES):
             woven[m] = later[:, (m - 4) * P : (m - 3) * P, :]
         ahead = {0: (2, 2, spent(2, slice(0, N))), 2: (4, 4, later[:])}
         for m in range(D_TILES):
-            slots = halves[1] if m == 0 else slice(0, N)
+            slots = halves[1] if m < EARLY else slice(0, N)
             columns = multiply(m, slots)
             if m in ahead:
                 first, count, source = ahead[m]
@@ -246,7 +247,7 @@ def tile_attend_gsig_w_kernel(tc, xT, w_words, w_scales, y, wt, xm, offs, out):
                 quantise_xm(first, count, source)
             scatter(m, columns, slots)
             if m < D_TILES - 1:
-                nc.sync.dma_start(out[m * P : (m + 1) * P, :], windows[m % WINDOWS][:])
+                nc.sync.dma_start(out[m * P : (m + 1) * P, :], windows[m % len(windows)][:])
             else:
                 for queue, cols in ((nc.sync, slice(0, T // 2)), (nc.scalar, slice(T // 2, T))):
-                    queue.dma_start(out[m * P : (m + 1) * P, cols], windows[m % WINDOWS][:, cols])
+                    queue.dma_start(out[m * P : (m + 1) * P, cols], windows[m % len(windows)][:, cols])

@@ -78,11 +78,14 @@ def tile_attend_gsig_w_kernel(tc, xT, w_words, w_scales, y, wt, xm, offs, out):
             engine.memset(window[:].bitcast(I32), 0)
             return window
 
-        windows = [zeroed_window(nc.vector, "window%d" % w) for w in range(3)] + [zeroed_window(nc.gpsimd, "weights")]
+        windows = [zeroed_window(nc.vector, "window%d" % w) for w in range(2)] + [zeroed_window(nc.gpsimd, "weights")]
 
         picked_scales = keep.tile([P, N], U8, name="picked_scales", align_bytes=64)
         nc.vector.tensor_copy(picked_scales[:], table_scales[:].indirect(offsets[:]))
-        nc.scalar.dma_start(moved_plane[0:SHIFTED, :].bitcast(I32), picked_scales[4 : 4 + SHIFTED, :].bitcast(I32))
+        for q in range(4):
+            nc.scalar.dma_start(
+                moved_plane[32 * q : 32 * q + 4, :].bitcast(I32), picked_scales[32 * q + 4 : 32 * q + 8, :].bitcast(I32)
+            )
         w_planes = [picked_scales, moved_plane]
         picked_words = keep.tile([P, N], U32, name="picked_words")
         nc.vector.tensor_copy(picked_words[:], table_words[:].bitcast(U32).indirect(offsets[:]))
@@ -147,8 +150,9 @@ def tile_attend_gsig_w_kernel(tc, xT, w_words, w_scales, y, wt, xm, offs, out):
         margins = keep.tile([P, PACK, N], F32, name="margins", align_bytes=64)
         sigmoids = keep.tile([P, PACK, N], F32, name="sigmoids", align_bytes=64)
         factors = keep.tile([P, PACK, N], F32, name="factors", align_bytes=64)
-        for j in range(PACK):
-            nc.gpsimd.tensor_scalar(factors[:, j, :], signs[:, j, :], negated[:, j : j + 1], 0.0, MULT, ADD)
+        pieces = [(j, slice(0, N)) for j in range(PAIR)] + [(j, cols) for cols in halves for j in range(PAIR, PACK)]
+        for j, cols in pieces:
+            nc.gpsimd.tensor_scalar(factors[:, j, cols], signs[:, j, cols], negated[:, j : j + 1], 0.0, MULT, ADD)
 
         def margin(j, cols):
             nc.vector.tensor_tensor(margins[:, j, cols], banks[j][:, cols], signs[:, j, cols], MULT)

@@ -19,29 +19,31 @@ ADD = mybir.AluOpType.add
 SIGMOID = mybir.ActivationFunctionType.Sigmoid
 
 P = 128
+QUADRANT = 32
 PACK = 4
 K_PASS = P * PACK
 PASSES = D // K_PASS
 PAIR = 2
 D_TILES = D // P
-WINDOWS = 3
-SHIFTED = 112
+PER_COLUMN = 16
+WINDOWS = 4
 EARLY = 2
+STAGED = 6
 
 
 def tile_attend_gsig_w_kernel(tc, xT, w_words, w_scales, y, wt, xm, offs, out):
     nc = tc.nc
     with ExitStack() as ctx:
         keep = ctx.enter_context(tc.tile_pool(name="keep", bufs=1))
-        ring = ctx.enter_context(tc.tile_pool(name="ring", bufs=6))
+        ring = ctx.enter_context(tc.tile_pool(name="ring", bufs=STAGED))
         score_psum = ctx.enter_context(tc.psum_pool(name="score_psum", bufs=1))
         grad_psum = ctx.enter_context(tc.psum_pool(name="grad_psum", bufs=4))
         half_n = N // 2
         halves = [slice(0, half_n), slice(half_n, N)]
-        half_r = R // 2
+        whole = slice(0, N)
 
-        offsets = keep.tile([P, N // 16], U16, name="offsets")
-        weights = keep.tile([P, PACK], F32, name="weights")
+        offsets = keep.tile([P, N // PER_COLUMN], U16, name="offsets")
+        weights = keep.tile([P, PACK], F32, name="weights", align_bytes=64)
         nc.scalar.dma_start(weights[:], wt[0].rearrange("(p j) o -> p (j o)", j=PACK))
         table_words = keep.tile([P, T], I32, name="table_words")
         nc.sync.dma_start(table_words[:], w_words[0].rearrange("p t b -> p (t b)").bitcast(I32))
@@ -49,9 +51,10 @@ def tile_attend_gsig_w_kernel(tc, xT, w_words, w_scales, y, wt, xm, offs, out):
 
         table_scales = keep.tile([P, T], U8, name="table_scales")
         nc.vector.memset(table_scales[:].bitcast(I32), 0)
-        for q in range(4):
+        for q in range(P // QUADRANT):
             nc.sync.dma_start(
-                table_scales[32 * q : 32 * q + 8, :].bitcast(I32), w_scales[:, 4 * q : 4 * q + 4, :].bitcast(I32)
+                table_scales[QUADRANT * q : QUADRANT * q + PASSES * PACK, :].bitcast(I32),
+                w_scales[:, PACK * q : PACK * (q + 1), :].bitcast(I32),
             )
         moved_plane = keep.tile([P, N], U8, name="moved_plane", align_bytes=64)
         nc.vector.memset(moved_plane[:].bitcast(I32), 0)
@@ -74,17 +77,18 @@ def tile_attend_gsig_w_kernel(tc, xT, w_words, w_scales, y, wt, xm, offs, out):
         nc.gpsimd.tensor_scalar(negated[:], weights[:], -1.0, 0.0, MULT, ADD)
 
         def zeroed_window(engine, tag):
-            window = keep.tile([P, T], F32, name="window", tag=tag)
+            window = keep.tile([P, T], F32, name="window", tag=tag, align_bytes=64)
             engine.memset(window[:].bitcast(I32), 0)
             return window
 
-        windows = [zeroed_window(nc.vector, "window%d" % w) for w in range(2)] + [zeroed_window(nc.gpsimd, "weights")]
+        windows = [zeroed_window(nc.vector, "window0"), zeroed_window(nc.vector, "window1"), zeroed_window(nc.gpsimd, "weights")]
 
         picked_scales = keep.tile([P, N], U8, name="picked_scales", align_bytes=64)
         nc.vector.tensor_copy(picked_scales[:], table_scales[:].indirect(offsets[:]))
-        for q in range(4):
+        for q in range(P // QUADRANT):
             nc.scalar.dma_start(
-                moved_plane[32 * q : 32 * q + 4, :].bitcast(I32), picked_scales[32 * q + 4 : 32 * q + 8, :].bitcast(I32)
+                moved_plane[QUADRANT * q : QUADRANT * q + PACK, :].bitcast(I32),
+                picked_scales[QUADRANT * q + PACK : QUADRANT * q + PASSES * PACK, :].bitcast(I32),
             )
         w_planes = [picked_scales, moved_plane]
         picked_words = keep.tile([P, N], U32, name="picked_words")
@@ -100,15 +104,15 @@ def tile_attend_gsig_w_kernel(tc, xT, w_words, w_scales, y, wt, xm, offs, out):
         x_codes = [keep.tile([P, R], U32, name="x_codes%d" % o, align_bytes=64) for o in range(PASSES)]
         x_planes = [keep.tile([P, R], U8, name="x_plane%d" % o, align_bytes=64) for o in range(PASSES)]
         x_woven = [
-            [keep.tile([P, PAIR, P, PACK], BF16, name="x_woven%d_%d" % (o, e), align_bytes=64) for e in range(2)]
+            [keep.tile([P, PAIR, P, PACK], BF16, name="x_woven%d_%d" % (o, e), align_bytes=64) for e in range(PACK // PAIR)]
             for o in range(PASSES)
         ]
 
-        def weave_x(o, raw, places):
+        def weave_x(o):
             for copy, first in ((nc.vector.tensor_copy, 0), (nc.scalar.copy, PAIR)):
                 copy(
-                    x_woven[o][first // PAIR][:, :, places, :].rearrange("p j s t -> p s t j"),
-                    raw[:].rearrange("p t (s j) -> p s t j", j=PACK)[:, :, :, first : first + PAIR],
+                    x_woven[o][first // PAIR][:].rearrange("p j s t -> p s t j"),
+                    x_raw[o][:].rearrange("p t (s j) -> p s t j", j=PACK)[:, :, :, first : first + PAIR],
                 )
 
         def quantise_x(o, cuts):
@@ -121,17 +125,18 @@ def tile_attend_gsig_w_kernel(tc, xT, w_words, w_scales, y, wt, xm, offs, out):
                 )
 
         for o, cuts in enumerate(((0, 2, 4), (0, 1, 2, 4))):
-            weave_x(o, x_raw[o], slice(0, P))
+            weave_x(o)
             quantise_x(o, cuts)
 
         quarter = D // 4
+        low_tiles = D_TILES // 2
         xm_low = keep.tile([P, 2, PACK, quarter], F32, name="xm_low", tag="x_raw0")
         xm_high = keep.tile([P, PACK, D // 2], F32, name="xm_high", tag="x_raw1")
         for c in range(2):
             load_rows(xm_low[:, c], xm[0, :, c * quarter : (c + 1) * quarter])
         load_rows(xm_high[:], xm[0, :, D // 2 :])
-        xm_raw = [xm_low[:, m // 2, :, m % 2 * P : (m % 2 + 1) * P] for m in range(4)]
-        xm_raw.extend(xm_high[:, :, m * P : (m + 1) * P] for m in range(4))
+        xm_raw = [xm_low[:, m // 2, :, m % 2 * P : (m % 2 + 1) * P] for m in range(low_tiles)]
+        xm_raw.extend(xm_high[:, :, m * P : (m + 1) * P] for m in range(low_tiles))
 
         banks = [score_psum.tile([P, N], F32, name="scores%d" % j) for j in range(PACK)]
         for o in range(PASSES):
@@ -150,7 +155,7 @@ def tile_attend_gsig_w_kernel(tc, xT, w_words, w_scales, y, wt, xm, offs, out):
         margins = keep.tile([P, PACK, N], F32, name="margins", align_bytes=64)
         sigmoids = keep.tile([P, PACK, N], F32, name="sigmoids", align_bytes=64)
         factors = keep.tile([P, PACK, N], F32, name="factors", align_bytes=64)
-        pieces = [(j, slice(0, N)) for j in range(PAIR)] + [(j, cols) for cols in halves for j in range(PAIR, PACK)]
+        pieces = [(j, whole) for j in range(PAIR)] + [(j, cols) for cols in halves for j in range(PAIR, PACK)]
         for j, cols in pieces:
             nc.gpsimd.tensor_scalar(factors[:, j, cols], signs[:, j, cols], negated[:, j : j + 1], 0.0, MULT, ADD)
 
@@ -161,7 +166,7 @@ def tile_attend_gsig_w_kernel(tc, xT, w_words, w_scales, y, wt, xm, offs, out):
             nc.scalar.activation(sigmoids[:, j, cols], margins[:, j, cols], SIGMOID, scale=-1.0)
 
         for j in range(PACK):
-            margin(j, slice(0, N) if j < PAIR else halves[0])
+            margin(j, whole if j < PAIR else halves[0])
             sigmoid(j, halves[0])
         for j in range(PAIR, PACK):
             margin(j, halves[1])
@@ -194,7 +199,7 @@ def tile_attend_gsig_w_kernel(tc, xT, w_words, w_scales, y, wt, xm, offs, out):
         def quantise_g(cols, g_woven):
             nc.vector.quantize_mx(g_codes[:, cols].bitcast(E5M2), g_plane[:, cols], g_woven[:].rearrange("p n j -> p (n j)"))
 
-        spent_loads = {1: "x_raw0", 3: "x_raw1"}
+        spent_loads = {1: "x_raw0", 2: "x_raw1"}
 
         def multiply(m, slots):
             cols = slice(m * P, (m + 1) * P)
@@ -216,8 +221,8 @@ def tile_attend_gsig_w_kernel(tc, xT, w_words, w_scales, y, wt, xm, offs, out):
             return columns
 
         def scatter(m, columns, slots):
-            listed = offsets[:, slots.start // 16 : slots.stop // 16]
-            nc.vector.tensor_copy(windows[m % len(windows)][:].indirect(listed), columns[:, slots])
+            listed = offsets[:, slots.start // PER_COLUMN : slots.stop // PER_COLUMN]
+            nc.vector.tensor_copy(windows[m % WINDOWS][:].indirect(listed), columns[:, slots])
 
         def spent(j, cols):
             return margins[:, j, cols].bitcast(BF16).rearrange("p (c t) -> p c t", t=PACK)
@@ -238,20 +243,22 @@ def tile_attend_gsig_w_kernel(tc, xT, w_words, w_scales, y, wt, xm, offs, out):
         quantise_g(halves[1], g_second)
         scatter(1, early[1], halves[0])
         later = keep.tile([P, D // 2, PACK], BF16, name="later", tag="sigmoids", align_bytes=64)
-        for m in range(4, D_TILES):
-            woven[m] = later[:, (m - 4) * P : (m - 3) * P, :]
-        ahead = {0: (2, 2, spent(2, slice(0, N))), 2: (4, 4, later[:])}
+        for m in range(low_tiles):
+            woven[low_tiles + m] = later[:, m * P : (m + 1) * P, :]
+        ahead = {0: (EARLY, low_tiles - EARLY, spent(2, whole)), 1: (low_tiles, low_tiles, later[:])}
         for m in range(D_TILES):
-            slots = halves[1] if m < EARLY else slice(0, N)
+            slots = halves[1] if m < EARLY else whole
             columns = multiply(m, slots)
             if m in ahead:
                 first, count, source = ahead[m]
                 for k in range(first, first + count):
                     weave_xm(k)
                 quantise_xm(first, count, source)
+            if m == EARLY - 1:
+                windows.append(zeroed_window(nc.gpsimd, "sigmoids"))
             scatter(m, columns, slots)
             if m < D_TILES - 1:
-                nc.sync.dma_start(out[m * P : (m + 1) * P, :], windows[m % len(windows)][:])
+                nc.sync.dma_start(out[m * P : (m + 1) * P, :], windows[m % WINDOWS][:])
             else:
                 for queue, cols in ((nc.sync, slice(0, T // 2)), (nc.scalar, slice(T // 2, T))):
-                    queue.dma_start(out[m * P : (m + 1) * P, cols], windows[m % len(windows)][:, cols])
+                    queue.dma_start(out[m * P : (m + 1) * P, cols], windows[m % WINDOWS][:, cols])

@@ -20,6 +20,7 @@ SIGMOID = mybir.ActivationFunctionType.Sigmoid
 
 P = 128
 QUADRANT = 32
+HALF_QUADRANT = 16
 PACK = 4
 K_PASS = P * PACK
 PASSES = D // K_PASS
@@ -51,11 +52,9 @@ def tile_attend_gsig_w_kernel(tc, xT, w_words, w_scales, y, wt, xm, offs, out):
 
         table_scales = keep.tile([P, T], U8, name="table_scales")
         nc.vector.memset(table_scales[:].bitcast(I32), 0)
-        for q in range(P // QUADRANT):
-            nc.sync.dma_start(
-                table_scales[QUADRANT * q : QUADRANT * q + PASSES * PACK, :].bitcast(I32),
-                w_scales[:, PACK * q : PACK * (q + 1), :].bitcast(I32),
-            )
+        scale_rows = w_scales.rearrange("o (q r) t -> r q o t", r=PACK)
+        for r in range(PACK):
+            nc.sync.dma_start(table_scales[r:P:HALF_QUADRANT, :].bitcast(I32), scale_rows[r].bitcast(I32))
         moved_plane = keep.tile([P, N], U8, name="moved_plane", align_bytes=64)
         nc.vector.memset(moved_plane[:].bitcast(I32), 0)
         g_codes = keep.tile([P, N], U32, name="g_codes", align_bytes=64)
@@ -83,16 +82,16 @@ def tile_attend_gsig_w_kernel(tc, xT, w_words, w_scales, y, wt, xm, offs, out):
 
         windows = [zeroed_window(nc.vector, "window0"), zeroed_window(nc.vector, "window1"), zeroed_window(nc.gpsimd, "weights")]
 
+        picked_words = keep.tile([P, N], U32, name="picked_words")
+        nc.vector.tensor_copy(picked_words[:], table_words[:].bitcast(U32).indirect(offsets[:]))
         picked_scales = keep.tile([P, N], U8, name="picked_scales", align_bytes=64)
         nc.vector.tensor_copy(picked_scales[:], table_scales[:].indirect(offsets[:]))
         for q in range(P // QUADRANT):
             nc.scalar.dma_start(
                 moved_plane[QUADRANT * q : QUADRANT * q + PACK, :].bitcast(I32),
-                picked_scales[QUADRANT * q + PACK : QUADRANT * q + PASSES * PACK, :].bitcast(I32),
+                picked_scales[QUADRANT * q + HALF_QUADRANT : QUADRANT * q + HALF_QUADRANT + PACK, :].bitcast(I32),
             )
         w_planes = [picked_scales, moved_plane]
-        picked_words = keep.tile([P, N], U32, name="picked_words")
-        nc.vector.tensor_copy(picked_words[:], table_words[:].bitcast(U32).indirect(offsets[:]))
         w_codes = keep.tile([P, PASSES, N], U16, name="w_codes", align_bytes=64)
         nc.vector.tensor_copy(w_codes[:], picked_words[:].bitcast(U16).rearrange("p (n o) -> p o n", o=PASSES))
 

@@ -21,6 +21,7 @@ SIGMOID = mybir.ActivationFunctionType.Sigmoid
 P = 128
 QUADRANT = 32
 HALF_QUADRANT = 16
+LEAD = T // 4
 PACK = 4
 K_PASS = P * PACK
 PASSES = D // K_PASS
@@ -28,7 +29,7 @@ PAIR = 2
 D_TILES = D // P
 PER_COLUMN = 16
 WINDOWS = 4
-EARLY = 2
+EARLY = 3
 STAGED = 6
 
 
@@ -47,14 +48,16 @@ def tile_attend_gsig_w_kernel(tc, xT, w_words, w_scales, y, wt, xm, offs, out):
         weights = keep.tile([P, PACK], F32, name="weights", align_bytes=64)
         nc.scalar.dma_start(weights[:], wt[0].rearrange("(p j) o -> p (j o)", j=PACK))
         table_words = keep.tile([P, T], I32, name="table_words")
-        nc.sync.dma_start(table_words[:], w_words[0].rearrange("p t b -> p (t b)").bitcast(I32))
+        words = w_words[0].rearrange("p t b -> p (t b)").bitcast(I32)
         nc.sync.dma_start(offsets[:], offs)
+        nc.sync.dma_start(table_words[:, :LEAD], words[:, :LEAD])
 
         table_scales = keep.tile([P, T], U8, name="table_scales")
         nc.vector.memset(table_scales[:].bitcast(I32), 0)
         scale_rows = w_scales.rearrange("o (q r) t -> r q o t", r=PACK)
         for r in range(PACK):
             nc.sync.dma_start(table_scales[r:P:HALF_QUADRANT, :].bitcast(I32), scale_rows[r].bitcast(I32))
+        nc.sync.dma_start(table_words[:, LEAD:], words[:, LEAD:])
         moved_plane = keep.tile([P, N], U8, name="moved_plane", align_bytes=64)
         nc.vector.memset(moved_plane[:].bitcast(I32), 0)
         g_codes = keep.tile([P, N], U32, name="g_codes", align_bytes=64)
@@ -82,8 +85,6 @@ def tile_attend_gsig_w_kernel(tc, xT, w_words, w_scales, y, wt, xm, offs, out):
 
         windows = [zeroed_window(nc.vector, "window0"), zeroed_window(nc.vector, "window1"), zeroed_window(nc.gpsimd, "weights")]
 
-        picked_words = keep.tile([P, N], U32, name="picked_words")
-        nc.vector.tensor_copy(picked_words[:], table_words[:].bitcast(U32).indirect(offsets[:]))
         picked_scales = keep.tile([P, N], U8, name="picked_scales", align_bytes=64)
         nc.vector.tensor_copy(picked_scales[:], table_scales[:].indirect(offsets[:]))
         for q in range(P // QUADRANT):
@@ -92,6 +93,8 @@ def tile_attend_gsig_w_kernel(tc, xT, w_words, w_scales, y, wt, xm, offs, out):
                 picked_scales[QUADRANT * q + HALF_QUADRANT : QUADRANT * q + HALF_QUADRANT + PACK, :].bitcast(I32),
             )
         w_planes = [picked_scales, moved_plane]
+        picked_words = keep.tile([P, N], U32, name="picked_words")
+        nc.vector.tensor_copy(picked_words[:], table_words[:].bitcast(U32).indirect(offsets[:]))
         w_codes = keep.tile([P, PASSES, N], U16, name="w_codes", align_bytes=64)
         nc.vector.tensor_copy(w_codes[:], picked_words[:].bitcast(U16).rearrange("p (n o) -> p o n", o=PASSES))
 
@@ -151,71 +154,60 @@ def tile_attend_gsig_w_kernel(tc, xT, w_words, w_scales, y, wt, xm, offs, out):
                     stop=(o == PASSES - 1),
                 )
 
-        margins = keep.tile([P, PACK, N], F32, name="margins", align_bytes=64)
-        sigmoids = keep.tile([P, PACK, N], F32, name="sigmoids", align_bytes=64)
-        factors = keep.tile([P, PACK, N], F32, name="factors", align_bytes=64)
-        pieces = [(j, whole) for j in range(PAIR)] + [(j, cols) for cols in halves for j in range(PAIR, PACK)]
-        for j, cols in pieces:
-            nc.gpsimd.tensor_scalar(factors[:, j, cols], signs[:, j, cols], negated[:, j : j + 1], 0.0, MULT, ADD)
+        margins = [keep.tile([P, PACK, half_n], F32, name="margins%d" % h, align_bytes=64) for h in range(2)]
+        sigmoids = [keep.tile([P, PACK, half_n], F32, name="sigmoids%d" % h, align_bytes=64) for h in range(2)]
 
-        def margin(j, cols):
-            nc.vector.tensor_tensor(margins[:, j, cols], banks[j][:, cols], signs[:, j, cols], MULT)
+        def form_factors(h, tag):
+            factors = keep.tile([P, PACK, half_n], F32, name="factors%d" % h, tag=tag, align_bytes=64)
+            for j in range(PACK):
+                nc.gpsimd.tensor_scalar(factors[:, j, :], signs[:, j, halves[h]], negated[:, j : j + 1], 0.0, MULT, ADD)
+            return factors
 
-        def sigmoid(j, cols):
-            nc.scalar.activation(sigmoids[:, j, cols], margins[:, j, cols], SIGMOID, scale=-1.0)
+        def form_sigmoids(h):
+            for j in range(PACK):
+                nc.vector.tensor_tensor(margins[h][:, j, :], banks[j][:, halves[h]], signs[:, j, halves[h]], MULT)
+                nc.scalar.activation(sigmoids[h][:, j, :], margins[h][:, j, :], SIGMOID, scale=-1.0)
 
-        for j in range(PACK):
-            margin(j, whole if j < PAIR else halves[0])
-            sigmoid(j, halves[0])
-        for j in range(PAIR, PACK):
-            margin(j, halves[1])
-
-        xm_codes = keep.tile([P, D], U32, name="xm_codes", align_bytes=64)
-        xm_plane = keep.tile([P, D], U8, name="xm_plane", align_bytes=64)
-
-        woven = {}
-
-        def weave_xm(m):
-            nc.scalar.copy(
-                woven[m].rearrange("p (c i) t -> p c t i", i=PACK),
-                xm_raw[m].rearrange("p t (c i) -> p c t i", i=PACK),
-            )
-
-        def quantise_xm(first, count, source):
-            cols = slice(first * P, (first + count) * P)
-            nc.vector.quantize_mx(xm_codes[:, cols].bitcast(E4M3), xm_plane[:, cols], source.rearrange("p c t -> p (c t)"))
-
-        def form_g(cols):
-            g_woven = keep.tile([P, half_n, PACK], BF16, name="g_woven", align_bytes=64)
-            nc.vector.tensor_tensor(
-                g_woven[:].rearrange("p (c i) j -> p c j i", i=PAIR),
-                sigmoids[:, :, cols].rearrange("p j (c i) -> p c j i", i=PAIR),
-                factors[:, :, cols].rearrange("p j (c i) -> p c j i", i=PAIR),
+        def form_g(engine, h, factors, run):
+            g_woven = keep.tile([P, half_n, PACK], BF16, name="g_woven%d" % h, align_bytes=64)
+            engine.tensor_tensor(
+                g_woven[:].rearrange("p (c i) j -> p c j i", i=run),
+                sigmoids[h][:].rearrange("p j (c i) -> p c j i", i=run),
+                factors[:].rearrange("p j (c i) -> p c j i", i=run),
                 MULT,
             )
             return g_woven
 
-        def quantise_g(cols, g_woven):
+        def quantise_g(h, g_woven):
+            cols = halves[h]
             nc.vector.quantize_mx(g_codes[:, cols].bitcast(E5M2), g_plane[:, cols], g_woven[:].rearrange("p n j -> p (n j)"))
 
-        spent_loads = {1: "x_raw0", 2: "x_raw1"}
+        xm_plane = keep.tile([P, D], U8, name="xm_plane", align_bytes=64)
+
+        def weave_xm(m, woven):
+            nc.scalar.copy(
+                woven.rearrange("p (c i) t -> p c t i", i=PACK),
+                xm_raw[m].rearrange("p t (c i) -> p c t i", i=PACK),
+            )
+
+        def quantise_xm(first, count, codes, woven):
+            plane = xm_plane[:, first * P : (first + count) * P]
+            nc.vector.quantize_mx(codes.bitcast(E4M3), plane, woven.rearrange("p c t -> p (c t)"))
+
+        xm_codes = {}
 
         def multiply(m, slots):
-            cols = slice(m * P, (m + 1) * P)
             bank = grad_psum.tile([P, N], F32, name="grad")
             nc.tensor.matmul_mx(
                 bank[:],
-                lhsT=xm_codes[:, cols].bitcast(E4M3),
-                lhsT_scale=xm_plane[:, cols],
+                lhsT=xm_codes[m].bitcast(E4M3),
+                lhsT_scale=xm_plane[:, m * P : (m + 1) * P],
                 rhs=g_codes[:].bitcast(E5M2),
                 rhs_scale=g_plane[:],
                 start=True,
                 stop=True,
             )
-            if slots.stop == N and m in spent_loads:
-                columns = keep.tile([P, N], F32, name="columns%d" % m, tag=spent_loads[m])
-            else:
-                columns = ring.tile([P, N], F32, name="columns")
+            columns = ring.tile([P, N], F32, name="columns")
             nc.scalar.copy(columns[:, slots], bank[:, slots])
             return columns
 
@@ -223,39 +215,39 @@ def tile_attend_gsig_w_kernel(tc, xT, w_words, w_scales, y, wt, xm, offs, out):
             listed = offsets[:, slots.start // PER_COLUMN : slots.stop // PER_COLUMN]
             nc.vector.tensor_copy(windows[m % WINDOWS][:].indirect(listed), columns[:, slots])
 
-        def spent(j, cols):
-            return margins[:, j, cols].bitcast(BF16).rearrange("p (c t) -> p c t", t=PACK)
-
-        woven[0] = woven[1] = spent(3, halves[0])
-        woven[2], woven[3] = spent(2, halves[0]), spent(2, halves[1])
-        weave_xm(0)
-        for j in range(PACK):
-            sigmoid(j, halves[1])
-        quantise_g(halves[0], form_g(halves[0]))
-        quantise_xm(0, 1, woven[0])
+        factors = form_factors(0, "x_woven%d_%d" % (PASSES - 1, 1))
+        form_sigmoids(0)
+        early_woven = keep.tile([P, EARLY, P, PACK], BF16, name="early_woven", tag="margins0", align_bytes=64)
+        early_codes = keep.tile([P, EARLY, P], U32, name="early_codes", align_bytes=64)
+        for m in range(EARLY):
+            weave_xm(m, early_woven[:, m])
+            xm_codes[m] = early_codes[:, m, :]
+        g_first = form_g(nc.vector, 0, factors, PAIR)
+        quantise_xm(0, 1, xm_codes[0], early_woven[:, 0])
+        quantise_g(0, g_first)
         early = [multiply(0, halves[0])]
-        weave_xm(1)
-        g_second = form_g(halves[1])
-        quantise_xm(1, 1, woven[1])
-        early.append(multiply(1, halves[0]))
-        scatter(0, early[0], halves[0])
-        quantise_g(halves[1], g_second)
-        scatter(1, early[1], halves[0])
-        later = keep.tile([P, D // 2, PACK], BF16, name="later", tag="sigmoids", align_bytes=64)
-        for m in range(low_tiles):
-            woven[low_tiles + m] = later[:, m * P : (m + 1) * P, :]
-        ahead = {0: (EARLY, low_tiles - EARLY, spent(2, whole)), 1: (low_tiles, low_tiles, later[:])}
+        quantise_xm(1, 1, xm_codes[1], early_woven[:, 1])
+        factors = form_factors(1, "g_woven0")
+        form_sigmoids(1)
+        quantise_xm(2, 1, xm_codes[2], early_woven[:, 2])
+        early.extend(multiply(m, halves[0]) for m in range(1, EARLY))
+        g_second = form_g(nc.gpsimd, 1, factors, PACK)
+        for m in range(EARLY):
+            scatter(m, early[m], halves[0])
+        quantise_g(1, g_second)
+        late = D_TILES - EARLY
+        late_woven = keep.tile([P, late * P, PACK], BF16, name="late_woven", tag="margins1", align_bytes=64)
+        late_codes = keep.tile([P, late * P], U32, name="late_codes", tag="g_woven1", align_bytes=64)
+        for m in range(EARLY, D_TILES):
+            cols = slice((m - EARLY) * P, (m - EARLY + 1) * P)
+            weave_xm(m, late_woven[:, cols, :])
+            xm_codes[m] = late_codes[:, cols]
+        quantise_xm(EARLY, 1, late_codes[:, :P], late_woven[:, :P, :])
+        quantise_xm(EARLY + 1, late - 1, late_codes[:, P:], late_woven[:, P:, :])
+        windows.append(zeroed_window(nc.gpsimd, "margins1"))
         for m in range(D_TILES):
             slots = halves[1] if m < EARLY else whole
-            columns = multiply(m, slots)
-            if m in ahead:
-                first, count, source = ahead[m]
-                for k in range(first, first + count):
-                    weave_xm(k)
-                quantise_xm(first, count, source)
-            if m == EARLY - 1:
-                windows.append(zeroed_window(nc.gpsimd, "sigmoids"))
-            scatter(m, columns, slots)
+            scatter(m, multiply(m, slots), slots)
             if m < D_TILES - 1:
                 nc.sync.dma_start(out[m * P : (m + 1) * P, :], windows[m % WINDOWS][:])
             else:

@@ -16,12 +16,13 @@ E5M2 = mybir.dt.float8_e5m2_x4
 E2M1 = mybir.dt.float4_e2m1fn_x4
 MULT = mybir.AluOpType.mult
 ADD = mybir.AluOpType.add
+COPY = mybir.ActivationFunctionType.Copy
 SIGMOID = mybir.ActivationFunctionType.Sigmoid
 
 P = 128
 QUADRANT = 32
 HALF_QUADRANT = 16
-LEAD = T // 4
+LEAD = T // 2
 PACK = 4
 K_PASS = P * PACK
 PASSES = D // K_PASS
@@ -37,9 +38,9 @@ def tile_attend_gsig_w_kernel(tc, xT, w_words, w_scales, y, wt, xm, offs, out):
     nc = tc.nc
     with ExitStack() as ctx:
         keep = ctx.enter_context(tc.tile_pool(name="keep", bufs=1))
+        loads = ctx.enter_context(tc.tile_pool(name="loads", bufs=1))
         ring = ctx.enter_context(tc.tile_pool(name="ring", bufs=STAGED))
-        score_psum = ctx.enter_context(tc.psum_pool(name="score_psum", bufs=1))
-        grad_psum = ctx.enter_context(tc.psum_pool(name="grad_psum", bufs=4))
+        psum = ctx.enter_context(tc.psum_pool(name="psum", bufs=1))
         half_n = N // 2
         halves = [slice(0, half_n), slice(half_n, N)]
         whole = slice(0, N)
@@ -49,8 +50,8 @@ def tile_attend_gsig_w_kernel(tc, xT, w_words, w_scales, y, wt, xm, offs, out):
         nc.scalar.dma_start(weights[:], wt[0].rearrange("(p j) o -> p (j o)", j=PACK))
         table_words = keep.tile([P, T], I32, name="table_words")
         words = w_words[0].rearrange("p t b -> p (t b)").bitcast(I32)
-        nc.sync.dma_start(offsets[:], offs)
         nc.sync.dma_start(table_words[:, :LEAD], words[:, :LEAD])
+        nc.sync.dma_start(offsets[:], offs)
 
         table_scales = keep.tile([P, T], U8, name="table_scales")
         nc.vector.memset(table_scales[:].bitcast(I32), 0)
@@ -71,9 +72,14 @@ def tile_attend_gsig_w_kernel(tc, xT, w_words, w_scales, y, wt, xm, offs, out):
         def load_rows(tile, rows):
             nc.sync.dma_start(tile, rows.rearrange("(p t) c -> p t c", t=PACK))
 
-        x_raw = [keep.tile([P, PACK, R], F32, name="x_raw%d" % o) for o in range(PASSES)]
+        early_d = EARLY * P
+        room = PACK * 4 * (early_d + half_n)
+        x_raw = [loads.tile([P, PACK, R], F32, name="x_raw%d" % o, offset=o * room) for o in range(PASSES)]
+        x_places = [slice(0, PAIR), slice(PAIR, PACK)]
         for o in range(PASSES):
-            load_rows(x_raw[o][:], xT[0, o * K_PASS : (o + 1) * K_PASS, :])
+            rows = xT[0, o * K_PASS : (o + 1) * K_PASS, :].rearrange("(p t) c -> p t c", t=PACK)
+            for places in x_places:
+                nc.sync.dma_start(x_raw[o][:, places, :], rows[:, places, :])
 
         negated = keep.tile([P, PACK], F32, name="negated")
         nc.gpsimd.tensor_scalar(negated[:], weights[:], -1.0, 0.0, MULT, ADD)
@@ -88,7 +94,7 @@ def tile_attend_gsig_w_kernel(tc, xT, w_words, w_scales, y, wt, xm, offs, out):
         picked_scales = keep.tile([P, N], U8, name="picked_scales", align_bytes=64)
         nc.vector.tensor_copy(picked_scales[:], table_scales[:].indirect(offsets[:]))
         for q in range(P // QUADRANT):
-            nc.scalar.dma_start(
+            nc.sync.dma_start(
                 moved_plane[QUADRANT * q : QUADRANT * q + PACK, :].bitcast(I32),
                 picked_scales[QUADRANT * q + HALF_QUADRANT : QUADRANT * q + HALF_QUADRANT + PACK, :].bitcast(I32),
             )
@@ -96,12 +102,11 @@ def tile_attend_gsig_w_kernel(tc, xT, w_words, w_scales, y, wt, xm, offs, out):
         picked_words = keep.tile([P, N], U32, name="picked_words")
         nc.vector.tensor_copy(picked_words[:], table_words[:].bitcast(U32).indirect(offsets[:]))
         w_codes = keep.tile([P, PASSES, N], U16, name="w_codes", align_bytes=64)
-        nc.vector.tensor_copy(w_codes[:], picked_words[:].bitcast(U16).rearrange("p (n o) -> p o n", o=PASSES))
+        word_pairs = picked_words[:].bitcast(U16).rearrange("p (n o) -> p o n", o=PASSES)
+        nc.vector.tensor_copy(w_codes[:, 0, :], word_pairs[:, 0, :])
 
-        signs = keep.tile([P, PACK, N], F32, name="signs", tag="table_words")
-        y_rows = y[0].rearrange("(p j) n -> p j n", j=PACK)
-        for first in range(0, PACK, PAIR):
-            nc.sync.dma_start(signs[:, first : first + PAIR, :], y_rows[:, first : first + PAIR, :])
+        signs = [keep.tile([P, PACK, half_n], F32, name="signs0", tag="table_words")]
+        load_rows(signs[0][:], y[0, :, halves[0]])
 
         x_codes = [keep.tile([P, R], U32, name="x_codes%d" % o, align_bytes=64) for o in range(PASSES)]
         x_planes = [keep.tile([P, R], U8, name="x_plane%d" % o, align_bytes=64) for o in range(PASSES)]
@@ -111,10 +116,15 @@ def tile_attend_gsig_w_kernel(tc, xT, w_words, w_scales, y, wt, xm, offs, out):
         ]
 
         def weave_x(o):
-            for copy, first in ((nc.vector.tensor_copy, 0), (nc.scalar.copy, PAIR)):
+            low, high = x_places
+            if o == 0:
+                shares = ((nc.scalar.copy, 0, low), (nc.vector.tensor_copy, 0, high), (nc.scalar.copy, PAIR, slice(0, PACK)))
+            else:
+                shares = [(copy, first, places) for places in x_places for copy, first in ((nc.vector.tensor_copy, 0), (nc.scalar.copy, PAIR))]
+            for copy, first, places in shares:
                 copy(
-                    x_woven[o][first // PAIR][:].rearrange("p j s t -> p s t j"),
-                    x_raw[o][:].rearrange("p t (s j) -> p s t j", j=PACK)[:, :, :, first : first + PAIR],
+                    x_woven[o][first // PAIR][:].rearrange("p j s t -> p s t j")[:, :, places, :],
+                    x_raw[o][:].rearrange("p t (s j) -> p s t j", j=PACK)[:, :, places, first : first + PAIR],
                 )
 
         def quantise_x(o, cuts):
@@ -126,56 +136,93 @@ def tile_attend_gsig_w_kernel(tc, xT, w_words, w_scales, y, wt, xm, offs, out):
                     x_woven[o][lo // PAIR][:, lo % PAIR : lo % PAIR + hi - lo, :, :].rearrange("p j s t -> p (j s t)"),
                 )
 
-        for o, cuts in enumerate(((0, 2, 4), (0, 1, 2, 4))):
+        for o, cuts in enumerate(((0, 1, 2, 4), (0, 1, 2, 4))):
             weave_x(o)
+            if o == 0:
+                nc.vector.tensor_copy(w_codes[:, 1, :], word_pairs[:, 1, :])
             quantise_x(o, cuts)
 
-        quarter = D // 4
-        low_tiles = D_TILES // 2
-        xm_low = keep.tile([P, 2, PACK, quarter], F32, name="xm_low", tag="x_raw0")
-        xm_high = keep.tile([P, PACK, D // 2], F32, name="xm_high", tag="x_raw1")
-        for c in range(2):
-            load_rows(xm_low[:, c], xm[0, :, c * quarter : (c + 1) * quarter])
-        load_rows(xm_high[:], xm[0, :, D // 2 :])
-        xm_raw = [xm_low[:, m // 2, :, m % 2 * P : (m % 2 + 1) * P] for m in range(low_tiles)]
-        xm_raw.extend(xm_high[:, :, m * P : (m + 1) * P] for m in range(low_tiles))
+        xm_early = loads.tile([P, PACK, early_d], F32, name="xm_early", offset=0)
+        signs.append(loads.tile([P, PACK, half_n], F32, name="signs1", offset=PACK * 4 * early_d))
+        xm_late = loads.tile([P, PACK, D - early_d], F32, name="xm_late", offset=room)
+        load_rows(xm_early[:], xm[0, :, :early_d])
+        load_rows(signs[1][:], y[0, :, halves[1]])
+        load_rows(xm_late[:], xm[0, :, early_d:])
+        xm_raw = [xm_early[:, :, m * P : (m + 1) * P] for m in range(EARLY)]
+        xm_raw.extend(xm_late[:, :, m * P : (m + 1) * P] for m in range(D_TILES - EARLY))
 
-        banks = [score_psum.tile([P, N], F32, name="scores%d" % j) for j in range(PACK)]
+        def score_pass(bank, o, j, slots):
+            cols = slice(j * P, (j + 1) * P)
+            nc.tensor.matmul_mx(
+                bank,
+                lhsT=x_codes[o][:, cols].bitcast(E4M3),
+                lhsT_scale=x_planes[o][:, cols],
+                rhs=w_codes[:, o, slots].bitcast(E2M1),
+                rhs_scale=w_planes[o][:, slots],
+                start=(o == 0),
+                stop=(o == PASSES - 1),
+            )
+
+        quarters = [slice(c * P, (c + 1) * P) for c in range(N // P)]
+        scores = {}
+        groups = []
+        for j in range(PAIR):
+            bank = psum.tile([P, N], F32, name="scores%d" % j)
+            groups.append((bank[:], j, whole))
+            for h in range(2):
+                scores[h, j] = [(bank[:, halves[h]], slice(0, half_n))]
+        for j in range(PAIR, PACK):
+            scores[0, j] = []
+            for c in range(2):
+                bank = psum.tile([P, P], F32, name="scores%d_%d" % (j, c))
+                groups.append((bank[:], j, quarters[c]))
+                scores[0, j].append((bank[:], quarters[c]))
         for o in range(PASSES):
-            for j in range(PACK):
-                cols = slice(j * P, (j + 1) * P)
-                nc.tensor.matmul_mx(
-                    banks[j][:],
-                    lhsT=x_codes[o][:, cols].bitcast(E4M3),
-                    lhsT_scale=x_planes[o][:, cols],
-                    rhs=w_codes[:, o, :].bitcast(E2M1),
-                    rhs_scale=w_planes[o][:],
-                    start=(o == 0),
-                    stop=(o == PASSES - 1),
-                )
+            for bank, j, slots in groups:
+                score_pass(bank, o, j, slots)
 
-        margins = [keep.tile([P, PACK, half_n], F32, name="margins%d" % h, align_bytes=64) for h in range(2)]
-        sigmoids = [keep.tile([P, PACK, half_n], F32, name="sigmoids%d" % h, align_bytes=64) for h in range(2)]
+        def second_scores():
+            for j in range(PAIR, PACK):
+                bank = psum.tile([P, half_n], F32, name="second%d" % j, tag="scores%d_0" % j)
+                scores[1, j] = [(bank[:], slice(0, half_n))]
+                for c in range(2):
+                    for o in range(PASSES):
+                        score_pass(bank[:, quarters[c]], o, j, quarters[2 + c])
+
+        grad_tags = ["grad0", "grad1", "scores2_1", "scores3_1"]
+        grad_count = []
+
+        margins, sigmoids = [], []
+
+        def pieces(split):
+            return [slice(0, half_n // 2), slice(half_n // 2, half_n)] if split else [slice(0, half_n)]
 
         def form_factors(h, tag):
             factors = keep.tile([P, PACK, half_n], F32, name="factors%d" % h, tag=tag, align_bytes=64)
             for j in range(PACK):
-                nc.gpsimd.tensor_scalar(factors[:, j, :], signs[:, j, halves[h]], negated[:, j : j + 1], 0.0, MULT, ADD)
+                if h == 0 and j < PAIR:
+                    nc.scalar.activation(factors[:, j, :], signs[h][:, j, :], COPY, scale=negated[:, j : j + 1])
+                else:
+                    nc.gpsimd.tensor_scalar(factors[:, j, :], signs[h][:, j, :], negated[:, j : j + 1], 0.0, MULT, ADD)
             return factors
 
-        def form_sigmoids(h):
-            for j in range(PACK):
-                nc.vector.tensor_tensor(margins[h][:, j, :], banks[j][:, halves[h]], signs[:, j, halves[h]], MULT)
-                nc.scalar.activation(sigmoids[h][:, j, :], margins[h][:, j, :], SIGMOID, scale=-1.0)
+        def form_sigmoids(h, tag):
+            margins.append(keep.tile([P, PACK, half_n], F32, name="margins%d" % h, tag=tag, align_bytes=64))
+            sigmoids.append(keep.tile([P, PACK, half_n], F32, name="sigmoids%d" % h, align_bytes=64))
+            parts = [(cols.start, j, bank, cols) for j in range(PACK) for bank, cols in scores[h, j]]
+            for start, j, bank, cols in sorted(parts, key=lambda part: part[:2]):
+                nc.vector.tensor_tensor(margins[h][:, j, cols], bank, signs[h][:, j, cols], MULT)
+                nc.scalar.activation(sigmoids[h][:, j, cols], margins[h][:, j, cols], SIGMOID, scale=-1.0)
 
         def form_g(engine, h, factors, run):
             g_woven = keep.tile([P, half_n, PACK], BF16, name="g_woven%d" % h, align_bytes=64)
-            engine.tensor_tensor(
-                g_woven[:].rearrange("p (c i) j -> p c j i", i=run),
-                sigmoids[h][:].rearrange("p j (c i) -> p c j i", i=run),
-                factors[:].rearrange("p j (c i) -> p c j i", i=run),
-                MULT,
-            )
+            for cols in pieces(h == 0):
+                engine.tensor_tensor(
+                    g_woven[:, cols, :].rearrange("p (c i) j -> p c j i", i=run),
+                    sigmoids[h][:, :, cols].rearrange("p j (c i) -> p c j i", i=run),
+                    factors[:, :, cols].rearrange("p j (c i) -> p c j i", i=run),
+                    MULT,
+                )
             return g_woven
 
         def quantise_g(h, g_woven):
@@ -197,7 +244,8 @@ def tile_attend_gsig_w_kernel(tc, xT, w_words, w_scales, y, wt, xm, offs, out):
         xm_codes = {}
 
         def multiply(m, slots):
-            bank = grad_psum.tile([P, N], F32, name="grad")
+            bank = psum.tile([P, N], F32, name="grad", tag=grad_tags[len(grad_count) % len(grad_tags)])
+            grad_count.append(m)
             nc.tensor.matmul_mx(
                 bank[:],
                 lhsT=xm_codes[m].bitcast(E4M3),
@@ -216,7 +264,8 @@ def tile_attend_gsig_w_kernel(tc, xT, w_words, w_scales, y, wt, xm, offs, out):
             nc.vector.tensor_copy(windows[m % WINDOWS][:].indirect(listed), columns[:, slots])
 
         factors = form_factors(0, "x_woven%d_%d" % (PASSES - 1, 1))
-        form_sigmoids(0)
+        form_sigmoids(0, "margins0")
+        second_scores()
         early_woven = keep.tile([P, EARLY, P, PACK], BF16, name="early_woven", tag="margins0", align_bytes=64)
         early_codes = keep.tile([P, EARLY, P], U32, name="early_codes", align_bytes=64)
         for m in range(EARLY):
@@ -228,7 +277,7 @@ def tile_attend_gsig_w_kernel(tc, xT, w_words, w_scales, y, wt, xm, offs, out):
         early = [multiply(0, halves[0])]
         quantise_xm(1, 1, xm_codes[1], early_woven[:, 1])
         factors = form_factors(1, "g_woven0")
-        form_sigmoids(1)
+        form_sigmoids(1, "sigmoids0")
         quantise_xm(2, 1, xm_codes[2], early_woven[:, 2])
         early.extend(multiply(m, halves[0]) for m in range(1, EARLY))
         g_second = form_g(nc.gpsimd, 1, factors, PACK)
@@ -236,7 +285,7 @@ def tile_attend_gsig_w_kernel(tc, xT, w_words, w_scales, y, wt, xm, offs, out):
             scatter(m, early[m], halves[0])
         quantise_g(1, g_second)
         late = D_TILES - EARLY
-        late_woven = keep.tile([P, late * P, PACK], BF16, name="late_woven", tag="margins1", align_bytes=64)
+        late_woven = keep.tile([P, late * P, PACK], BF16, name="late_woven", tag="sigmoids0", align_bytes=64)
         late_codes = keep.tile([P, late * P], U32, name="late_codes", tag="g_woven1", align_bytes=64)
         for m in range(EARLY, D_TILES):
             cols = slice((m - EARLY) * P, (m - EARLY + 1) * P)
@@ -244,7 +293,7 @@ def tile_attend_gsig_w_kernel(tc, xT, w_words, w_scales, y, wt, xm, offs, out):
             xm_codes[m] = late_codes[:, cols]
         quantise_xm(EARLY, 1, late_codes[:, :P], late_woven[:, :P, :])
         quantise_xm(EARLY + 1, late - 1, late_codes[:, P:], late_woven[:, P:, :])
-        windows.append(zeroed_window(nc.gpsimd, "margins1"))
+        windows.append(zeroed_window(nc.gpsimd, "sigmoids0"))
         for m in range(D_TILES):
             slots = halves[1] if m < EARLY else whole
             scatter(m, multiply(m, slots), slots)

@@ -38,7 +38,6 @@ def tile_attend_gsig_w_kernel(tc, xT, w_words, w_scales, y, wt, xm, offs, out):
     nc = tc.nc
     with ExitStack() as ctx:
         keep = ctx.enter_context(tc.tile_pool(name="keep", bufs=1))
-        loads = ctx.enter_context(tc.tile_pool(name="loads", bufs=1))
         ring = ctx.enter_context(tc.tile_pool(name="ring", bufs=STAGED))
         psum = ctx.enter_context(tc.psum_pool(name="psum", bufs=1))
         half_n = N // 2
@@ -72,9 +71,7 @@ def tile_attend_gsig_w_kernel(tc, xT, w_words, w_scales, y, wt, xm, offs, out):
         def load_rows(tile, rows):
             nc.sync.dma_start(tile, rows.rearrange("(p t) c -> p t c", t=PACK))
 
-        early_d = EARLY * P
-        room = PACK * 4 * (early_d + half_n)
-        x_raw = [loads.tile([P, PACK, R], F32, name="x_raw%d" % o, offset=o * room) for o in range(PASSES)]
+        x_raw = [keep.tile([P, PACK, R], F32, name="x_raw%d" % o) for o in range(PASSES)]
         x_places = [slice(0, PAIR), slice(PAIR, PACK)]
         for o in range(PASSES):
             rows = xT[0, o * K_PASS : (o + 1) * K_PASS, :].rearrange("(p t) c -> p t c", t=PACK)
@@ -105,8 +102,11 @@ def tile_attend_gsig_w_kernel(tc, xT, w_words, w_scales, y, wt, xm, offs, out):
         word_pairs = picked_words[:].bitcast(U16).rearrange("p (n o) -> p o n", o=PASSES)
         nc.vector.tensor_copy(w_codes[:, 0, :], word_pairs[:, 0, :])
 
-        signs = [keep.tile([P, PACK, half_n], F32, name="signs0", tag="table_words")]
-        load_rows(signs[0][:], y[0, :, halves[0]])
+        all_signs = keep.tile([P, PACK, N], F32, name="signs", tag="table_words")
+        y_rows = y[0].rearrange("(p j) n -> p j n", j=PACK)
+        for first in range(0, PACK, PAIR):
+            nc.sync.dma_start(all_signs[:, first : first + PAIR, :], y_rows[:, first : first + PAIR, :])
+        signs = [all_signs[:, :, cols] for cols in halves]
 
         x_codes = [keep.tile([P, R], U32, name="x_codes%d" % o, align_bytes=64) for o in range(PASSES)]
         x_planes = [keep.tile([P, R], U8, name="x_plane%d" % o, align_bytes=64) for o in range(PASSES)]
@@ -142,14 +142,15 @@ def tile_attend_gsig_w_kernel(tc, xT, w_words, w_scales, y, wt, xm, offs, out):
                 nc.vector.tensor_copy(w_codes[:, 1, :], word_pairs[:, 1, :])
             quantise_x(o, cuts)
 
-        xm_early = loads.tile([P, PACK, early_d], F32, name="xm_early", offset=0)
-        signs.append(loads.tile([P, PACK, half_n], F32, name="signs1", offset=PACK * 4 * early_d))
-        xm_late = loads.tile([P, PACK, D - early_d], F32, name="xm_late", offset=room)
-        load_rows(xm_early[:], xm[0, :, :early_d])
-        load_rows(signs[1][:], y[0, :, halves[1]])
-        load_rows(xm_late[:], xm[0, :, early_d:])
-        xm_raw = [xm_early[:, :, m * P : (m + 1) * P] for m in range(EARLY)]
-        xm_raw.extend(xm_late[:, :, m * P : (m + 1) * P] for m in range(D_TILES - EARLY))
+        quarter = D // 4
+        low_tiles = D_TILES // 2
+        xm_low = keep.tile([P, 2, PACK, quarter], F32, name="xm_low", tag="x_raw0")
+        xm_high = keep.tile([P, PACK, D // 2], F32, name="xm_high", tag="x_raw1")
+        for c in range(2):
+            load_rows(xm_low[:, c], xm[0, :, c * quarter : (c + 1) * quarter])
+        load_rows(xm_high[:], xm[0, :, D // 2 :])
+        xm_raw = [xm_low[:, m // 2, :, m % 2 * P : (m % 2 + 1) * P] for m in range(low_tiles)]
+        xm_raw.extend(xm_high[:, :, m * P : (m + 1) * P] for m in range(low_tiles))
 
         def score_pass(bank, o, j, slots):
             cols = slice(j * P, (j + 1) * P)
@@ -192,7 +193,7 @@ def tile_attend_gsig_w_kernel(tc, xT, w_words, w_scales, y, wt, xm, offs, out):
         grad_tags = ["grad0", "grad1", "scores2_1", "scores3_1"]
         grad_count = []
 
-        margins, sigmoids = [], []
+        sigmoids = [keep.tile([P, PACK, half_n], F32, name="sigmoids%d" % h, align_bytes=64) for h in range(2)]
 
         def pieces(split):
             return [slice(0, half_n // 2), slice(half_n // 2, half_n)] if split else [slice(0, half_n)]
@@ -206,13 +207,13 @@ def tile_attend_gsig_w_kernel(tc, xT, w_words, w_scales, y, wt, xm, offs, out):
                     nc.gpsimd.tensor_scalar(factors[:, j, :], signs[h][:, j, :], negated[:, j : j + 1], 0.0, MULT, ADD)
             return factors
 
-        def form_sigmoids(h, tag):
-            margins.append(keep.tile([P, PACK, half_n], F32, name="margins%d" % h, tag=tag, align_bytes=64))
-            sigmoids.append(keep.tile([P, PACK, half_n], F32, name="sigmoids%d" % h, align_bytes=64))
-            parts = [(cols.start, j, bank, cols) for j in range(PACK) for bank, cols in scores[h, j]]
+        def form_sigmoids(h, tiles, tag):
+            margins = keep.tile([P, len(tiles), half_n], F32, name="margins", tag=tag, align_bytes=64)
+            parts = [(cols.start, j, bank, cols) for j in tiles for bank, cols in scores[h, j]]
             for start, j, bank, cols in sorted(parts, key=lambda part: part[:2]):
-                nc.vector.tensor_tensor(margins[h][:, j, cols], bank, signs[h][:, j, cols], MULT)
-                nc.scalar.activation(sigmoids[h][:, j, cols], margins[h][:, j, cols], SIGMOID, scale=-1.0)
+                margin = margins[:, j - tiles.start, cols]
+                nc.vector.tensor_tensor(margin, bank, signs[h][:, j, cols], MULT)
+                nc.scalar.activation(sigmoids[h][:, j, cols], margin, SIGMOID, scale=-1.0)
 
         def form_g(engine, h, factors, run):
             g_woven = keep.tile([P, half_n, PACK], BF16, name="g_woven%d" % h, align_bytes=64)
@@ -264,7 +265,8 @@ def tile_attend_gsig_w_kernel(tc, xT, w_words, w_scales, y, wt, xm, offs, out):
             nc.vector.tensor_copy(windows[m % WINDOWS][:].indirect(listed), columns[:, slots])
 
         factors = form_factors(0, "x_woven%d_%d" % (PASSES - 1, 1))
-        form_sigmoids(0, "margins0")
+        form_sigmoids(0, range(PACK), "margins0")
+        form_sigmoids(1, range(1), "margins1")
         second_scores()
         early_woven = keep.tile([P, EARLY, P, PACK], BF16, name="early_woven", tag="margins0", align_bytes=64)
         early_codes = keep.tile([P, EARLY, P], U32, name="early_codes", align_bytes=64)
@@ -277,7 +279,7 @@ def tile_attend_gsig_w_kernel(tc, xT, w_words, w_scales, y, wt, xm, offs, out):
         early = [multiply(0, halves[0])]
         quantise_xm(1, 1, xm_codes[1], early_woven[:, 1])
         factors = form_factors(1, "g_woven0")
-        form_sigmoids(1, "sigmoids0")
+        form_sigmoids(1, range(1, PACK), "sigmoids0")
         quantise_xm(2, 1, xm_codes[2], early_woven[:, 2])
         early.extend(multiply(m, halves[0]) for m in range(1, EARLY))
         g_second = form_g(nc.gpsimd, 1, factors, PACK)

@@ -244,7 +244,7 @@ def tile_attend_gsig_w_kernel(tc, xT, w_words, w_scales, y, wt, xm, offs, out):
 
         xm_codes = {}
 
-        def multiply(m, slots):
+        def multiply(m, slots, columns=None):
             bank = psum.tile([P, N], F32, name="grad", tag=grad_tags[len(grad_count) % len(grad_tags)])
             grad_count.append(m)
             nc.tensor.matmul_mx(
@@ -256,7 +256,8 @@ def tile_attend_gsig_w_kernel(tc, xT, w_words, w_scales, y, wt, xm, offs, out):
                 start=True,
                 stop=True,
             )
-            columns = ring.tile([P, N], F32, name="columns")
+            if columns is None:
+                columns = ring.tile([P, N], F32, name="columns")
             nc.scalar.copy(columns[:, slots], bank[:, slots])
             return columns
 
@@ -281,22 +282,20 @@ def tile_attend_gsig_w_kernel(tc, xT, w_words, w_scales, y, wt, xm, offs, out):
         factors = form_factors(1, "g_woven0")
         form_sigmoids(1, range(1, PACK), "sigmoids0")
         quantise_xm(2, 1, xm_codes[2], early_woven[:, 2])
-        early.extend(multiply(m, halves[0]) for m in range(1, EARLY))
-        g_second = form_g(nc.gpsimd, 1, factors, PACK)
-        for m in range(EARLY):
-            scatter(m, early[m], halves[0])
-        quantise_g(1, g_second)
-        late = D_TILES - EARLY
-        late_woven = keep.tile([P, late * P, PACK], BF16, name="late_woven", tag="sigmoids0", align_bytes=64)
-        late_codes = keep.tile([P, late * P], U32, name="late_codes", tag="g_woven1", align_bytes=64)
-        for m in range(EARLY, D_TILES):
-            cols = slice((m - EARLY) * P, (m - EARLY + 1) * P)
-            weave_xm(m, late_woven[:, cols, :])
-            xm_codes[m] = late_codes[:, cols]
-        quantise_xm(EARLY, 1, late_codes[:, :P], late_woven[:, :P, :])
-        quantise_xm(EARLY + 1, late - 1, late_codes[:, P:], late_woven[:, P:, :])
-        windows.append(zeroed_window(nc.gpsimd, "sigmoids0"))
-        for m in range(D_TILES):
+        early.append(multiply(1, halves[0]))
+
+        def late_xm(first, count, tag):
+            woven = keep.tile([P, count * P, PACK], BF16, name="late_woven", tag=tag, align_bytes=64)
+            codes = keep.tile([P, count * P], U32, name="late_codes%d" % first, align_bytes=64)
+            for k in range(count):
+                cols = slice(k * P, (k + 1) * P)
+                weave_xm(first + k, woven[:, cols, :])
+                xm_codes[first + k] = codes[:, cols]
+            for k in range(0, count, PAIR):
+                cols = slice(k * P, min(k + PAIR, count) * P)
+                quantise_xm(first + k, min(PAIR, count - k), codes[:, cols], woven[:, cols, :])
+
+        def finish(m):
             slots = halves[1] if m < EARLY else whole
             scatter(m, multiply(m, slots), slots)
             if m < D_TILES - 1:
@@ -304,3 +303,17 @@ def tile_attend_gsig_w_kernel(tc, xT, w_words, w_scales, y, wt, xm, offs, out):
             else:
                 for queue, cols in ((nc.sync, slice(0, T // 2)), (nc.scalar, slice(T // 2, T))):
                     queue.dma_start(out[m * P : (m + 1) * P, cols], windows[m % WINDOWS][:, cols])
+
+        g_second = form_g(nc.gpsimd, 1, factors, PACK)
+        for m in range(EARLY - 1):
+            scatter(m, early[m], halves[0])
+        late_xm(3, 2, "sigmoids0")
+        held = keep.tile([P, N], F32, name="held", tag="sigmoids1", align_bytes=64)
+        early.append(multiply(EARLY - 1, halves[0], held))
+        quantise_g(1, g_second)
+        scatter(EARLY - 1, early[EARLY - 1], halves[0])
+        late_xm(5, 3, "g_woven0")
+        finish(0)
+        windows.append(zeroed_window(nc.gpsimd, "g_woven0"))
+        for m in range(1, D_TILES):
+            finish(m)

@@ -198,14 +198,12 @@ def tile_attend_gsig_w_kernel(tc, xT, w_words, w_scales, y, wt, xm, offs, out):
         def pieces(split):
             return [slice(0, half_n // 2), slice(half_n // 2, half_n)] if split else [slice(0, half_n)]
 
-        def form_factors(h, tag):
-            factors = keep.tile([P, PACK, half_n], F32, name="factors%d" % h, tag=tag, align_bytes=64)
-            for j in range(PACK):
-                if h == 0 and j < PAIR:
+        def form_factors(h, factors, tiles):
+            for j in tiles:
+                if j < PAIR:
                     nc.scalar.activation(factors[:, j, :], signs[h][:, j, :], COPY, scale=negated[:, j : j + 1])
                 else:
                     nc.gpsimd.tensor_scalar(factors[:, j, :], signs[h][:, j, :], negated[:, j : j + 1], 0.0, MULT, ADD)
-            return factors
 
         def form_sigmoids(h, tiles, tag):
             margins = keep.tile([P, len(tiles), half_n], F32, name="margins", tag=tag, align_bytes=64)
@@ -215,8 +213,7 @@ def tile_attend_gsig_w_kernel(tc, xT, w_words, w_scales, y, wt, xm, offs, out):
                 nc.vector.tensor_tensor(margin, bank, signs[h][:, j, cols], MULT)
                 nc.scalar.activation(sigmoids[h][:, j, cols], margin, SIGMOID, scale=-1.0)
 
-        def form_g(engine, h, factors, run):
-            g_woven = keep.tile([P, half_n, PACK], BF16, name="g_woven%d" % h, align_bytes=64)
+        def form_g(engine, h, factors, g_woven, run):
             for cols in pieces(h == 0):
                 engine.tensor_tensor(
                     g_woven[:, cols, :].rearrange("p (c i) j -> p c j i", i=run),
@@ -224,11 +221,10 @@ def tile_attend_gsig_w_kernel(tc, xT, w_words, w_scales, y, wt, xm, offs, out):
                     factors[:, :, cols].rearrange("p j (c i) -> p c j i", i=run),
                     MULT,
                 )
-            return g_woven
 
         def quantise_g(h, g_woven):
             cols = halves[h]
-            nc.vector.quantize_mx(g_codes[:, cols].bitcast(E5M2), g_plane[:, cols], g_woven[:].rearrange("p n j -> p (n j)"))
+            nc.vector.quantize_mx(g_codes[:, cols].bitcast(E5M2), g_plane[:, cols], g_woven.rearrange("p n j -> p (n j)"))
 
         xm_plane = keep.tile([P, D], U8, name="xm_plane", align_bytes=64)
 
@@ -265,7 +261,12 @@ def tile_attend_gsig_w_kernel(tc, xT, w_words, w_scales, y, wt, xm, offs, out):
             listed = offsets[:, slots.start // PER_COLUMN : slots.stop // PER_COLUMN]
             nc.vector.tensor_copy(windows[m % WINDOWS][:].indirect(listed), columns[:, slots])
 
-        factors = form_factors(0, "x_woven%d_%d" % (PASSES - 1, 1))
+        factors = keep.tile([P, PACK, half_n], F32, name="factors0", tag="x_woven%d_%d" % (PASSES - 1, 1), align_bytes=64)
+        form_factors(0, factors, range(PACK))
+        second_bytes = keep.tile([P, PACK * half_n], F32, name="second_bytes", align_bytes=64)
+        second_factors = second_bytes[:].rearrange("p (j n) -> p j n", j=PACK)
+        g_first = second_bytes[:, PAIR * half_n :].bitcast(BF16).rearrange("p (n j) -> p n j", j=PACK)
+        form_factors(1, second_factors, range(PAIR))
         form_sigmoids(0, range(PACK), "margins0")
         form_sigmoids(1, range(1), "margins1")
         second_scores()
@@ -274,14 +275,14 @@ def tile_attend_gsig_w_kernel(tc, xT, w_words, w_scales, y, wt, xm, offs, out):
         for m in range(EARLY):
             weave_xm(m, early_woven[:, m])
             xm_codes[m] = early_codes[:, m, :]
-        g_first = form_g(nc.vector, 0, factors, PAIR)
+        form_g(nc.vector, 0, factors, g_first, PAIR)
         quantise_xm(0, 1, xm_codes[0], early_woven[:, 0])
         quantise_g(0, g_first)
         early = [multiply(0, halves[0])]
-        quantise_xm(1, 1, xm_codes[1], early_woven[:, 1])
-        factors = form_factors(1, "g_woven0")
+        form_factors(1, second_factors, range(PAIR, PACK))
         form_sigmoids(1, range(1, PACK), "sigmoids0")
-        quantise_xm(2, 1, xm_codes[2], early_woven[:, 2])
+        for m in range(1, EARLY):
+            quantise_xm(m, 1, xm_codes[m], early_woven[:, m])
         early.append(multiply(1, halves[0]))
 
         def late_xm(first, count, tag):
@@ -304,16 +305,17 @@ def tile_attend_gsig_w_kernel(tc, xT, w_words, w_scales, y, wt, xm, offs, out):
                 for queue, cols in ((nc.sync, slice(0, T // 2)), (nc.scalar, slice(T // 2, T))):
                     queue.dma_start(out[m * P : (m + 1) * P, cols], windows[m % WINDOWS][:, cols])
 
-        g_second = form_g(nc.gpsimd, 1, factors, PACK)
+        g_second = keep.tile([P, half_n, PACK], BF16, name="g_second", align_bytes=64)
+        form_g(nc.gpsimd, 1, second_factors, g_second[:], PACK)
         for m in range(EARLY - 1):
             scatter(m, early[m], halves[0])
         late_xm(3, 2, "sigmoids0")
         held = keep.tile([P, N], F32, name="held", tag="sigmoids1", align_bytes=64)
         early.append(multiply(EARLY - 1, halves[0], held))
-        quantise_g(1, g_second)
+        quantise_g(1, g_second[:])
         scatter(EARLY - 1, early[EARLY - 1], halves[0])
-        late_xm(5, 3, "g_woven0")
+        late_xm(5, 3, "second_bytes")
         finish(0)
-        windows.append(zeroed_window(nc.gpsimd, "g_woven0"))
+        windows.append(zeroed_window(nc.gpsimd, "second_bytes"))
         for m in range(1, D_TILES):
             finish(m)

@@ -30,7 +30,7 @@ PAIR = 2
 D_TILES = D // P
 PER_COLUMN = 16
 WINDOWS = 4
-EARLY = 3
+EARLY = 4
 STAGED = 6
 
 
@@ -78,15 +78,15 @@ def tile_attend_gsig_w_kernel(tc, xT, w_words, w_scales, y, wt, xm, offs, out):
             for places in x_places:
                 nc.sync.dma_start(x_raw[o][:, places, :], rows[:, places, :])
 
-        negated = keep.tile([P, PACK], F32, name="negated")
-        nc.gpsimd.tensor_scalar(negated[:], weights[:], -1.0, 0.0, MULT, ADD)
-
         def zeroed_window(engine, tag):
             window = keep.tile([P, T], F32, name="window", tag=tag, align_bytes=64)
             engine.memset(window[:].bitcast(I32), 0)
             return window
 
-        windows = [zeroed_window(nc.vector, "window0"), zeroed_window(nc.vector, "window1"), zeroed_window(nc.gpsimd, "weights")]
+        windows = [zeroed_window(nc.vector, "window%d" % m) for m in range(WINDOWS - 1)]
+        negated = keep.tile([P, PACK], F32, name="negated")
+        nc.vector.tensor_scalar(negated[:], weights[:], -1.0, 0.0, MULT, ADD)
+        windows.append(zeroed_window(nc.gpsimd, "weights"))
 
         picked_scales = keep.tile([P, N], U8, name="picked_scales", align_bytes=64)
         nc.vector.tensor_copy(picked_scales[:], table_scales[:].indirect(offsets[:]))
@@ -270,33 +270,51 @@ def tile_attend_gsig_w_kernel(tc, xT, w_words, w_scales, y, wt, xm, offs, out):
         form_sigmoids(0, range(PACK), "margins0")
         form_sigmoids(1, range(1), "margins1")
         second_scores()
-        early_woven = keep.tile([P, EARLY, P, PACK], BF16, name="early_woven", tag="margins0", align_bytes=64)
+        ahead = EARLY - 1
+        early_woven = keep.tile([P, ahead, P, PACK], BF16, name="early_woven", tag="margins0", align_bytes=64)
         early_codes = keep.tile([P, EARLY, P], U32, name="early_codes", align_bytes=64)
         for m in range(EARLY):
-            weave_xm(m, early_woven[:, m])
             xm_codes[m] = early_codes[:, m, :]
+        for m in range(ahead):
+            weave_xm(m, early_woven[:, m])
         form_g(nc.vector, 0, factors, g_first, PAIR)
         quantise_xm(0, 1, xm_codes[0], early_woven[:, 0])
         quantise_g(0, g_first)
         early = [multiply(0, halves[0])]
         form_factors(1, second_factors, range(PAIR, PACK))
-        form_sigmoids(1, range(1, PACK), "sigmoids0")
-        for m in range(1, EARLY):
+        form_sigmoids(1, range(1, PACK - 1), "sigmoids0")
+        g_second = keep.tile([P, half_n, PACK], BF16, name="g_second", tag="sigmoids0", align_bytes=64)
+        weave_xm(ahead, g_second[:, :P, :])
+        last_margins = "x_woven%d_%d" % (PASSES - 1, 1)
+        margin_last = keep.tile([P, half_n], F32, name="margin_last", tag=last_margins, align_bytes=64)
+        nc.vector.tensor_tensor(margin_last[:], scores[1, PACK - 1][0][0], signs[1][:, PACK - 1, :], MULT)
+        for m in range(1, ahead):
             quantise_xm(m, 1, xm_codes[m], early_woven[:, m])
         early.append(multiply(1, halves[0]))
+        nc.scalar.activation(sigmoids[1][:, PACK - 1, :], margin_last[:], SIGMOID, scale=-1.0)
+        scatter(0, early[0], halves[0])
+        quantise_xm(ahead, 1, xm_codes[ahead], g_second[:, :P, :])
+        early.append(multiply(2, halves[0]))
 
-        def late_xm(first, count, tag):
-            woven = keep.tile([P, count * P, PACK], BF16, name="late_woven", tag=tag, align_bytes=64)
-            codes = keep.tile([P, count * P], U32, name="late_codes%d" % first, align_bytes=64)
-            for k in range(count):
+        def late_xm(first, tag):
+            woven = keep.tile([P, PAIR * P, PACK], BF16, name="late_woven", tag=tag, align_bytes=64)
+            codes = keep.tile([P, PAIR * P], U32, name="late_codes%d" % first, align_bytes=64)
+            for k in range(PAIR):
                 cols = slice(k * P, (k + 1) * P)
                 weave_xm(first + k, woven[:, cols, :])
                 xm_codes[first + k] = codes[:, cols]
-            for k in range(0, count, PAIR):
-                cols = slice(k * P, min(k + PAIR, count) * P)
-                quantise_xm(first + k, min(PAIR, count - k), codes[:, cols], woven[:, cols, :])
+            quantise_xm(first, PAIR, codes[:], woven[:])
 
-        def finish(m):
+        form_g(nc.gpsimd, 1, second_factors, g_second[:], PACK)
+        for m in range(1, ahead):
+            scatter(m, early[m], halves[0])
+        late_xm(EARLY, last_margins)
+        held = keep.tile([P, N], F32, name="held", tag="sigmoids1", align_bytes=64)
+        early.append(multiply(ahead, halves[0], held))
+        quantise_g(1, g_second[:])
+        scatter(ahead, early[ahead], halves[0])
+        late_xm(EARLY + PAIR, "second_bytes")
+        for m in range(D_TILES):
             slots = halves[1] if m < EARLY else whole
             scatter(m, multiply(m, slots), slots)
             if m < D_TILES - 1:
@@ -304,18 +322,3 @@ def tile_attend_gsig_w_kernel(tc, xT, w_words, w_scales, y, wt, xm, offs, out):
             else:
                 for queue, cols in ((nc.sync, slice(0, T // 2)), (nc.scalar, slice(T // 2, T))):
                     queue.dma_start(out[m * P : (m + 1) * P, cols], windows[m % WINDOWS][:, cols])
-
-        g_second = keep.tile([P, half_n, PACK], BF16, name="g_second", align_bytes=64)
-        form_g(nc.gpsimd, 1, second_factors, g_second[:], PACK)
-        for m in range(EARLY - 1):
-            scatter(m, early[m], halves[0])
-        late_xm(3, 2, "sigmoids0")
-        held = keep.tile([P, N], F32, name="held", tag="sigmoids1", align_bytes=64)
-        early.append(multiply(EARLY - 1, halves[0], held))
-        quantise_g(1, g_second[:])
-        scatter(EARLY - 1, early[EARLY - 1], halves[0])
-        late_xm(5, 3, "second_bytes")
-        finish(0)
-        windows.append(zeroed_window(nc.gpsimd, "second_bytes"))
-        for m in range(1, D_TILES):
-            finish(m)

@@ -22,13 +22,13 @@ SIGMOID = mybir.ActivationFunctionType.Sigmoid
 P = 128
 QUADRANT = 32
 HALF_QUADRANT = 16
-LEAD = T // 2
 PACK = 4
+PAIR = 2
 K_PASS = P * PACK
 PASSES = D // K_PASS
-PAIR = 2
 D_TILES = D // P
 PER_COLUMN = 16
+HALF = N // 2
 WINDOWS = 4
 EARLY = 4
 STAGED = 6
@@ -40,55 +40,53 @@ def tile_attend_gsig_w_kernel(tc, xT, w_words, w_scales, y, wt, xm, offs, out):
         keep = ctx.enter_context(tc.tile_pool(name="keep", bufs=1))
         ring = ctx.enter_context(tc.tile_pool(name="ring", bufs=STAGED))
         psum = ctx.enter_context(tc.psum_pool(name="psum", bufs=1))
-        half_n = N // 2
-        halves = [slice(0, half_n), slice(half_n, N)]
-        whole = slice(0, N)
+        halves = [slice(0, HALF), slice(HALF, N)]
+        quarters = [slice(c * P, (c + 1) * P) for c in range(N // P)]
+        pairs = [slice(0, PAIR), slice(PAIR, PACK)]
+
+        def tile(shape, dtype, name, tag=None):
+            return keep.tile(shape, dtype, name=name, tag=tag or name, align_bytes=64)
 
         offsets = keep.tile([P, N // PER_COLUMN], U16, name="offsets")
-        weights = keep.tile([P, PACK], F32, name="weights", align_bytes=64)
+        weights = tile([P, PACK], F32, "weights")
         nc.scalar.dma_start(weights[:], wt[0].rearrange("(p j) o -> p (j o)", j=PACK))
-        table_words = keep.tile([P, T], I32, name="table_words")
+        table_words = tile([P, T], I32, "table_words")
         words = w_words[0].rearrange("p t b -> p (t b)").bitcast(I32)
-        nc.sync.dma_start(table_words[:, :LEAD], words[:, :LEAD])
+        nc.sync.dma_start(table_words[:, : T // 2], words[:, : T // 2])
         nc.sync.dma_start(offsets[:], offs)
-
-        table_scales = keep.tile([P, T], U8, name="table_scales")
+        table_scales = tile([P, T], U8, "table_scales")
         nc.vector.memset(table_scales[:].bitcast(I32), 0)
         scale_rows = w_scales.rearrange("o (q r) t -> r q o t", r=PACK)
         for r in range(PACK):
             nc.sync.dma_start(table_scales[r:P:HALF_QUADRANT, :].bitcast(I32), scale_rows[r].bitcast(I32))
-        nc.sync.dma_start(table_words[:, LEAD:], words[:, LEAD:])
-        moved_plane = keep.tile([P, N], U8, name="moved_plane", align_bytes=64)
+        nc.sync.dma_start(table_words[:, T // 2 :], words[:, T // 2 :])
+        x_first = tile([P, PACK, R], F32, "x_first")
+        x_third = tile([P, PAIR, R], F32, "x_third")
+        x_last = tile([P, PAIR, R], F32, "x_last")
+        x_raw = [[x_first[:, places, :] for places in pairs], [x_third[:], x_last[:]]]
+        for o in range(PASSES):
+            rows = xT[0, o * K_PASS : (o + 1) * K_PASS, :].rearrange("(p t) c -> p t c", t=PACK)
+            for e in range(PAIR):
+                nc.sync.dma_start(x_raw[o][e], rows[:, pairs[e], :])
+
+        moved_plane = tile([P, N], U8, "moved_plane")
         nc.vector.memset(moved_plane[:].bitcast(I32), 0)
-        g_codes = keep.tile([P, N], U32, name="g_codes", align_bytes=64)
-        g_plane = keep.tile([P, N], U8, name="g_plane", align_bytes=64)
-        nc.vector.memset(g_codes[:, halves[1]].bitcast(I32), 0)
-        nc.vector.memset(g_plane[:, halves[1]].bitcast(I32), 0)
         warm = keep.tile([P, 2], F32, name="warm")
         nc.vector.memset(warm[:, 0:1], 0.0)
         nc.scalar.activation(warm[:, 1:2], warm[:, 0:1], SIGMOID)
 
-        def load_rows(tile, rows):
-            nc.sync.dma_start(tile, rows.rearrange("(p t) c -> p t c", t=PACK))
-
-        x_raw = [keep.tile([P, PACK, R], F32, name="x_raw%d" % o) for o in range(PASSES)]
-        x_places = [slice(0, PAIR), slice(PAIR, PACK)]
-        for o in range(PASSES):
-            rows = xT[0, o * K_PASS : (o + 1) * K_PASS, :].rearrange("(p t) c -> p t c", t=PACK)
-            for places in x_places:
-                nc.sync.dma_start(x_raw[o][:, places, :], rows[:, places, :])
-
         def zeroed_window(engine, tag):
-            window = keep.tile([P, T], F32, name="window", tag=tag, align_bytes=64)
+            window = tile([P, T], F32, "window", tag)
             engine.memset(window[:].bitcast(I32), 0)
             return window
 
-        windows = [zeroed_window(nc.vector, "window%d" % m) for m in range(WINDOWS - 1)]
+        windows = [zeroed_window(nc.vector, "window%d" % m) for m in range(PAIR)]
         negated = keep.tile([P, PACK], F32, name="negated")
         nc.vector.tensor_scalar(negated[:], weights[:], -1.0, 0.0, MULT, ADD)
+        windows.append(zeroed_window(nc.vector, "window2"))
         windows.append(zeroed_window(nc.gpsimd, "weights"))
 
-        picked_scales = keep.tile([P, N], U8, name="picked_scales", align_bytes=64)
+        picked_scales = tile([P, N], U8, "picked_scales")
         nc.vector.tensor_copy(picked_scales[:], table_scales[:].indirect(offsets[:]))
         for q in range(P // QUADRANT):
             nc.sync.dma_start(
@@ -96,157 +94,145 @@ def tile_attend_gsig_w_kernel(tc, xT, w_words, w_scales, y, wt, xm, offs, out):
                 picked_scales[QUADRANT * q + HALF_QUADRANT : QUADRANT * q + HALF_QUADRANT + PACK, :].bitcast(I32),
             )
         w_planes = [picked_scales, moved_plane]
-        picked_words = keep.tile([P, N], U32, name="picked_words")
+        picked_words = tile([P, N], U32, "picked_words")
         nc.vector.tensor_copy(picked_words[:], table_words[:].bitcast(U32).indirect(offsets[:]))
-        w_codes = keep.tile([P, PASSES, N], U16, name="w_codes", align_bytes=64)
+        w_codes = tile([P, PASSES, N], U16, "w_codes")
         word_pairs = picked_words[:].bitcast(U16).rearrange("p (n o) -> p o n", o=PASSES)
         nc.vector.tensor_copy(w_codes[:, 0, :], word_pairs[:, 0, :])
 
-        all_signs = keep.tile([P, PACK, N], F32, name="signs", tag="table_words")
         y_rows = y[0].rearrange("(p j) n -> p j n", j=PACK)
-        for first in range(0, PACK, PAIR):
-            nc.sync.dma_start(all_signs[:, first : first + PAIR, :], y_rows[:, first : first + PAIR, :])
-        signs = [all_signs[:, :, cols] for cols in halves]
+        sign_tags = ["table_scales", "table_words"]
+        sign_pairs = [tile([P, PAIR, HALF], F32, "first_signs", tag) for tag in sign_tags]
+        for e in range(PAIR):
+            nc.sync.dma_start(sign_pairs[e][:], y_rows[:, pairs[e], halves[0]])
+        first_signs = [sign_pairs[j // PAIR][:, j % PAIR, :] for j in range(PACK)]
 
-        x_codes = [keep.tile([P, R], U32, name="x_codes%d" % o, align_bytes=64) for o in range(PASSES)]
-        x_planes = [keep.tile([P, R], U8, name="x_plane%d" % o, align_bytes=64) for o in range(PASSES)]
-        x_woven = [
-            [keep.tile([P, PAIR, P, PACK], BF16, name="x_woven%d_%d" % (o, e), align_bytes=64) for e in range(PACK // PAIR)]
-            for o in range(PASSES)
-        ]
+        x_codes = [tile([P, R], U32, "x_codes%d" % o) for o in range(PASSES)]
+        x_planes = [tile([P, R], U8, "x_plane%d" % o) for o in range(PASSES)]
+        x_woven = [[tile([P, PAIR, P, PACK], BF16, "x_woven%d_%d" % (o, e)) for e in range(PAIR)] for o in range(PASSES)]
 
-        def weave_x(o):
-            low, high = x_places
-            if o == 0:
-                shares = ((nc.scalar.copy, 0, low), (nc.vector.tensor_copy, 0, high), (nc.scalar.copy, PAIR, slice(0, PACK)))
-            else:
-                shares = [(copy, first, places) for places in x_places for copy, first in ((nc.vector.tensor_copy, 0), (nc.scalar.copy, PAIR))]
-            for copy, first, places in shares:
-                copy(
-                    x_woven[o][first // PAIR][:].rearrange("p j s t -> p s t j")[:, :, places, :],
-                    x_raw[o][:].rearrange("p t (s j) -> p s t j", j=PACK)[:, :, places, first : first + PAIR],
-                )
+        def weave_x(copy, o, e, places, raw):
+            copy(
+                x_woven[o][e][:].rearrange("p j s t -> p s t j")[:, :, places, :],
+                raw.rearrange("p t (s j) -> p s t j", j=PACK)[:, :, :, pairs[e]],
+            )
 
-        def quantise_x(o, cuts):
-            for lo, hi in zip(cuts[:-1], cuts[1:]):
-                cols = slice(lo * P, hi * P)
-                nc.vector.quantize_mx(
-                    x_codes[o][:, cols].bitcast(E4M3),
-                    x_planes[o][:, cols],
-                    x_woven[o][lo // PAIR][:, lo % PAIR : lo % PAIR + hi - lo, :, :].rearrange("p j s t -> p (j s t)"),
-                )
+        def quantise_x(o, first, count):
+            cols = slice(first * P, (first + count) * P)
+            woven = x_woven[o][first // PAIR][:, first % PAIR : first % PAIR + count, :, :]
+            nc.vector.quantize_mx(x_codes[o][:, cols].bitcast(E4M3), x_planes[o][:, cols], woven.rearrange("p j s t -> p (j s t)"))
 
-        for o, cuts in enumerate(((0, 1, 2, 4), (0, 1, 2, 4))):
-            weave_x(o)
-            if o == 0:
-                nc.vector.tensor_copy(w_codes[:, 1, :], word_pairs[:, 1, :])
-            quantise_x(o, cuts)
+        weave_x(nc.scalar.copy, 0, 0, pairs[0], x_raw[0][0])
+        weave_x(nc.vector.tensor_copy, 0, 0, pairs[1], x_raw[0][1])
+        weave_x(nc.scalar.copy, 0, 1, slice(0, PACK), x_first[:])
+        nc.vector.tensor_copy(w_codes[:, 1, :], word_pairs[:, 1, :])
+        for e in range(PAIR):
+            quantise_x(0, e * PAIR, PAIR)
+        for places in range(PAIR):
+            weave_x(nc.vector.tensor_copy, 1, 0, pairs[places], x_raw[1][places])
+            weave_x(nc.scalar.copy, 1, 1, pairs[places], x_raw[1][places])
+        for j in range(PACK):
+            quantise_x(1, j, 1)
 
-        quarter = D // 4
-        low_tiles = D_TILES // 2
-        xm_low = keep.tile([P, 2, PACK, quarter], F32, name="xm_low", tag="x_raw0")
-        xm_high = keep.tile([P, PACK, D // 2], F32, name="xm_high", tag="x_raw1")
-        for c in range(2):
-            load_rows(xm_low[:, c], xm[0, :, c * quarter : (c + 1) * quarter])
-        load_rows(xm_high[:], xm[0, :, D // 2 :])
-        xm_raw = [xm_low[:, m // 2, :, m % 2 * P : (m % 2 + 1) * P] for m in range(low_tiles)]
-        xm_raw.extend(xm_high[:, :, m * P : (m + 1) * P] for m in range(low_tiles))
+        xm_rows = xm[0].rearrange("(p t) c -> p t c", t=PACK)
+        after_first = tile([P, PAIR, PACK, HALF], F32, "after_first", "x_first")
+        xm_second = tile([P, PACK, PAIR * P], F32, "xm_second", "x_third")
+        xm_high = tile([P, PACK, D // 2], F32, "xm_high", "x_last")
+        nc.sync.dma_start(after_first[:, 0], xm_rows[:, :, : PAIR * P])
+        nc.sync.dma_start(after_first[:, 1], y_rows[:, :, halves[1]])
+        nc.sync.dma_start(xm_second[:], xm_rows[:, :, PAIR * P : PACK * P])
+        nc.sync.dma_start(xm_high[:], xm_rows[:, :, D // 2 :])
+        second_signs = [after_first[:, 1, j, :] for j in range(PACK)]
+        xm_raw = [after_first[:, 0, :, cols] for cols in quarters[:PAIR]]
+        xm_raw.extend(xm_second[:, :, cols] for cols in quarters[:PAIR])
+        xm_raw.extend(xm_high[:, :, cols] for cols in quarters)
 
         def score_pass(bank, o, j, slots):
-            cols = slice(j * P, (j + 1) * P)
             nc.tensor.matmul_mx(
                 bank,
-                lhsT=x_codes[o][:, cols].bitcast(E4M3),
-                lhsT_scale=x_planes[o][:, cols],
+                lhsT=x_codes[o][:, quarters[j]].bitcast(E4M3),
+                lhsT_scale=x_planes[o][:, quarters[j]],
                 rhs=w_codes[:, o, slots].bitcast(E2M1),
                 rhs_scale=w_planes[o][:, slots],
                 start=(o == 0),
                 stop=(o == PASSES - 1),
             )
 
-        quarters = [slice(c * P, (c + 1) * P) for c in range(N // P)]
-        scores = {}
-        groups = []
-        for j in range(PAIR):
-            bank = psum.tile([P, N], F32, name="scores%d" % j)
-            groups.append((bank[:], j, whole))
-            for h in range(2):
-                scores[h, j] = [(bank[:, halves[h]], slice(0, half_n))]
-        for j in range(PAIR, PACK):
-            scores[0, j] = []
-            for c in range(2):
-                bank = psum.tile([P, P], F32, name="scores%d_%d" % (j, c))
-                groups.append((bank[:], j, quarters[c]))
-                scores[0, j].append((bank[:], quarters[c]))
+        first_scores = [[psum.tile([P, P], F32, name="scores", tag="bank%d" % (PACK * c + j)) for j in range(PACK)] for c in range(PAIR)]
         for o in range(PASSES):
-            for bank, j, slots in groups:
-                score_pass(bank, o, j, slots)
+            for c in range(PAIR):
+                for j in range(PACK):
+                    score_pass(first_scores[c][j][:], o, j, quarters[c])
 
-        def second_scores():
-            for j in range(PAIR, PACK):
-                bank = psum.tile([P, half_n], F32, name="second%d" % j, tag="scores%d_0" % j)
-                scores[1, j] = [(bank[:], slice(0, half_n))]
-                for c in range(2):
-                    for o in range(PASSES):
-                        score_pass(bank[:, quarters[c]], o, j, quarters[2 + c])
+        first_factors = tile([P, PACK, HALF], F32, "first_factors", "x_woven1_1")
 
-        grad_tags = ["grad0", "grad1", "scores2_1", "scores3_1"]
-        grad_count = []
-
-        sigmoids = [keep.tile([P, PACK, half_n], F32, name="sigmoids%d" % h, align_bytes=64) for h in range(2)]
-
-        def pieces(split):
-            return [slice(0, half_n // 2), slice(half_n // 2, half_n)] if split else [slice(0, half_n)]
-
-        def form_factors(h, factors, tiles):
-            for j in tiles:
+        def form_factors(factors, signs):
+            for j in range(PACK):
                 if j < PAIR:
-                    nc.scalar.activation(factors[:, j, :], signs[h][:, j, :], COPY, scale=negated[:, j : j + 1])
+                    nc.scalar.activation(factors[:, j, :], signs[j], COPY, scale=negated[:, j : j + 1])
                 else:
-                    nc.gpsimd.tensor_scalar(factors[:, j, :], signs[h][:, j, :], negated[:, j : j + 1], 0.0, MULT, ADD)
+                    nc.gpsimd.tensor_scalar(factors[:, j, :], signs[j], negated[:, j : j + 1], 0.0, MULT, ADD)
 
-        def form_sigmoids(h, tiles, tag):
-            margins = keep.tile([P, len(tiles), half_n], F32, name="margins", tag=tag, align_bytes=64)
-            parts = [(cols.start, j, bank, cols) for j in tiles for bank, cols in scores[h, j]]
-            for start, j, bank, cols in sorted(parts, key=lambda part: part[:2]):
-                margin = margins[:, j - tiles.start, cols]
-                nc.vector.tensor_tensor(margin, bank, signs[h][:, j, cols], MULT)
-                nc.scalar.activation(sigmoids[h][:, j, cols], margin, SIGMOID, scale=-1.0)
+        form_factors(first_factors[:], first_signs)
+        shared = tile([P, PACK * HALF], F32, "shared")
+        own = tile([P, PACK * HALF], F32, "own")
+        first_sigmoids = [t[:, :N].rearrange("p (j n) -> p j n", j=PACK) for t in (own, shared)]
+        first_margins = [t[:, N:].rearrange("p (j n) -> p j n", j=PACK) for t in (own, shared)]
+        for c in range(PAIR):
+            for tiles in (range(0, PAIR), range(PAIR, PAIR + 1), range(PAIR + 1, PACK)):
+                for j in tiles:
+                    nc.vector.tensor_tensor(first_margins[c][:, j, :], first_scores[c][j][:], first_signs[j][:, quarters[c]], MULT)
+                these = slice(tiles.start, tiles.stop)
+                nc.scalar.activation(first_sigmoids[c][:, these, :], first_margins[c][:, these, :], SIGMOID, scale=-1.0)
 
-        def form_g(engine, h, factors, g_woven, run):
-            for cols in pieces(h == 0):
-                engine.tensor_tensor(
-                    g_woven[:, cols, :].rearrange("p (c i) j -> p c j i", i=run),
-                    sigmoids[h][:, :, cols].rearrange("p j (c i) -> p c j i", i=run),
-                    factors[:, :, cols].rearrange("p j (c i) -> p c j i", i=run),
-                    MULT,
-                )
+        g_plane = tile([P, N], U8, "g_plane", sign_tags[0])
+        g_codes = tile([P, N], U32, "g_codes", sign_tags[1])
+        nc.gpsimd.memset(g_plane[:, halves[1]].bitcast(I32), 0)
+        nc.gpsimd.memset(g_codes[:, halves[1]].bitcast(I32), 0)
 
-        def quantise_g(h, g_woven):
+        second_scores = []
+        for j in range(PACK):
+            bank = psum.tile([P, HALF], F32, name="scores", tag="bank%d" % j)
+            second_scores.append(bank)
+            for c in range(PAIR):
+                for o in range(PASSES):
+                    score_pass(bank[:, quarters[c]], o, j, quarters[PAIR + c])
+
+        def form_g(engine, woven, sigmoids, factors, run):
+            engine.tensor_tensor(
+                woven.rearrange("p (c i) j -> p c j i", i=run),
+                sigmoids.rearrange("p j (c i) -> p c j i", i=run),
+                factors.rearrange("p j (c i) -> p c j i", i=run),
+                MULT,
+            )
+
+        def quantise_g(h, woven):
             cols = halves[h]
-            nc.vector.quantize_mx(g_codes[:, cols].bitcast(E5M2), g_plane[:, cols], g_woven.rearrange("p n j -> p (n j)"))
+            nc.vector.quantize_mx(g_codes[:, cols].bitcast(E5M2), g_plane[:, cols], woven.rearrange("p n j -> p (n j)"))
 
-        xm_plane = keep.tile([P, D], U8, name="xm_plane", align_bytes=64)
+        xm_codes = tile([P, D], U32, "xm_codes")
+        xm_plane = tile([P, D], U8, "xm_plane")
 
-        def weave_xm(m, woven):
-            nc.scalar.copy(
+        def weave_views(m, woven):
+            return (
                 woven.rearrange("p (c i) t -> p c t i", i=PACK),
                 xm_raw[m].rearrange("p t (c i) -> p c t i", i=PACK),
             )
 
-        def quantise_xm(first, count, codes, woven):
-            plane = xm_plane[:, first * P : (first + count) * P]
-            nc.vector.quantize_mx(codes.bitcast(E4M3), plane, woven.rearrange("p c t -> p (c t)"))
+        def quantise_xm(first, count, woven):
+            cols = slice(first * P, (first + count) * P)
+            nc.vector.quantize_mx(xm_codes[:, cols].bitcast(E4M3), xm_plane[:, cols], woven.rearrange("p c t -> p (c t)"))
 
-        xm_codes = {}
+        passes_done = []
 
         def multiply(m, slots, columns=None):
-            bank = psum.tile([P, N], F32, name="grad", tag=grad_tags[len(grad_count) % len(grad_tags)])
-            grad_count.append(m)
+            bank = psum.tile([P, N], F32, name="grad", tag="bank%d" % (PACK + len(passes_done) % PACK))
+            passes_done.append(m)
+            cols = slice(m * P, (m + 1) * P)
             nc.tensor.matmul_mx(
                 bank[:],
-                lhsT=xm_codes[m].bitcast(E4M3),
-                lhsT_scale=xm_plane[:, m * P : (m + 1) * P],
+                lhsT=xm_codes[:, cols].bitcast(E4M3),
+                lhsT_scale=xm_plane[:, cols],
                 rhs=g_codes[:].bitcast(E5M2),
                 rhs_scale=g_plane[:],
                 start=True,
@@ -261,61 +247,65 @@ def tile_attend_gsig_w_kernel(tc, xT, w_words, w_scales, y, wt, xm, offs, out):
             listed = offsets[:, slots.start // PER_COLUMN : slots.stop // PER_COLUMN]
             nc.vector.tensor_copy(windows[m % WINDOWS][:].indirect(listed), columns[:, slots])
 
-        factors = keep.tile([P, PACK, half_n], F32, name="factors0", tag="x_woven%d_%d" % (PASSES - 1, 1), align_bytes=64)
-        form_factors(0, factors, range(PACK))
-        second_bytes = keep.tile([P, PACK * half_n], F32, name="second_bytes", align_bytes=64)
-        second_factors = second_bytes[:].rearrange("p (j n) -> p j n", j=PACK)
-        g_first = second_bytes[:, PAIR * half_n :].bitcast(BF16).rearrange("p (n j) -> p n j", j=PACK)
-        form_factors(1, second_factors, range(PAIR))
-        form_sigmoids(0, range(PACK), "margins0")
-        form_sigmoids(1, range(1), "margins1")
-        second_scores()
-        ahead = EARLY - 1
-        early_woven = keep.tile([P, ahead, P, PACK], BF16, name="early_woven", tag="margins0", align_bytes=64)
-        early_codes = keep.tile([P, EARLY, P], U32, name="early_codes", align_bytes=64)
-        for m in range(EARLY):
-            xm_codes[m] = early_codes[:, m, :]
-        for m in range(ahead):
-            weave_xm(m, early_woven[:, m])
-        form_g(nc.vector, 0, factors, g_first, PAIR)
-        quantise_xm(0, 1, xm_codes[0], early_woven[:, 0])
-        quantise_g(0, g_first)
+        low_woven = shared[:, N:].bitcast(BF16).rearrange("p (m c t) -> p m c t", m=PAIR, t=PACK)
+        for m in range(PAIR):
+            nc.scalar.copy(*weave_views(m, low_woven[:, m]))
+        g_first = tile([P, HALF, PACK], BF16, "g_first")
+        for c in range(PAIR):
+            form_g(nc.vector, g_first[:, quarters[c], :], first_sigmoids[c], first_factors[:, :, quarters[c]], PAIR)
+        quantise_xm(0, 1, low_woven[:, 0])
+        quantise_g(0, g_first[:])
         early = [multiply(0, halves[0])]
-        form_factors(1, second_factors, range(PAIR, PACK))
-        form_sigmoids(1, range(1, PACK - 1), "sigmoids0")
-        g_second = keep.tile([P, half_n, PACK], BF16, name="g_second", tag="sigmoids0", align_bytes=64)
-        weave_xm(ahead, g_second[:, :P, :])
-        last_margins = "x_woven%d_%d" % (PASSES - 1, 1)
-        margin_last = keep.tile([P, half_n], F32, name="margin_last", tag=last_margins, align_bytes=64)
-        nc.vector.tensor_tensor(margin_last[:], scores[1, PACK - 1][0][0], signs[1][:, PACK - 1, :], MULT)
-        for m in range(1, ahead):
-            quantise_xm(m, 1, xm_codes[m], early_woven[:, m])
+        quantise_xm(1, 1, low_woven[:, 1])
+
+        second_factors = shared[:].rearrange("p (j n) -> p j n", j=PACK)
+        form_factors(second_factors, second_signs)
+        second_sigmoids = tile([P, PACK, HALF], F32, "second_sigmoids")
+        second_margins = tile([P, (PACK + 1) * HALF], F32, "second_margins", "g_first")
+        margin_of = [second_margins[:, (j + 1) * HALF : (j + 2) * HALF] for j in range(PACK)]
+
+        def rewoven(first):
+            words = second_margins[:, first * HALF : first * HALF + N]
+            return words.bitcast(BF16).rearrange("p (n j) -> p n j", j=PACK)
+
+        def second_margin(j):
+            nc.vector.tensor_tensor(margin_of[j], second_scores[j][:], second_signs[j], MULT)
+
+        def second_sigmoid(j):
+            nc.scalar.activation(second_sigmoids[:, j, :], margin_of[j], SIGMOID, scale=-1.0)
+
+        for j in range(PACK):
+            second_margin(j)
+        for j in range(PAIR):
+            second_sigmoid(j)
+        mid_woven = rewoven(0)
+        g_second = rewoven(1)
+        woven, raw = weave_views(PAIR, mid_woven[:, quarters[0], :])
+        nc.gpsimd.tensor_scalar(woven, raw, 1.0, 0.0, MULT, ADD)
+        nc.scalar.copy(*weave_views(PAIR + 1, mid_woven[:, quarters[1], :]))
         early.append(multiply(1, halves[0]))
-        nc.scalar.activation(sigmoids[1][:, PACK - 1, :], margin_last[:], SIGMOID, scale=-1.0)
+        for j in range(PAIR, PACK):
+            second_sigmoid(j)
         scatter(0, early[0], halves[0])
-        quantise_xm(ahead, 1, xm_codes[ahead], g_second[:, :P, :])
-        early.append(multiply(2, halves[0]))
+        quantise_xm(PAIR, PAIR, mid_woven)
+        form_g(nc.gpsimd, g_second, second_sigmoids[:], second_factors, PACK)
+        scatter(1, early[1], halves[0])
+        scatter(PAIR, multiply(PAIR, halves[0]), halves[0])
 
-        def late_xm(first, tag):
-            woven = keep.tile([P, PAIR * P, PACK], BF16, name="late_woven", tag=tag, align_bytes=64)
-            codes = keep.tile([P, PAIR * P], U32, name="late_codes%d" % first, align_bytes=64)
+        def late_xm(first, late_woven):
             for k in range(PAIR):
-                cols = slice(k * P, (k + 1) * P)
-                weave_xm(first + k, woven[:, cols, :])
-                xm_codes[first + k] = codes[:, cols]
-            quantise_xm(first, PAIR, codes[:], woven[:])
+                nc.scalar.copy(*weave_views(first + k, late_woven[:, quarters[k], :]))
+            quantise_xm(first, PAIR, late_woven)
 
-        form_g(nc.gpsimd, 1, second_factors, g_second[:], PACK)
-        for m in range(1, ahead):
-            scatter(m, early[m], halves[0])
-        late_xm(EARLY, last_margins)
-        held = keep.tile([P, N], F32, name="held", tag="sigmoids1", align_bytes=64)
-        early.append(multiply(ahead, halves[0], held))
-        quantise_g(1, g_second[:])
-        scatter(ahead, early[ahead], halves[0])
-        late_xm(EARLY + PAIR, "second_bytes")
+        late_xm(EARLY, rewoven(PAIR + 1))
+        held = tile([P, HALF], F32, "held", "second_sigmoids")
+        multiply(EARLY - 1, halves[0], held)
+        quantise_g(1, g_second)
+        scatter(EARLY - 1, held, halves[0])
+        last_woven = tile([P, PAIR * P, PACK], BF16, "last_woven", "shared")
+        late_xm(EARLY + PAIR, last_woven[:])
         for m in range(D_TILES):
-            slots = halves[1] if m < EARLY else whole
+            slots = halves[1] if m < EARLY else slice(0, N)
             scatter(m, multiply(m, slots), slots)
             if m < D_TILES - 1:
                 nc.sync.dma_start(out[m * P : (m + 1) * P, :], windows[m % WINDOWS][:])

@@ -135,15 +135,17 @@ def tile_attend_gsig_w_kernel(tc, xT, w_words, w_scales, y, wt, xm, offs, out):
             quantise_x(1, j, 1)
 
         xm_rows = xm[0].rearrange("(p t) c -> p t c", t=PACK)
-        after_first = tile([P, PAIR, PACK, HALF], F32, "after_first", "x_first")
+        after_first = tile([P, PAIR * PACK * HALF], F32, "after_first", "x_first")
+        xm_first = after_first[:, : PACK * HALF].rearrange("p (t c) -> p t c", t=PACK)
+        y_second = after_first[:, PACK * HALF :].rearrange("p (j n) -> p j n", j=PACK)
         xm_second = tile([P, PACK, PAIR * P], F32, "xm_second", "x_third")
         xm_high = tile([P, PACK, D // 2], F32, "xm_high", "x_last")
-        nc.sync.dma_start(after_first[:, 0], xm_rows[:, :, : PAIR * P])
-        nc.sync.dma_start(after_first[:, 1], y_rows[:, :, halves[1]])
+        nc.sync.dma_start(xm_first, xm_rows[:, :, : PAIR * P])
+        nc.sync.dma_start(y_second, y_rows[:, :, halves[1]])
         nc.sync.dma_start(xm_second[:], xm_rows[:, :, PAIR * P : PACK * P])
         nc.sync.dma_start(xm_high[:], xm_rows[:, :, D // 2 :])
-        second_signs = [after_first[:, 1, j, :] for j in range(PACK)]
-        xm_raw = [after_first[:, 0, :, cols] for cols in quarters[:PAIR]]
+        second_signs = [y_second[:, j, :] for j in range(PACK)]
+        xm_raw = [xm_first[:, :, cols] for cols in quarters[:PAIR]]
         xm_raw.extend(xm_second[:, :, cols] for cols in quarters[:PAIR])
         xm_raw.extend(xm_high[:, :, cols] for cols in quarters)
 
@@ -174,10 +176,10 @@ def tile_attend_gsig_w_kernel(tc, xT, w_words, w_scales, y, wt, xm, offs, out):
                     nc.gpsimd.tensor_scalar(factors[:, j, :], signs[j], negated[:, j : j + 1], 0.0, MULT, ADD)
 
         form_factors(first_factors[:], first_signs)
-        shared = tile([P, PACK * HALF], F32, "shared")
+        shared = tile([P, (PACK + 1) * HALF], F32, "shared")
         own = tile([P, PACK * HALF], F32, "own")
         first_sigmoids = [t[:, :N].rearrange("p (j n) -> p j n", j=PACK) for t in (own, shared)]
-        first_margins = [t[:, N:].rearrange("p (j n) -> p j n", j=PACK) for t in (own, shared)]
+        first_margins = [t[:, N : PAIR * N].rearrange("p (j n) -> p j n", j=PACK) for t in (own, shared)]
         for c in range(PAIR):
             for tiles in (range(0, PAIR), range(PAIR, PAIR + 1), range(PAIR + 1, PACK)):
                 for j in tiles:
@@ -247,25 +249,27 @@ def tile_attend_gsig_w_kernel(tc, xT, w_words, w_scales, y, wt, xm, offs, out):
             listed = offsets[:, slots.start // PER_COLUMN : slots.stop // PER_COLUMN]
             nc.vector.tensor_copy(windows[m % WINDOWS][:].indirect(listed), columns[:, slots])
 
-        low_woven = shared[:, N:].bitcast(BF16).rearrange("p (m c t) -> p m c t", m=PAIR, t=PACK)
+        split = PAIR * N - P // 2
+        low_woven = [
+            shared[:, first : first + HALF].bitcast(BF16).rearrange("p (c t) -> p c t", t=PACK) for first in (split, split - HALF)
+        ]
         for m in range(PAIR):
-            nc.scalar.copy(*weave_views(m, low_woven[:, m]))
+            nc.scalar.copy(*weave_views(m, low_woven[m]))
         g_first = tile([P, HALF, PACK], BF16, "g_first")
         for c in range(PAIR):
             form_g(nc.vector, g_first[:, quarters[c], :], first_sigmoids[c], first_factors[:, :, quarters[c]], PAIR)
-        quantise_xm(0, 1, low_woven[:, 0])
+        quantise_xm(0, 1, low_woven[0])
         quantise_g(0, g_first[:])
         early = [multiply(0, halves[0])]
-        quantise_xm(1, 1, low_woven[:, 1])
+        quantise_xm(1, 1, low_woven[1])
 
-        second_factors = shared[:].rearrange("p (j n) -> p j n", j=PACK)
+        second_factors = shared[:, : PACK * HALF].rearrange("p (j n) -> p j n", j=PACK)
         form_factors(second_factors, second_signs)
         second_sigmoids = tile([P, PACK, HALF], F32, "second_sigmoids")
-        second_margins = tile([P, (PACK + 1) * HALF], F32, "second_margins", "g_first")
-        margin_of = [second_margins[:, (j + 1) * HALF : (j + 2) * HALF] for j in range(PACK)]
+        second_margins = tile([P, PACK * HALF], F32, "second_margins", "g_first")
+        margin_of = [second_margins[:, j * HALF : (j + 1) * HALF] for j in range(PACK)]
 
-        def rewoven(first):
-            words = second_margins[:, first * HALF : first * HALF + N]
+        def rewoven(words):
             return words.bitcast(BF16).rearrange("p (n j) -> p n j", j=PACK)
 
         def second_margin(j):
@@ -278,16 +282,15 @@ def tile_attend_gsig_w_kernel(tc, xT, w_words, w_scales, y, wt, xm, offs, out):
             second_margin(j)
         for j in range(PAIR):
             second_sigmoid(j)
-        mid_woven = rewoven(0)
-        g_second = rewoven(1)
-        woven, raw = weave_views(PAIR, mid_woven[:, quarters[0], :])
+        g_second = rewoven(after_first[:, PACK * HALF : PACK * HALF + N])
+        woven, raw = weave_views(PAIR, g_second[:, quarters[0], :])
         nc.gpsimd.tensor_scalar(woven, raw, 1.0, 0.0, MULT, ADD)
-        nc.scalar.copy(*weave_views(PAIR + 1, mid_woven[:, quarters[1], :]))
+        nc.scalar.copy(*weave_views(PAIR + 1, g_second[:, quarters[1], :]))
         early.append(multiply(1, halves[0]))
         for j in range(PAIR, PACK):
             second_sigmoid(j)
         scatter(0, early[0], halves[0])
-        quantise_xm(PAIR, PAIR, mid_woven)
+        quantise_xm(PAIR, PAIR, g_second)
         form_g(nc.gpsimd, g_second, second_sigmoids[:], second_factors, PACK)
         scatter(1, early[1], halves[0])
         scatter(PAIR, multiply(PAIR, halves[0]), halves[0])
@@ -297,7 +300,7 @@ def tile_attend_gsig_w_kernel(tc, xT, w_words, w_scales, y, wt, xm, offs, out):
                 nc.scalar.copy(*weave_views(first + k, late_woven[:, quarters[k], :]))
             quantise_xm(first, PAIR, late_woven)
 
-        late_xm(EARLY, rewoven(PAIR + 1))
+        late_xm(EARLY, rewoven(second_margins[:, N:]))
         held = tile([P, HALF], F32, "held", "second_sigmoids")
         multiply(EARLY - 1, halves[0], held)
         quantise_g(1, g_second)

@@ -56,21 +56,19 @@ def tile_attend_gsig_w_kernel(tc, xT, w_words, w_scales, y, wt, xm, offs, out):
         nc.sync.dma_start(offsets[:], offs)
         table_scales = tile([P, T], U8, "table_scales")
         nc.vector.memset(table_scales[:].bitcast(I32), 0)
-        scale_rows = w_scales.rearrange("o (q r) t -> r q o t", r=PACK)
-        for r in range(PACK):
-            nc.sync.dma_start(table_scales[r:P:HALF_QUADRANT, :].bitcast(I32), scale_rows[r].bitcast(I32))
+        nc.sync.dma_start(table_scales[0:P:PACK, :].bitcast(I32), w_scales.rearrange("o f t -> (o f) t").bitcast(I32))
         nc.sync.dma_start(table_words[:, T // 2 :], words[:, T // 2 :])
         x_first = tile([P, PACK, R], F32, "x_first")
         x_third = tile([P, PAIR, R], F32, "x_third")
-        x_last = tile([P, PAIR, R], F32, "x_last")
-        x_raw = [[x_first[:, places, :] for places in pairs], [x_third[:], x_last[:]]]
-        for o in range(PASSES):
-            rows = xT[0, o * K_PASS : (o + 1) * K_PASS, :].rearrange("(p t) c -> p t c", t=PACK)
-            for e in range(PAIR):
-                nc.sync.dma_start(x_raw[o][e], rows[:, pairs[e], :])
+        x_rows = [xT[0, o * K_PASS : (o + 1) * K_PASS, :].rearrange("(p t) c -> p t c", t=PACK) for o in range(PASSES)]
+        for places in pairs:
+            nc.sync.dma_start(x_first[:, places, :], x_rows[0][:, places, :])
+        nc.sync.dma_start(x_third[:], x_rows[1][:, pairs[0], :])
 
-        moved_plane = tile([P, N], U8, "moved_plane")
-        nc.vector.memset(moved_plane[:].bitcast(I32), 0)
+        planes = tile([P, (PASSES + 1) * N], U8, "planes")
+        nc.vector.memset(planes[:].bitcast(I32), 0)
+        w_planes = [planes[:, o * N : (o + 1) * N] for o in range(PASSES)]
+        g_plane = planes[:, PASSES * N :]
         warm = keep.tile([P, 2], F32, name="warm")
         nc.vector.memset(warm[:, 0:1], 0.0)
         nc.scalar.activation(warm[:, 1:2], warm[:, 0:1], SIGMOID)
@@ -88,12 +86,18 @@ def tile_attend_gsig_w_kernel(tc, xT, w_words, w_scales, y, wt, xm, offs, out):
 
         picked_scales = tile([P, N], U8, "picked_scales")
         nc.vector.tensor_copy(picked_scales[:], table_scales[:].indirect(offsets[:]))
-        for q in range(P // QUADRANT):
-            nc.sync.dma_start(
-                moved_plane[QUADRANT * q : QUADRANT * q + PACK, :].bitcast(I32),
-                picked_scales[QUADRANT * q + HALF_QUADRANT : QUADRANT * q + HALF_QUADRANT + PACK, :].bitcast(I32),
-            )
-        w_planes = [picked_scales, moved_plane]
+
+        def move_plane(o):
+            for r in range(PACK):
+                first = P // PASSES * o + PACK * r
+                rows = picked_scales[first : P // PASSES * (o + 1) : HALF_QUADRANT, :]
+                nc.sync.dma_start(w_planes[o][r:P:QUADRANT, :].bitcast(I32), rows.bitcast(I32))
+
+        move_plane(0)
+        x_last = tile([P, PAIR, R], F32, "x_last", "table_scales")
+        nc.sync.dma_start(x_last[:], x_rows[1][:, pairs[1], :])
+        move_plane(1)
+        x_raw = [[x_first[:, places, :] for places in pairs], [x_third[:], x_last[:]]]
         picked_words = tile([P, N], U32, "picked_words")
         nc.vector.tensor_copy(picked_words[:], table_words[:].bitcast(U32).indirect(offsets[:]))
         w_codes = tile([P, PASSES, N], U16, "w_codes")
@@ -101,11 +105,10 @@ def tile_attend_gsig_w_kernel(tc, xT, w_words, w_scales, y, wt, xm, offs, out):
         nc.vector.tensor_copy(w_codes[:, 0, :], word_pairs[:, 0, :])
 
         y_rows = y[0].rearrange("(p j) n -> p j n", j=PACK)
-        sign_tags = ["table_scales", "table_words"]
-        sign_pairs = [tile([P, PAIR, HALF], F32, "first_signs", tag) for tag in sign_tags]
-        for e in range(PAIR):
-            nc.sync.dma_start(sign_pairs[e][:], y_rows[:, pairs[e], halves[0]])
-        first_signs = [sign_pairs[j // PAIR][:, j % PAIR, :] for j in range(PACK)]
+        y_first = tile([P, PACK, HALF], F32, "y_first", "table_words")
+        for tiles in pairs:
+            nc.sync.dma_start(y_first[:, tiles, :], y_rows[:, tiles, halves[0]])
+        first_signs = [y_first[:, j, :] for j in range(PACK)]
 
         x_codes = [tile([P, R], U32, "x_codes%d" % o) for o in range(PASSES)]
         x_planes = [tile([P, R], U8, "x_plane%d" % o) for o in range(PASSES)]
@@ -139,7 +142,7 @@ def tile_attend_gsig_w_kernel(tc, xT, w_words, w_scales, y, wt, xm, offs, out):
         xm_first = after_first[:, : PACK * HALF].rearrange("p (t c) -> p t c", t=PACK)
         y_second = after_first[:, PACK * HALF :].rearrange("p (j n) -> p j n", j=PACK)
         xm_second = tile([P, PACK, PAIR * P], F32, "xm_second", "x_third")
-        xm_high = tile([P, PACK, D // 2], F32, "xm_high", "x_last")
+        xm_high = tile([P, PACK, D // 2], F32, "xm_high", "table_scales")
         nc.sync.dma_start(xm_first, xm_rows[:, :, : PAIR * P])
         nc.sync.dma_start(y_second, y_rows[:, :, halves[1]])
         nc.sync.dma_start(xm_second[:], xm_rows[:, :, PAIR * P : PACK * P])
@@ -187,9 +190,7 @@ def tile_attend_gsig_w_kernel(tc, xT, w_words, w_scales, y, wt, xm, offs, out):
                 these = slice(tiles.start, tiles.stop)
                 nc.scalar.activation(first_sigmoids[c][:, these, :], first_margins[c][:, these, :], SIGMOID, scale=-1.0)
 
-        g_plane = tile([P, N], U8, "g_plane", sign_tags[0])
-        g_codes = tile([P, N], U32, "g_codes", sign_tags[1])
-        nc.gpsimd.memset(g_plane[:, halves[1]].bitcast(I32), 0)
+        g_codes = tile([P, N], U32, "g_codes", "table_words")
         nc.gpsimd.memset(g_codes[:, halves[1]].bitcast(I32), 0)
 
         second_scores = []
@@ -236,7 +237,7 @@ def tile_attend_gsig_w_kernel(tc, xT, w_words, w_scales, y, wt, xm, offs, out):
                 lhsT=xm_codes[:, cols].bitcast(E4M3),
                 lhsT_scale=xm_plane[:, cols],
                 rhs=g_codes[:].bitcast(E5M2),
-                rhs_scale=g_plane[:],
+                rhs_scale=g_plane,
                 start=True,
                 stop=True,
             )

@@ -94,21 +94,23 @@ def tile_attend_gsig_w_kernel(tc, xT, w_words, w_scales, y, wt, xm, offs, out):
                 nc.sync.dma_start(w_planes[o][r:P:QUADRANT, :].bitcast(I32), rows.bitcast(I32))
 
         move_plane(0)
-        x_last = tile([P, PAIR, R], F32, "x_last", "table_scales")
-        nc.sync.dma_start(x_last[:], x_rows[1][:, pairs[1], :])
+        y_rows = y[0].rearrange("(p j) n -> p j n", j=PACK)
+        after_scales = tile([P, PAIR * (R + HALF)], F32, "after_scales", "table_scales")
+        x_last = after_scales[:, : PAIR * R].rearrange("p (t c) -> p t c", t=PAIR)
+        y_low = after_scales[:, PAIR * R :].rearrange("p (j n) -> p j n", j=PAIR)
+        nc.sync.dma_start(x_last, x_rows[1][:, pairs[1], :])
+        nc.sync.dma_start(y_low, y_rows[:, pairs[0], halves[0]])
         move_plane(1)
-        x_raw = [[x_first[:, places, :] for places in pairs], [x_third[:], x_last[:]]]
+        x_raw = [[x_first[:, places, :] for places in pairs], [x_third[:], x_last]]
         picked_words = tile([P, N], U32, "picked_words")
         nc.vector.tensor_copy(picked_words[:], table_words[:].bitcast(U32).indirect(offsets[:]))
         w_codes = tile([P, PASSES, N], U16, "w_codes")
         word_pairs = picked_words[:].bitcast(U16).rearrange("p (n o) -> p o n", o=PASSES)
         nc.vector.tensor_copy(w_codes[:, 0, :], word_pairs[:, 0, :])
 
-        y_rows = y[0].rearrange("(p j) n -> p j n", j=PACK)
-        y_first = tile([P, PACK, HALF], F32, "y_first", "table_words")
-        for tiles in pairs:
-            nc.sync.dma_start(y_first[:, tiles, :], y_rows[:, tiles, halves[0]])
-        first_signs = [y_first[:, j, :] for j in range(PACK)]
+        y_high = tile([P, PAIR, HALF], F32, "y_high", "table_words")
+        nc.sync.dma_start(y_high[:], y_rows[:, pairs[1], halves[0]])
+        first_signs = [pair[:, j, :] for pair in (y_low, y_high) for j in range(PAIR)]
 
         x_codes = [tile([P, R], U32, "x_codes%d" % o) for o in range(PASSES)]
         x_planes = [tile([P, R], U8, "x_plane%d" % o) for o in range(PASSES)]

@@ -66,12 +66,11 @@ def tile_attend_gsig_w_kernel(tc, xT, w_words, w_scales, y, wt, xm, offs, out):
         nc.sync.dma_start(x_third[:], x_rows[1][:, pairs[0], :])
 
         planes = tile([P, (PASSES + 1) * N], U8, "planes")
-        nc.vector.memset(planes[:].bitcast(I32), 0)
-        w_planes = [planes[:, o * N : (o + 1) * N] for o in range(PASSES)]
-        g_plane = planes[:, PASSES * N :]
-        warm = keep.tile([P, 2], F32, name="warm")
-        nc.vector.memset(warm[:, 0:1], 0.0)
-        nc.scalar.activation(warm[:, 1:2], warm[:, 0:1], SIGMOID)
+        nc.gpsimd.memset(planes[:, HALF:].bitcast(I32), 0)
+        g_plane = planes[:, :N]
+        w_planes = [planes[:, (o + 1) * N : (o + 2) * N] for o in range(PASSES)]
+        warm = keep.tile([P, 1], F32, name="warm")
+        nc.scalar.activation(warm[:], weights[:, 0:1], SIGMOID)
 
         def zeroed_window(engine, tag):
             window = tile([P, T], F32, "window", tag)
@@ -114,11 +113,15 @@ def tile_attend_gsig_w_kernel(tc, xT, w_words, w_scales, y, wt, xm, offs, out):
 
         x_codes = [tile([P, R], U32, "x_codes%d" % o) for o in range(PASSES)]
         x_planes = [tile([P, R], U8, "x_plane%d" % o) for o in range(PASSES)]
-        x_woven = [[tile([P, PAIR, P, PACK], BF16, "x_woven%d_%d" % (o, e)) for e in range(PAIR)] for o in range(PASSES)]
+        factor_words = tile([P, PACK * HALF], F32, "factor_words")
+        first_factors = factor_words[:].rearrange("p (j n) -> p j n", j=PACK)
+        x_woven = [[tile([P, PAIR, P, PACK], BF16, "x_woven0_%d" % e)[:] for e in range(PAIR)]]
+        last_share = factor_words[:, N:].bitcast(BF16).rearrange("p (j s t) -> p j s t", j=PAIR, t=PACK)
+        x_woven.append([tile([P, PAIR, P, PACK], BF16, "x_woven1_0")[:], last_share])
 
         def weave_x(copy, o, e, places, raw):
             copy(
-                x_woven[o][e][:].rearrange("p j s t -> p s t j")[:, :, places, :],
+                x_woven[o][e].rearrange("p j s t -> p s t j")[:, :, places, :],
                 raw.rearrange("p t (s j) -> p s t j", j=PACK)[:, :, :, pairs[e]],
             )
 
@@ -171,8 +174,6 @@ def tile_attend_gsig_w_kernel(tc, xT, w_words, w_scales, y, wt, xm, offs, out):
                 for j in range(PACK):
                     score_pass(first_scores[c][j][:], o, j, quarters[c])
 
-        first_factors = tile([P, PACK, HALF], F32, "first_factors", "x_woven1_1")
-
         def form_factors(factors, signs):
             for j in range(PACK):
                 if j < PAIR:
@@ -180,7 +181,7 @@ def tile_attend_gsig_w_kernel(tc, xT, w_words, w_scales, y, wt, xm, offs, out):
                 else:
                     nc.gpsimd.tensor_scalar(factors[:, j, :], signs[j], negated[:, j : j + 1], 0.0, MULT, ADD)
 
-        form_factors(first_factors[:], first_signs)
+        form_factors(first_factors, first_signs)
         shared = tile([P, (PACK + 1) * HALF], F32, "shared")
         own = tile([P, PACK * HALF], F32, "own")
         first_sigmoids = [t[:, :N].rearrange("p (j n) -> p j n", j=PACK) for t in (own, shared)]

@@ -182,10 +182,11 @@ def tile_attend_gsig_w_kernel(tc, xT, w_words, w_scales, y, wt, xm, offs, out):
                     nc.gpsimd.tensor_scalar(factors[:, j, :], signs[j], negated[:, j : j + 1], 0.0, MULT, ADD)
 
         form_factors(first_factors, first_signs)
-        shared = tile([P, (PACK + 1) * HALF], F32, "shared")
+        shared = tile([P, PACK * N], F32, "shared")
         own = tile([P, PACK * HALF], F32, "own")
         first_sigmoids = [t[:, :N].rearrange("p (j n) -> p j n", j=PACK) for t in (own, shared)]
-        first_margins = [t[:, N : PAIR * N].rearrange("p (j n) -> p j n", j=PACK) for t in (own, shared)]
+        shift = P // 2
+        first_margins = [t[:, N + k : PAIR * N + k].rearrange("p (j n) -> p j n", j=PACK) for t, k in ((own, 0), (shared, shift))]
         for c in range(PAIR):
             for tiles in (range(0, PAIR), range(PAIR, PAIR + 1), range(PAIR + 1, PACK)):
                 for j in tiles:
@@ -198,7 +199,7 @@ def tile_attend_gsig_w_kernel(tc, xT, w_words, w_scales, y, wt, xm, offs, out):
 
         second_scores = []
         for j in range(PACK):
-            bank = psum.tile([P, HALF], F32, name="scores", tag="bank%d" % j)
+            bank = psum.tile([P, HALF], F32, name="scores", tag="bank%d" % (j + PACK * (j // PAIR)))
             second_scores.append(bank)
             for c in range(PAIR):
                 for o in range(PASSES):
@@ -212,8 +213,7 @@ def tile_attend_gsig_w_kernel(tc, xT, w_words, w_scales, y, wt, xm, offs, out):
                 MULT,
             )
 
-        def quantise_g(h, woven):
-            cols = halves[h]
+        def quantise_g(cols, woven):
             nc.vector.quantize_mx(g_codes[:, cols].bitcast(E5M2), g_plane[:, cols], woven.rearrange("p n j -> p (n j)"))
 
         xm_codes = tile([P, D], U32, "xm_codes")
@@ -232,7 +232,7 @@ def tile_attend_gsig_w_kernel(tc, xT, w_words, w_scales, y, wt, xm, offs, out):
         passes_done = []
 
         def multiply(m, slots, columns=None):
-            bank = psum.tile([P, N], F32, name="grad", tag="bank%d" % (PACK + len(passes_done) % PACK))
+            bank = psum.tile([P, N], F32, name="grad", tag="bank%d" % (PAIR + len(passes_done) % PACK))
             passes_done.append(m)
             cols = slice(m * P, (m + 1) * P)
             nc.tensor.matmul_mx(
@@ -253,34 +253,38 @@ def tile_attend_gsig_w_kernel(tc, xT, w_words, w_scales, y, wt, xm, offs, out):
             listed = offsets[:, slots.start // PER_COLUMN : slots.stop // PER_COLUMN]
             nc.vector.tensor_copy(windows[m % WINDOWS][:].indirect(listed), columns[:, slots])
 
-        split = PAIR * N - P // 2
         low_woven = [
-            shared[:, first : first + HALF].bitcast(BF16).rearrange("p (c t) -> p c t", t=PACK) for first in (split, split - HALF)
+            shared[:, first : first + HALF].bitcast(BF16).rearrange("p (c t) -> p c t", t=PACK)
+            for first in (PAIR * N, PAIR * N - HALF - shift // 2)
         ]
         for m in range(PAIR):
             nc.scalar.copy(*weave_views(m, low_woven[m]))
         g_first = tile([P, HALF, PACK], BF16, "g_first")
         for c in range(PAIR):
             form_g(nc.vector, g_first[:, quarters[c], :], first_sigmoids[c], first_factors[:, :, quarters[c]], PAIR)
+        for cols in quarters[:PAIR]:
+            quantise_g(cols, g_first[:, cols, :])
         quantise_xm(0, 1, low_woven[0])
-        quantise_g(0, g_first[:])
         early = [multiply(0, halves[0])]
         quantise_xm(1, 1, low_woven[1])
 
         second_factors = shared[:, : PACK * HALF].rearrange("p (j n) -> p j n", j=PACK)
         form_factors(second_factors, second_signs)
         second_sigmoids = tile([P, PACK, HALF], F32, "second_sigmoids")
-        second_margins = tile([P, PACK * HALF], F32, "second_margins", "g_first")
-        margin_of = [second_margins[:, j * HALF : (j + 1) * HALF] for j in range(PACK)]
+        second_margins = shared[:, PAIR * N :]
+        margin_of = [second_margins.rearrange("p (u j n) -> p j u n", u=PACK, j=PACK)[:, j] for j in range(PACK)]
+
+        def in_runs(columns):
+            return columns.rearrange("p (u n) -> p u n", u=PACK)
 
         def rewoven(words):
             return words.bitcast(BF16).rearrange("p (n j) -> p n j", j=PACK)
 
         def second_margin(j):
-            nc.vector.tensor_tensor(margin_of[j], second_scores[j][:], second_signs[j], MULT)
+            nc.vector.tensor_tensor(margin_of[j], in_runs(second_scores[j][:]), in_runs(second_signs[j]), MULT)
 
         def second_sigmoid(j):
-            nc.scalar.activation(second_sigmoids[:, j, :], margin_of[j], SIGMOID, scale=-1.0)
+            nc.scalar.activation(in_runs(second_sigmoids[:, j, :]), margin_of[j], SIGMOID, scale=-1.0)
 
         for j in range(PACK):
             second_margin(j)
@@ -307,10 +311,9 @@ def tile_attend_gsig_w_kernel(tc, xT, w_words, w_scales, y, wt, xm, offs, out):
         late_xm(EARLY, rewoven(second_margins[:, N:]))
         held = tile([P, HALF], F32, "held", "second_sigmoids")
         multiply(EARLY - 1, halves[0], held)
-        quantise_g(1, g_second)
+        quantise_g(halves[1], g_second)
         scatter(EARLY - 1, held, halves[0])
-        last_woven = tile([P, PAIR * P, PACK], BF16, "last_woven", "shared")
-        late_xm(EARLY + PAIR, last_woven[:])
+        late_xm(EARLY + PAIR, rewoven(shared[:, :N]))
         for m in range(D_TILES):
             slots = halves[1] if m < EARLY else slice(0, N)
             scatter(m, multiply(m, slots), slots)

@@ -30,22 +30,24 @@ D_TILES = D // P
 PER_COLUMN = 16
 HALF = N // 2
 WINDOWS = 4
-EARLY = 4
-STAGED = 6
+LINE = 16
 
 
 def tile_attend_gsig_w_kernel(tc, xT, w_words, w_scales, y, wt, xm, offs, out):
     nc = tc.nc
     with ExitStack() as ctx:
         keep = ctx.enter_context(tc.tile_pool(name="keep", bufs=1))
-        ring = ctx.enter_context(tc.tile_pool(name="ring", bufs=STAGED))
         psum = ctx.enter_context(tc.psum_pool(name="psum", bufs=1))
         halves = [slice(0, HALF), slice(HALF, N)]
         quarters = [slice(c * P, (c + 1) * P) for c in range(N // P)]
         pairs = [slice(0, PAIR), slice(PAIR, PACK)]
+        whole = slice(0, N)
 
         def tile(shape, dtype, name, tag=None):
             return keep.tile(shape, dtype, name=name, tag=tag or name, align_bytes=64)
+
+        def woven_view(words):
+            return words.bitcast(BF16).rearrange("p (n j) -> p n j", j=PACK)
 
         offsets = keep.tile([P, N // PER_COLUMN], U16, name="offsets")
         weights = tile([P, PACK], F32, "weights")
@@ -65,10 +67,9 @@ def tile_attend_gsig_w_kernel(tc, xT, w_words, w_scales, y, wt, xm, offs, out):
             nc.sync.dma_start(x_first[:, places, :], x_rows[0][:, places, :])
         nc.sync.dma_start(x_third[:], x_rows[1][:, pairs[0], :])
 
-        planes = tile([P, (PASSES + 1) * N], U8, "planes")
-        nc.gpsimd.memset(planes[:, HALF:].bitcast(I32), 0)
-        g_plane = planes[:, :N]
-        w_planes = [planes[:, (o + 1) * N : (o + 2) * N] for o in range(PASSES)]
+        planes = tile([P, PASSES * N], U8, "planes")
+        nc.gpsimd.memset(planes[:].bitcast(I32), 0)
+        w_planes = [planes[:, o * N : (o + 1) * N] for o in range(PASSES)]
         warm = keep.tile([P, 1], F32, name="warm")
         nc.scalar.activation(warm[:], weights[:, 0:1], SIGMOID)
 
@@ -94,11 +95,10 @@ def tile_attend_gsig_w_kernel(tc, xT, w_words, w_scales, y, wt, xm, offs, out):
 
         move_plane(0)
         y_rows = y[0].rearrange("(p j) n -> p j n", j=PACK)
-        after_scales = tile([P, PAIR * (R + HALF)], F32, "after_scales", "table_scales")
+        after_scales = tile([P, PAIR * R + N], F32, "after_scales", "table_scales")
         x_last = after_scales[:, : PAIR * R].rearrange("p (t c) -> p t c", t=PAIR)
-        y_low = after_scales[:, PAIR * R :].rearrange("p (j n) -> p j n", j=PAIR)
         nc.sync.dma_start(x_last, x_rows[1][:, pairs[1], :])
-        nc.sync.dma_start(y_low, y_rows[:, pairs[0], halves[0]])
+        nc.sync.dma_start(after_scales[:, PAIR * R :], y_rows[:, 0, :])
         move_plane(1)
         x_raw = [[x_first[:, places, :] for places in pairs], [x_third[:], x_last]]
         picked_words = tile([P, N], U32, "picked_words")
@@ -107,16 +107,17 @@ def tile_attend_gsig_w_kernel(tc, xT, w_words, w_scales, y, wt, xm, offs, out):
         word_pairs = picked_words[:].bitcast(U16).rearrange("p (n o) -> p o n", o=PASSES)
         nc.vector.tensor_copy(w_codes[:, 0, :], word_pairs[:, 0, :])
 
-        y_high = tile([P, PAIR, HALF], F32, "y_high", "table_words")
-        nc.sync.dma_start(y_high[:], y_rows[:, pairs[1], halves[0]])
-        first_signs = [pair[:, j, :] for pair in (y_low, y_high) for j in range(PAIR)]
+        y_rest = tile([P, PACK - 1, N], F32, "y_rest", "table_words")
+        nc.sync.dma_start(y_rest[:, 0, :], y_rows[:, 1, :])
+        nc.sync.dma_start(y_rest[:, 1:, :], y_rows[:, pairs[1], :])
+        signs = [after_scales[:, PAIR * R :]] + [y_rest[:, j, :] for j in range(PACK - 1)]
 
         x_codes = [tile([P, R], U32, "x_codes%d" % o) for o in range(PASSES)]
         x_planes = [tile([P, R], U8, "x_plane%d" % o) for o in range(PASSES)]
-        factor_words = tile([P, PACK * HALF], F32, "factor_words")
-        first_factors = factor_words[:].rearrange("p (j n) -> p j n", j=PACK)
+        factor_words = tile([P, PACK * N], F32, "factor_words")
+        factors = factor_words[:].rearrange("p (j n) -> p j n", j=PACK)
         x_woven = [[tile([P, PAIR, P, PACK], BF16, "x_woven0_%d" % e)[:] for e in range(PAIR)]]
-        last_share = factor_words[:, N:].bitcast(BF16).rearrange("p (j s t) -> p j s t", j=PAIR, t=PACK)
+        last_share = factor_words[:, N : PAIR * N].bitcast(BF16).rearrange("p (j s t) -> p j s t", j=PAIR, t=PACK)
         x_woven.append([tile([P, PAIR, P, PACK], BF16, "x_woven1_0")[:], last_share])
 
         def weave_x(copy, o, e, places, raw):
@@ -143,81 +144,62 @@ def tile_attend_gsig_w_kernel(tc, xT, w_words, w_scales, y, wt, xm, offs, out):
             quantise_x(1, j, 1)
 
         xm_rows = xm[0].rearrange("(p t) c -> p t c", t=PACK)
-        after_first = tile([P, PAIR * PACK * HALF], F32, "after_first", "x_first")
-        xm_first = after_first[:, : PACK * HALF].rearrange("p (t c) -> p t c", t=PACK)
-        y_second = after_first[:, PACK * HALF :].rearrange("p (j n) -> p j n", j=PACK)
+        xm_first = tile([P, PACK, PAIR * P], F32, "xm_first", "x_first")
         xm_second = tile([P, PACK, PAIR * P], F32, "xm_second", "x_third")
         xm_high = tile([P, PACK, D // 2], F32, "xm_high", "table_scales")
-        nc.sync.dma_start(xm_first, xm_rows[:, :, : PAIR * P])
-        nc.sync.dma_start(y_second, y_rows[:, :, halves[1]])
+        nc.sync.dma_start(xm_first[:], xm_rows[:, :, : PAIR * P])
         nc.sync.dma_start(xm_second[:], xm_rows[:, :, PAIR * P : PACK * P])
         nc.sync.dma_start(xm_high[:], xm_rows[:, :, D // 2 :])
-        second_signs = [y_second[:, j, :] for j in range(PACK)]
         xm_raw = [xm_first[:, :, cols] for cols in quarters[:PAIR]]
         xm_raw.extend(xm_second[:, :, cols] for cols in quarters[:PAIR])
         xm_raw.extend(xm_high[:, :, cols] for cols in quarters)
 
-        def score_pass(bank, o, j, slots):
-            nc.tensor.matmul_mx(
-                bank,
-                lhsT=x_codes[o][:, quarters[j]].bitcast(E4M3),
-                lhsT_scale=x_planes[o][:, quarters[j]],
-                rhs=w_codes[:, o, slots].bitcast(E2M1),
-                rhs_scale=w_planes[o][:, slots],
-                start=(o == 0),
-                stop=(o == PASSES - 1),
-            )
-
-        first_scores = [[psum.tile([P, P], F32, name="scores", tag="bank%d" % (PACK * c + j)) for j in range(PACK)] for c in range(PAIR)]
+        pieces = [(0, 0), (0, 1), (1, 0), (1, 1), (2, 0), (3, 0), (2, 1), (3, 1)]
+        scores = {piece: psum.tile([P, HALF], F32, name="scores", tag="bank%d" % b) for b, piece in enumerate(pieces)}
         for o in range(PASSES):
-            for c in range(PAIR):
-                for j in range(PACK):
-                    score_pass(first_scores[c][j][:], o, j, quarters[c])
+            for j, h in pieces:
+                nc.tensor.matmul_mx(
+                    scores[j, h][:],
+                    lhsT=x_codes[o][:, quarters[j]].bitcast(E4M3),
+                    lhsT_scale=x_planes[o][:, quarters[j]],
+                    rhs=w_codes[:, o, halves[h]].bitcast(E2M1),
+                    rhs_scale=w_planes[o][:, halves[h]],
+                    start=(o == 0),
+                    stop=(o == PASSES - 1),
+                )
 
-        def form_factors(factors, signs):
-            for j in range(PACK):
-                if j < PAIR:
-                    nc.scalar.activation(factors[:, j, :], signs[j], COPY, scale=negated[:, j : j + 1])
-                else:
-                    nc.gpsimd.tensor_scalar(factors[:, j, :], signs[j], negated[:, j : j + 1], 0.0, MULT, ADD)
+        def scalar_factors(j, slots):
+            nc.scalar.activation(factors[:, j, slots], signs[j][:, slots], COPY, scale=negated[:, j : j + 1])
 
-        form_factors(first_factors, first_signs)
-        shared = tile([P, PACK * N], F32, "shared")
-        own = tile([P, PACK * HALF], F32, "own")
-        first_sigmoids = [t[:, :N].rearrange("p (j n) -> p j n", j=PACK) for t in (own, shared)]
-        shift = P // 2
-        first_margins = [t[:, N + k : PAIR * N + k].rearrange("p (j n) -> p j n", j=PACK) for t, k in ((own, 0), (shared, shift))]
-        for c in range(PAIR):
-            for tiles in (range(0, PAIR), range(PAIR, PAIR + 1), range(PAIR + 1, PACK)):
-                for j in tiles:
-                    nc.vector.tensor_tensor(first_margins[c][:, j, :], first_scores[c][j][:], first_signs[j][:, quarters[c]], MULT)
-                these = slice(tiles.start, tiles.stop)
-                nc.scalar.activation(first_sigmoids[c][:, these, :], first_margins[c][:, these, :], SIGMOID, scale=-1.0)
+        def gpsimd_factors(j, slots):
+            nc.gpsimd.tensor_scalar(factors[:, j, slots], signs[j][:, slots], negated[:, j : j + 1], 0.0, MULT, ADD)
 
-        g_codes = tile([P, N], U32, "g_codes", "table_words")
-        nc.gpsimd.memset(g_codes[:, halves[1]].bitcast(I32), 0)
+        scalar_factors(0, whole)
+        gpsimd_factors(1, whole)
+        for j, h in pieces[PACK:]:
+            gpsimd_factors(j, halves[h])
+        margin_words = tile([P, PACK * N], F32, "margin_words")
+        margins = {piece: margin_words[:, b * HALF : (b + 1) * HALF] for b, piece in enumerate(pieces)}
+        sigmoids = tile([P, PACK, N], F32, "sigmoids")
+        for j, h in pieces:
+            nc.vector.tensor_tensor(margins[j, h], scores[j, h][:], signs[j][:, halves[h]], MULT)
+            nc.scalar.activation(sigmoids[:, j, halves[h]], margins[j, h], SIGMOID, scale=-1.0)
 
-        second_scores = []
-        for j in range(PACK):
-            bank = psum.tile([P, HALF], F32, name="scores", tag="bank%d" % (j + PACK * (j // PAIR)))
-            second_scores.append(bank)
-            for c in range(PAIR):
-                for o in range(PASSES):
-                    score_pass(bank[:, quarters[c]], o, j, quarters[PAIR + c])
+        g_codes = tile([P, N], U32, "g_codes")
+        g_plane = tile([P, N], U8, "g_plane")
+        xm_codes = tile([P, D], U32, "xm_codes")
+        xm_plane = tile([P, D], U8, "xm_plane")
 
-        def form_g(engine, woven, sigmoids, factors, run):
-            engine.tensor_tensor(
-                woven.rearrange("p (c i) j -> p c j i", i=run),
-                sigmoids.rearrange("p j (c i) -> p c j i", i=run),
-                factors.rearrange("p j (c i) -> p c j i", i=run),
+        def form_g(woven, slots):
+            nc.vector.tensor_tensor(
+                woven.rearrange("p (c i) j -> p c j i", i=PAIR),
+                sigmoids[:, :, slots].rearrange("p j (c i) -> p c j i", i=PAIR),
+                factors[:, :, slots].rearrange("p j (c i) -> p c j i", i=PAIR),
                 MULT,
             )
 
-        def quantise_g(cols, woven):
-            nc.vector.quantize_mx(g_codes[:, cols].bitcast(E5M2), g_plane[:, cols], woven.rearrange("p n j -> p (n j)"))
-
-        xm_codes = tile([P, D], U32, "xm_codes")
-        xm_plane = tile([P, D], U8, "xm_plane")
+        def quantise_g(slots, woven):
+            nc.vector.quantize_mx(g_codes[:, slots].bitcast(E5M2), g_plane[:, slots], woven.rearrange("p n j -> p (n j)"))
 
         def weave_views(m, woven):
             return (
@@ -225,100 +207,101 @@ def tile_attend_gsig_w_kernel(tc, xT, w_words, w_scales, y, wt, xm, offs, out):
                 xm_raw[m].rearrange("p t (c i) -> p c t i", i=PACK),
             )
 
+        def gpsimd_weave(first, count, woven):
+            for k in range(count):
+                target, raw = weave_views(first + k, woven[:, quarters[k], :])
+                nc.gpsimd.tensor_scalar(target, raw, 1.0, 0.0, MULT, ADD)
+
         def quantise_xm(first, count, woven):
             cols = slice(first * P, (first + count) * P)
             nc.vector.quantize_mx(xm_codes[:, cols].bitcast(E4M3), xm_plane[:, cols], woven.rearrange("p c t -> p (c t)"))
 
         passes_done = []
 
-        def multiply(m, slots, columns=None):
-            bank = psum.tile([P, N], F32, name="grad", tag="bank%d" % (PAIR + len(passes_done) % PACK))
+        def multiply(m, slots):
+            bank = psum.tile([P, slots.stop - slots.start], F32, name="grad", tag="bank%d" % (len(passes_done) % len(pieces)))
             passes_done.append(m)
             cols = slice(m * P, (m + 1) * P)
             nc.tensor.matmul_mx(
                 bank[:],
                 lhsT=xm_codes[:, cols].bitcast(E4M3),
                 lhsT_scale=xm_plane[:, cols],
-                rhs=g_codes[:].bitcast(E5M2),
-                rhs_scale=g_plane,
+                rhs=g_codes[:, slots].bitcast(E5M2),
+                rhs_scale=g_plane[:, slots],
                 start=True,
                 stop=True,
             )
-            if columns is None:
-                columns = ring.tile([P, N], F32, name="columns")
-            nc.scalar.copy(columns[:, slots], bank[:, slots])
-            return columns
+            return bank
 
-        def scatter(m, columns, slots):
-            listed = offsets[:, slots.start // PER_COLUMN : slots.stop // PER_COLUMN]
-            nc.vector.tensor_copy(windows[m % WINDOWS][:].indirect(listed), columns[:, slots])
+        def listed(m, slots):
+            return windows[m % WINDOWS][:].indirect(offsets[:, slots.start // PER_COLUMN : slots.stop // PER_COLUMN])
 
-        low_woven = [
-            shared[:, first : first + HALF].bitcast(BF16).rearrange("p (c t) -> p c t", t=PACK)
-            for first in (PAIR * N, PAIR * N - HALF - shift // 2)
-        ]
+        def store(m):
+            nc.sync.dma_start(out[m * P : (m + 1) * P, :], windows[m % WINDOWS][:])
+
+        scalar_columns = [tile([P, N], F32, "scalar_columns%d" % k) for k in range(PAIR)]
+
+        def scalar_half(m, h, columns):
+            nc.scalar.activation(listed(m, halves[h]), columns[:, halves[h]], COPY)
+
+        low_woven = [woven_view(margins[PACK - 1, h]) for h in range(PAIR)]
         for m in range(PAIR):
             nc.scalar.copy(*weave_views(m, low_woven[m]))
         g_first = tile([P, HALF, PACK], BF16, "g_first")
-        for c in range(PAIR):
-            form_g(nc.vector, g_first[:, quarters[c], :], first_sigmoids[c], first_factors[:, :, quarters[c]], PAIR)
+        relay = tile([P, 3 * N], F32, "relay")
+        g_second = woven_view(relay[:, :N])
         for cols in quarters[:PAIR]:
-            quantise_g(cols, g_first[:, cols, :])
+            form_g(g_first[:, cols, :], cols)
         quantise_xm(0, 1, low_woven[0])
-        early = [multiply(0, halves[0])]
+        quantise_g(halves[0], g_first[:])
+        nc.scalar.copy(scalar_columns[0][:, halves[0]], multiply(0, halves[0])[:])
+        scalar_half(0, 0, scalar_columns[0])
+        for c in range(PAIR):
+            form_g(g_second[:, quarters[c], :], quarters[PAIR + c])
+        quantise_g(quarters[PAIR], g_second[:, quarters[0], :])
         quantise_xm(1, 1, low_woven[1])
+        quantise_g(quarters[PAIR + 1], g_second[:, quarters[1], :])
+        nc.scalar.copy(scalar_columns[0][:, halves[1]], multiply(0, halves[1])[:])
+        scalar_half(0, 1, scalar_columns[0])
+        store(0)
 
-        second_factors = shared[:, : PACK * HALF].rearrange("p (j n) -> p j n", j=PACK)
-        form_factors(second_factors, second_signs)
-        second_sigmoids = tile([P, PACK, HALF], F32, "second_sigmoids")
-        second_margins = shared[:, PAIR * N :]
-        margin_of = [second_margins.rearrange("p (u j n) -> p j u n", u=PACK, j=PACK)[:, j] for j in range(PACK)]
+        def relay_words(first, count):
+            return relay[:, first : first + count]
 
-        def in_runs(columns):
-            return columns.rearrange("p (u n) -> p u n", u=PACK)
+        def vector_tile(m, slots, columns):
+            nc.vector.tensor_copy(columns, multiply(m, slots)[:])
+            nc.vector.tensor_copy(listed(m, slots), columns)
 
-        def rewoven(words):
-            return words.bitcast(BF16).rearrange("p (n j) -> p n j", j=PACK)
+        def scalar_tile(m):
+            columns = scalar_columns[m // PAIR % PAIR]
+            nc.scalar.copy(columns[:], multiply(m, whole)[:])
+            for h in range(PAIR):
+                scalar_half(m, h, columns)
+            store(m)
 
-        def second_margin(j):
-            nc.vector.tensor_tensor(margin_of[j], in_runs(second_scores[j][:]), in_runs(second_signs[j]), MULT)
-
-        def second_sigmoid(j):
-            nc.scalar.activation(in_runs(second_sigmoids[:, j, :]), margin_of[j], SIGMOID, scale=-1.0)
-
-        for j in range(PACK):
-            second_margin(j)
-        for j in range(PAIR):
-            second_sigmoid(j)
-        g_second = rewoven(after_first[:, PACK * HALF : PACK * HALF + N])
-        woven, raw = weave_views(PAIR, g_second[:, quarters[0], :])
-        nc.gpsimd.tensor_scalar(woven, raw, 1.0, 0.0, MULT, ADD)
-        nc.scalar.copy(*weave_views(PAIR + 1, g_second[:, quarters[1], :]))
-        early.append(multiply(1, halves[0]))
-        for j in range(PAIR, PACK):
-            second_sigmoid(j)
-        scatter(0, early[0], halves[0])
-        quantise_xm(PAIR, PAIR, g_second)
-        form_g(nc.gpsimd, g_second, second_sigmoids[:], second_factors, PACK)
-        scatter(1, early[1], halves[0])
-        scatter(PAIR, multiply(PAIR, halves[0]), halves[0])
-
-        def late_xm(first, late_woven):
-            for k in range(PAIR):
-                nc.scalar.copy(*weave_views(first + k, late_woven[:, quarters[k], :]))
-            quantise_xm(first, PAIR, late_woven)
-
-        late_xm(EARLY, rewoven(second_margins[:, N:]))
-        held = tile([P, HALF], F32, "held", "second_sigmoids")
-        multiply(EARLY - 1, halves[0], held)
-        quantise_g(halves[1], g_second)
-        scatter(EARLY - 1, held, halves[0])
-        late_xm(EARLY + PAIR, rewoven(shared[:, :N]))
-        for m in range(D_TILES):
-            slots = halves[1] if m < EARLY else slice(0, N)
-            scatter(m, multiply(m, slots), slots)
-            if m < D_TILES - 1:
-                nc.sync.dma_start(out[m * P : (m + 1) * P, :], windows[m % WINDOWS][:])
-            else:
-                for queue, cols in ((nc.sync, slice(0, T // 2)), (nc.scalar, slice(T // 2, T))):
-                    queue.dma_start(out[m * P : (m + 1) * P, cols], windows[m % WINDOWS][:, cols])
+        woven_two = woven_view(relay_words(LINE, HALF))
+        nc.vector.tensor_copy(*weave_views(2, woven_two))
+        early = tile([P, HALF], F32, "early")
+        nc.vector.tensor_copy(early[:], multiply(1, halves[0])[:])
+        quantise_xm(2, 1, woven_two)
+        nc.vector.tensor_copy(listed(1, halves[0]), early[:])
+        woven_three = woven_view(relay_words(HALF, HALF))
+        gpsimd_weave(3, 1, woven_three)
+        quantise_xm(3, 1, woven_three)
+        vector_tile(1, halves[1], relay_words(LINE, HALF))
+        store(1)
+        scalar_tile(2)
+        woven_four = woven_view(relay_words(N - LINE, N))
+        gpsimd_weave(4, PAIR, woven_four)
+        quantise_xm(4, PAIR, woven_four)
+        vector_tile(3, whole, relay_words(0, N))
+        store(3)
+        scalar_tile(4)
+        woven_six = woven_view(relay_words(PAIR * (N - LINE), N))
+        gpsimd_weave(6, PAIR, woven_six)
+        quantise_xm(6, PAIR, woven_six)
+        vector_tile(5, whole, relay_words(N - LINE, N))
+        store(5)
+        scalar_tile(6)
+        vector_tile(7, whole, relay_words(0, N))
+        store(7)

@@ -29,8 +29,7 @@ PASSES = D // K_PASS
 D_TILES = D // P
 PER_COLUMN = 16
 HALF = N // 2
-WINDOWS = 4
-LINE = 16
+SCALAR_FACTORS = 3
 
 
 def tile_attend_gsig_w_kernel(tc, xT, w_words, w_scales, y, wt, xm, offs, out):
@@ -81,7 +80,6 @@ def tile_attend_gsig_w_kernel(tc, xT, w_words, w_scales, y, wt, xm, offs, out):
         windows = [zeroed_window(nc.vector, "window%d" % m) for m in range(PAIR)]
         negated = keep.tile([P, PACK], F32, name="negated")
         nc.vector.tensor_scalar(negated[:], weights[:], -1.0, 0.0, MULT, ADD)
-        windows.append(zeroed_window(nc.vector, "window2"))
         windows.append(zeroed_window(nc.gpsimd, "weights"))
 
         picked_scales = tile([P, N], U8, "picked_scales")
@@ -114,10 +112,10 @@ def tile_attend_gsig_w_kernel(tc, xT, w_words, w_scales, y, wt, xm, offs, out):
 
         x_codes = [tile([P, R], U32, "x_codes%d" % o) for o in range(PASSES)]
         x_planes = [tile([P, R], U8, "x_plane%d" % o) for o in range(PASSES)]
-        factor_words = tile([P, PACK * N], F32, "factor_words")
-        factors = factor_words[:].rearrange("p (j n) -> p j n", j=PACK)
+        factor_words = [tile([P, PACK * HALF], F32, "factor_words%d" % h) for h in range(PAIR)]
+        factors = [t[:].rearrange("p (j n) -> p j n", j=PACK) for t in factor_words]
         x_woven = [[tile([P, PAIR, P, PACK], BF16, "x_woven0_%d" % e)[:] for e in range(PAIR)]]
-        last_share = factor_words[:, N : PAIR * N].bitcast(BF16).rearrange("p (j s t) -> p j s t", j=PAIR, t=PACK)
+        last_share = factor_words[1][:, HALF : HALF + N].bitcast(BF16).rearrange("p (j s t) -> p j s t", j=PAIR, t=PACK)
         x_woven.append([tile([P, PAIR, P, PACK], BF16, "x_woven1_0")[:], last_share])
 
         def weave_x(copy, o, e, places, raw):
@@ -146,13 +144,12 @@ def tile_attend_gsig_w_kernel(tc, xT, w_words, w_scales, y, wt, xm, offs, out):
         xm_rows = xm[0].rearrange("(p t) c -> p t c", t=PACK)
         xm_first = tile([P, PACK, PAIR * P], F32, "xm_first", "x_first")
         xm_second = tile([P, PACK, PAIR * P], F32, "xm_second", "x_third")
-        xm_high = tile([P, PACK, D // 2], F32, "xm_high", "table_scales")
-        nc.sync.dma_start(xm_first[:], xm_rows[:, :, : PAIR * P])
-        nc.sync.dma_start(xm_second[:], xm_rows[:, :, PAIR * P : PACK * P])
-        nc.sync.dma_start(xm_high[:], xm_rows[:, :, D // 2 :])
-        xm_raw = [xm_first[:, :, cols] for cols in quarters[:PAIR]]
-        xm_raw.extend(xm_second[:, :, cols] for cols in quarters[:PAIR])
-        xm_raw.extend(xm_high[:, :, cols] for cols in quarters)
+        xm_third = tile([P, PACK, PAIR * P], F32, "xm_third", "table_scales")
+        xm_fourth = tile([P, PACK, PAIR * P], F32, "xm_fourth", "table_words")
+        xm_raw = []
+        for k, pair in enumerate((xm_first, xm_second, xm_third, xm_fourth)):
+            nc.sync.dma_start(pair[:], xm_rows[:, :, k * PAIR * P : (k + 1) * PAIR * P])
+            xm_raw.extend(pair[:, :, cols] for cols in quarters[:PAIR])
 
         pieces = [(0, 0), (0, 1), (1, 0), (1, 1), (2, 0), (3, 0), (2, 1), (3, 1)]
         scores = {piece: psum.tile([P, HALF], F32, name="scores", tag="bank%d" % b) for b, piece in enumerate(pieces)}
@@ -168,33 +165,28 @@ def tile_attend_gsig_w_kernel(tc, xT, w_words, w_scales, y, wt, xm, offs, out):
                     stop=(o == PASSES - 1),
                 )
 
-        def scalar_factors(j, slots):
-            nc.scalar.activation(factors[:, j, slots], signs[j][:, slots], COPY, scale=negated[:, j : j + 1])
-
-        def gpsimd_factors(j, slots):
-            nc.gpsimd.tensor_scalar(factors[:, j, slots], signs[j][:, slots], negated[:, j : j + 1], 0.0, MULT, ADD)
-
-        scalar_factors(0, whole)
-        gpsimd_factors(1, whole)
-        for j, h in pieces[PACK:]:
-            gpsimd_factors(j, halves[h])
+        for b, (j, h) in enumerate(pieces):
+            if b < SCALAR_FACTORS:
+                nc.scalar.activation(factors[h][:, j, :], signs[j][:, halves[h]], COPY, scale=negated[:, j : j + 1])
+            else:
+                nc.gpsimd.tensor_scalar(factors[h][:, j, :], signs[j][:, halves[h]], negated[:, j : j + 1], 0.0, MULT, ADD)
         margin_words = tile([P, PACK * N], F32, "margin_words")
         margins = {piece: margin_words[:, b * HALF : (b + 1) * HALF] for b, piece in enumerate(pieces)}
-        sigmoids = tile([P, PACK, N], F32, "sigmoids")
+        sigmoids = [tile([P, PACK, HALF], F32, "sigmoids%d" % h) for h in range(PAIR)]
         for j, h in pieces:
             nc.vector.tensor_tensor(margins[j, h], scores[j, h][:], signs[j][:, halves[h]], MULT)
-            nc.scalar.activation(sigmoids[:, j, halves[h]], margins[j, h], SIGMOID, scale=-1.0)
+            nc.scalar.activation(sigmoids[h][:, j, :], margins[j, h], SIGMOID, scale=-1.0)
 
         g_codes = tile([P, N], U32, "g_codes")
         g_plane = tile([P, N], U8, "g_plane")
         xm_codes = tile([P, D], U32, "xm_codes")
         xm_plane = tile([P, D], U8, "xm_plane")
 
-        def form_g(woven, slots):
+        def form_g(woven, h, slots):
             nc.vector.tensor_tensor(
                 woven.rearrange("p (c i) j -> p c j i", i=PAIR),
-                sigmoids[:, :, slots].rearrange("p j (c i) -> p c j i", i=PAIR),
-                factors[:, :, slots].rearrange("p j (c i) -> p c j i", i=PAIR),
+                sigmoids[h][:, :, slots].rearrange("p j (c i) -> p c j i", i=PAIR),
+                factors[h][:, :, slots].rearrange("p j (c i) -> p c j i", i=PAIR),
                 MULT,
             )
 
@@ -233,11 +225,13 @@ def tile_attend_gsig_w_kernel(tc, xT, w_words, w_scales, y, wt, xm, offs, out):
             )
             return bank
 
-        def listed(m, slots):
-            return windows[m % WINDOWS][:].indirect(offsets[:, slots.start // PER_COLUMN : slots.stop // PER_COLUMN])
+        window_of = [0, 1, 2, 3, 0, 4, 1, 2]
 
-        def store(m):
-            nc.sync.dma_start(out[m * P : (m + 1) * P, :], windows[m % WINDOWS][:])
+        def listed(m, slots):
+            return windows[window_of[m]][:].indirect(offsets[:, slots.start // PER_COLUMN : slots.stop // PER_COLUMN])
+
+        def store(queue, m):
+            queue.dma_start(out[m * P : (m + 1) * P, :], windows[window_of[m]][:])
 
         scalar_columns = [tile([P, N], F32, "scalar_columns%d" % k) for k in range(PAIR)]
 
@@ -247,61 +241,45 @@ def tile_attend_gsig_w_kernel(tc, xT, w_words, w_scales, y, wt, xm, offs, out):
         low_woven = [woven_view(margins[PACK - 1, h]) for h in range(PAIR)]
         for m in range(PAIR):
             nc.scalar.copy(*weave_views(m, low_woven[m]))
-        g_first = tile([P, HALF, PACK], BF16, "g_first")
-        relay = tile([P, 3 * N], F32, "relay")
-        g_second = woven_view(relay[:, :N])
-        for cols in quarters[:PAIR]:
-            form_g(g_first[:, cols, :], cols)
-        quantise_xm(0, 1, low_woven[0])
-        quantise_g(halves[0], g_first[:])
-        nc.scalar.copy(scalar_columns[0][:, halves[0]], multiply(0, halves[0])[:])
-        scalar_half(0, 0, scalar_columns[0])
-        for c in range(PAIR):
-            form_g(g_second[:, quarters[c], :], quarters[PAIR + c])
-        quantise_g(quarters[PAIR], g_second[:, quarters[0], :])
-        quantise_xm(1, 1, low_woven[1])
-        quantise_g(quarters[PAIR + 1], g_second[:, quarters[1], :])
-        nc.scalar.copy(scalar_columns[0][:, halves[1]], multiply(0, halves[1])[:])
-        scalar_half(0, 1, scalar_columns[0])
-        store(0)
+        for h in range(PAIR):
+            g_woven = [tile([P, P, PACK], BF16, "g_woven", tag) for tag in ("woven_even", "woven")]
+            for c in range(PAIR):
+                form_g(g_woven[c][:], h, quarters[c])
+            quantise_xm(h, 1, low_woven[h])
+            for c in range(PAIR):
+                quantise_g(quarters[PAIR * h + c], g_woven[c][:])
+            nc.scalar.copy(scalar_columns[0][:, halves[h]], multiply(0, halves[h])[:])
+            scalar_half(0, h, scalar_columns[0])
+        store(nc.scalar, 0)
 
-        def relay_words(first, count):
-            return relay[:, first : first + count]
-
-        def vector_tile(m, slots, columns):
-            nc.vector.tensor_copy(columns, multiply(m, slots)[:])
-            nc.vector.tensor_copy(listed(m, slots), columns)
-
-        def scalar_tile(m):
+        def scalar_tile(queue, m):
             columns = scalar_columns[m // PAIR % PAIR]
             nc.scalar.copy(columns[:], multiply(m, whole)[:])
             for h in range(PAIR):
                 scalar_half(m, h, columns)
-            store(m)
+            store(queue, m)
 
-        woven_two = woven_view(relay_words(LINE, HALF))
-        nc.vector.tensor_copy(*weave_views(2, woven_two))
-        early = tile([P, HALF], F32, "early")
-        nc.vector.tensor_copy(early[:], multiply(1, halves[0])[:])
-        quantise_xm(2, 1, woven_two)
-        nc.vector.tensor_copy(listed(1, halves[0]), early[:])
-        woven_three = woven_view(relay_words(HALF, HALF))
-        gpsimd_weave(3, 1, woven_three)
-        quantise_xm(3, 1, woven_three)
-        vector_tile(1, halves[1], relay_words(LINE, HALF))
-        store(1)
-        scalar_tile(2)
-        woven_four = woven_view(relay_words(N - LINE, N))
-        gpsimd_weave(4, PAIR, woven_four)
-        quantise_xm(4, PAIR, woven_four)
-        vector_tile(3, whole, relay_words(0, N))
-        store(3)
-        scalar_tile(4)
-        woven_six = woven_view(relay_words(PAIR * (N - LINE), N))
-        gpsimd_weave(6, PAIR, woven_six)
-        quantise_xm(6, PAIR, woven_six)
-        vector_tile(5, whole, relay_words(N - LINE, N))
-        store(5)
-        scalar_tile(6)
-        vector_tile(7, whole, relay_words(0, N))
-        store(7)
+        def vector_scatter(m, columns):
+            nc.vector.tensor_copy(listed(m, whole), columns[:])
+            store(nc.sync, m)
+
+        first_columns = tile([P, N], F32, "first_columns", "sigmoids1")
+        nc.vector.tensor_copy(first_columns[:, halves[0]], multiply(1, halves[0])[:])
+        woven = tile([P, HALF, PACK], BF16, "xm_woven", "woven")
+        for k in range(PAIR):
+            nc.vector.tensor_copy(*weave_views(PAIR + k, woven[:, quarters[k], :]))
+        nc.vector.tensor_copy(first_columns[:, halves[1]], multiply(1, halves[1])[:])
+        quantise_xm(PAIR, PAIR, woven[:])
+        vector_scatter(1, first_columns)
+        scalar_tile(nc.sync, 2)
+        vector_columns = tile([P, N], F32, "vector_columns")
+        for m, raw_tag in ((3, "table_scales"), (5, "table_words")):
+            woven = tile([P, HALF, PACK], BF16, "xm_woven", "woven")
+            gpsimd_weave(m + 1, PAIR, woven[:])
+            windows.append(zeroed_window(nc.gpsimd, raw_tag))
+            nc.vector.tensor_copy(vector_columns[:], multiply(m, whole)[:])
+            quantise_xm(m + 1, PAIR, woven[:])
+            vector_scatter(m, vector_columns)
+            scalar_tile(nc.scalar, m + 1)
+        nc.vector.tensor_copy(vector_columns[:], multiply(D_TILES - 1, whole)[:])
+        vector_scatter(D_TILES - 1, vector_columns)

@@ -80,6 +80,7 @@ def tile_attend_gsig_w_kernel(tc, xT, w_words, w_scales, y, wt, xm, offs, out):
         windows = [zeroed_window(nc.vector, "window%d" % m) for m in range(PAIR)]
         negated = keep.tile([P, PACK], F32, name="negated")
         nc.vector.tensor_scalar(negated[:], weights[:], -1.0, 0.0, MULT, ADD)
+        windows.append(zeroed_window(nc.vector, "window2"))
         windows.append(zeroed_window(nc.gpsimd, "weights"))
 
         picked_scales = tile([P, N], U8, "picked_scales")
@@ -225,7 +226,7 @@ def tile_attend_gsig_w_kernel(tc, xT, w_words, w_scales, y, wt, xm, offs, out):
             )
             return bank
 
-        window_of = [0, 1, 2, 3, 0, 4, 1, 2]
+        window_of = [m % len(windows) for m in range(D_TILES)]
 
         def listed(m, slots):
             return windows[window_of[m]][:].indirect(offsets[:, slots.start // PER_COLUMN : slots.stop // PER_COLUMN])
@@ -238,11 +239,12 @@ def tile_attend_gsig_w_kernel(tc, xT, w_words, w_scales, y, wt, xm, offs, out):
         def scalar_half(m, h, columns):
             nc.scalar.activation(listed(m, halves[h]), columns[:, halves[h]], COPY)
 
+        relay = ["relay_even", "relay_odd"]
         low_woven = [woven_view(margins[PACK - 1, h]) for h in range(PAIR)]
         for m in range(PAIR):
             nc.scalar.copy(*weave_views(m, low_woven[m]))
         for h in range(PAIR):
-            g_woven = [tile([P, P, PACK], BF16, "g_woven", tag) for tag in ("woven_even", "woven")]
+            g_woven = [tile([P, P, PACK], BF16, "g_woven", tag) for tag in relay]
             for c in range(PAIR):
                 form_g(g_woven[c][:], h, quarters[c])
             quantise_xm(h, 1, low_woven[h])
@@ -250,7 +252,7 @@ def tile_attend_gsig_w_kernel(tc, xT, w_words, w_scales, y, wt, xm, offs, out):
                 quantise_g(quarters[PAIR * h + c], g_woven[c][:])
             nc.scalar.copy(scalar_columns[0][:, halves[h]], multiply(0, halves[h])[:])
             scalar_half(0, h, scalar_columns[0])
-        store(nc.scalar, 0)
+        store(nc.sync, 0)
 
         def scalar_tile(queue, m):
             columns = scalar_columns[m // PAIR % PAIR]
@@ -265,21 +267,29 @@ def tile_attend_gsig_w_kernel(tc, xT, w_words, w_scales, y, wt, xm, offs, out):
 
         first_columns = tile([P, N], F32, "first_columns", "sigmoids1")
         nc.vector.tensor_copy(first_columns[:, halves[0]], multiply(1, halves[0])[:])
-        woven = tile([P, HALF, PACK], BF16, "xm_woven", "woven")
+        woven = [tile([P, P, PACK], BF16, "xm_woven", tag) for tag in relay]
         for k in range(PAIR):
-            nc.vector.tensor_copy(*weave_views(PAIR + k, woven[:, quarters[k], :]))
+            nc.vector.tensor_copy(*weave_views(2 + k, woven[k][:]))
         nc.vector.tensor_copy(first_columns[:, halves[1]], multiply(1, halves[1])[:])
-        quantise_xm(PAIR, PAIR, woven[:])
+        for k in range(PAIR):
+            quantise_xm(2 + k, 1, woven[k][:])
         vector_scatter(1, first_columns)
-        scalar_tile(nc.sync, 2)
-        vector_columns = tile([P, N], F32, "vector_columns")
-        for m, raw_tag in ((3, "table_scales"), (5, "table_words")):
-            woven = tile([P, HALF, PACK], BF16, "xm_woven", "woven")
-            gpsimd_weave(m + 1, PAIR, woven[:])
-            windows.append(zeroed_window(nc.gpsimd, raw_tag))
-            nc.vector.tensor_copy(vector_columns[:], multiply(m, whole)[:])
-            quantise_xm(m + 1, PAIR, woven[:])
-            vector_scatter(m, vector_columns)
-            scalar_tile(nc.scalar, m + 1)
-        nc.vector.tensor_copy(vector_columns[:], multiply(D_TILES - 1, whole)[:])
-        vector_scatter(D_TILES - 1, vector_columns)
+        scalar_tile(nc.scalar, 2)
+
+        def vector_tile(m, tag):
+            columns = tile([P, N], F32, "vector_columns", tag)
+            nc.vector.tensor_copy(columns[:], multiply(m, whole)[:])
+            vector_scatter(m, columns)
+
+        woven = [tile([P, P, PACK], BF16, "xm_woven", tag) for tag in relay]
+        for k in range(PAIR):
+            gpsimd_weave(4 + k, 1, woven[k][:])
+            quantise_xm(4 + k, 1, woven[k][:])
+        vector_tile(3, relay[0])
+        scalar_tile(nc.scalar, 4)
+        last_woven = tile([P, HALF, PACK], BF16, "last_woven", relay[1])
+        gpsimd_weave(6, PAIR, last_woven[:])
+        quantise_xm(6, PAIR, last_woven[:])
+        vector_tile(5, relay[1])
+        scalar_tile(nc.scalar, 6)
+        vector_tile(7, relay[0])

@@ -36,6 +36,7 @@ def tile_attend_gsig_w_kernel(tc, xT, w_words, w_scales, y, wt, xm, offs, out):
     nc = tc.nc
     with ExitStack() as ctx:
         keep = ctx.enter_context(tc.tile_pool(name="keep", bufs=1))
+        laid = ctx.enter_context(tc.tile_pool(name="laid", bufs=1))
         psum = ctx.enter_context(tc.psum_pool(name="psum", bufs=1))
         halves = [slice(0, HALF), slice(HALF, N)]
         quarters = [slice(c * P, (c + 1) * P) for c in range(N // P)]
@@ -44,6 +45,9 @@ def tile_attend_gsig_w_kernel(tc, xT, w_words, w_scales, y, wt, xm, offs, out):
 
         def tile(shape, dtype, name, tag=None):
             return keep.tile(shape, dtype, name=name, tag=tag or name, align_bytes=64)
+
+        def laid_tile(shape, dtype, name, offset):
+            return laid.tile(shape, dtype, name=name, align_bytes=64, offset=offset)
 
         def woven_view(words):
             return words.bitcast(BF16).rearrange("p (n j) -> p n j", j=PACK)
@@ -234,29 +238,36 @@ def tile_attend_gsig_w_kernel(tc, xT, w_words, w_scales, y, wt, xm, offs, out):
         def store(queue, m):
             queue.dma_start(out[m * P : (m + 1) * P, :], windows[window_of[m]][:])
 
-        scalar_columns = [tile([P, N], F32, "scalar_columns%d" % k) for k in range(PAIR)]
+        staged = 4 * N
+        scalar_base = 4 * staged
+        first_staged = laid_tile([P, N], F32, "first_staged", scalar_base)
 
         def scalar_half(m, h, columns):
             nc.scalar.activation(listed(m, halves[h]), columns[:, halves[h]], COPY)
 
-        relay = ["relay_even", "relay_odd"]
+        one, line = P * PACK * 2, 64
+        base = PAIR * one + line
         low_woven = [woven_view(margins[PACK - 1, h]) for h in range(PAIR)]
         for m in range(PAIR):
             nc.scalar.copy(*weave_views(m, low_woven[m]))
         for h in range(PAIR):
-            g_woven = [tile([P, P, PACK], BF16, "g_woven", tag) for tag in relay]
+            g_woven = [laid_tile([P, P, PACK], BF16, "g_even%d" % h, base), tile([P, P, PACK], BF16, "g_odd")]
             for c in range(PAIR):
                 form_g(g_woven[c][:], h, quarters[c])
             quantise_xm(h, 1, low_woven[h])
             for c in range(PAIR):
                 quantise_g(quarters[PAIR * h + c], g_woven[c][:])
-            nc.scalar.copy(scalar_columns[0][:, halves[h]], multiply(0, halves[h])[:])
-            scalar_half(0, h, scalar_columns[0])
+            copy = nc.scalar.copy if h == 0 else nc.vector.tensor_copy
+            for slots in quarters[PAIR * h : PAIR * (h + 1)]:
+                copy(first_staged[:, slots], multiply(0, slots)[:])
+            scalar_half(0, h, first_staged)
         store(nc.sync, 0)
 
-        def scalar_tile(queue, m):
-            columns = scalar_columns[m // PAIR % PAIR]
-            nc.scalar.copy(columns[:], multiply(m, whole)[:])
+        def scalar_tile(queue, m, offset):
+            columns = laid_tile([P, N], F32, "columns%d" % m, offset)
+            bank = multiply(m, whole)
+            for slots in halves:
+                nc.scalar.copy(columns[:, slots], bank[:, slots])
             for h in range(PAIR):
                 scalar_half(m, h, columns)
             store(queue, m)
@@ -265,31 +276,25 @@ def tile_attend_gsig_w_kernel(tc, xT, w_words, w_scales, y, wt, xm, offs, out):
             nc.vector.tensor_copy(listed(m, whole), columns[:])
             store(nc.sync, m)
 
-        first_columns = tile([P, N], F32, "first_columns", "sigmoids1")
-        nc.vector.tensor_copy(first_columns[:, halves[0]], multiply(1, halves[0])[:])
-        woven = [tile([P, P, PACK], BF16, "xm_woven", tag) for tag in relay]
-        for k in range(PAIR):
-            nc.vector.tensor_copy(*weave_views(2 + k, woven[k][:]))
-        nc.vector.tensor_copy(first_columns[:, halves[1]], multiply(1, halves[1])[:])
-        for k in range(PAIR):
-            quantise_xm(2 + k, 1, woven[k][:])
-        vector_scatter(1, first_columns)
-        scalar_tile(nc.scalar, 2)
-
-        def vector_tile(m, tag):
-            columns = tile([P, N], F32, "vector_columns", tag)
+        def vector_tile(m, offset):
+            columns = laid_tile([P, N], F32, "columns%d" % m, offset)
             nc.vector.tensor_copy(columns[:], multiply(m, whole)[:])
             vector_scatter(m, columns)
 
-        woven = [tile([P, P, PACK], BF16, "xm_woven", tag) for tag in relay]
-        for k in range(PAIR):
-            gpsimd_weave(4 + k, 1, woven[k][:])
-            quantise_xm(4 + k, 1, woven[k][:])
-        vector_tile(3, relay[0])
-        scalar_tile(nc.scalar, 4)
-        last_woven = tile([P, HALF, PACK], BF16, "last_woven", relay[1])
-        gpsimd_weave(6, PAIR, last_woven[:])
-        quantise_xm(6, PAIR, last_woven[:])
-        vector_tile(5, relay[1])
-        scalar_tile(nc.scalar, 6)
-        vector_tile(7, relay[0])
+        for m, offset in ((2, base), (3, base - one + line)):
+            woven = laid_tile([P, P, PACK], BF16, "woven%d" % m, offset)
+            nc.vector.tensor_copy(*weave_views(m, woven[:]))
+            quantise_xm(m, 1, woven[:])
+        first_columns = laid_tile([P, N], F32, "first_columns", base + one - line)
+        for h in range(PAIR):
+            nc.vector.tensor_copy(first_columns[:, halves[h]], multiply(1, halves[h])[:])
+        vector_scatter(1, first_columns)
+        scalar_tile(nc.scalar, 2, scalar_base + staged)
+        for m, offsets_of, columns_at in ((3, (base - one - line, base - line), base + one), (5, (base - one, base), base + one)):
+            for k in range(PAIR):
+                woven = laid_tile([P, P, PACK], BF16, "woven%d" % (m + 1 + k), offsets_of[k])
+                gpsimd_weave(m + 1 + k, 1, woven[:])
+                quantise_xm(m + 1 + k, 1, woven[:])
+            vector_tile(m, columns_at)
+            scalar_tile(nc.scalar, m + 1, scalar_base + PAIR * staged)
+        vector_tile(7, base + one)

@@ -206,8 +206,8 @@ def tile_attend_gsig_w_kernel(tc, xT, w_words, w_scales, y, wt, xm, offs, out):
 
         def gpsimd_weave(first, count, woven):
             for k in range(count):
-                target, raw = weave_views(first + k, woven[:, quarters[k], :])
-                nc.gpsimd.tensor_scalar(target, raw, 1.0, 0.0, MULT, ADD)
+                raw = xm_raw[first + k].rearrange("p t c -> p c t")
+                nc.gpsimd.tensor_scalar(woven[:, quarters[k], :], raw, 1.0, 0.0, MULT, ADD)
 
         def quantise_xm(first, count, woven):
             cols = slice(first * P, (first + count) * P)
@@ -246,12 +246,12 @@ def tile_attend_gsig_w_kernel(tc, xT, w_words, w_scales, y, wt, xm, offs, out):
             nc.scalar.activation(listed(m, halves[h]), columns[:, halves[h]], COPY)
 
         one, line = P * PACK * 2, 64
-        base = PAIR * one + line
+        base = 3 * one
         low_woven = [woven_view(margins[PACK - 1, h]) for h in range(PAIR)]
         for m in range(PAIR):
             nc.scalar.copy(*weave_views(m, low_woven[m]))
         for h in range(PAIR):
-            g_woven = [laid_tile([P, P, PACK], BF16, "g_even%d" % h, base), tile([P, P, PACK], BF16, "g_odd")]
+            g_woven = [laid_tile([P, P, PACK], BF16, "g_even%d" % h, base), laid_tile([P, P, PACK], BF16, "g_odd%d" % h, base - 2 * one)]
             for c in range(PAIR):
                 form_g(g_woven[c][:], h, quarters[c])
             quantise_xm(h, 1, low_woven[h])
@@ -260,6 +260,9 @@ def tile_attend_gsig_w_kernel(tc, xT, w_words, w_scales, y, wt, xm, offs, out):
             copy = nc.scalar.copy if h == 0 else nc.vector.tensor_copy
             for slots in quarters[PAIR * h : PAIR * (h + 1)]:
                 copy(first_staged[:, slots], multiply(0, slots)[:])
+            if h == 1:
+                first_columns = laid_tile([P, N], F32, "first_columns", base + one - line)
+                nc.scalar.copy(first_columns[:, halves[0]], multiply(1, halves[0])[:])
             scalar_half(0, h, first_staged)
         store(nc.sync, 0)
 
@@ -281,20 +284,18 @@ def tile_attend_gsig_w_kernel(tc, xT, w_words, w_scales, y, wt, xm, offs, out):
             nc.vector.tensor_copy(columns[:], multiply(m, whole)[:])
             vector_scatter(m, columns)
 
-        for m, offset in ((2, base), (3, base - one + line)):
+        for m, offset in ((2, base - one + line), (3, base - 2 * one)):
             woven = laid_tile([P, P, PACK], BF16, "woven%d" % m, offset)
             nc.vector.tensor_copy(*weave_views(m, woven[:]))
             quantise_xm(m, 1, woven[:])
-        first_columns = laid_tile([P, N], F32, "first_columns", base + one - line)
-        for h in range(PAIR):
-            nc.vector.tensor_copy(first_columns[:, halves[h]], multiply(1, halves[h])[:])
+        nc.vector.tensor_copy(first_columns[:, halves[1]], multiply(1, halves[1])[:])
         vector_scatter(1, first_columns)
-        scalar_tile(nc.scalar, 2, scalar_base + staged)
-        for m, offsets_of, columns_at in ((3, (base - one - line, base - line), base + one), (5, (base - one, base), base + one)):
+        scalar_tile(nc.sync, 2, scalar_base + staged)
+        for m, offsets_of, columns_at in ((3, (base - 5 * one // 2, base - 3 * one // 2), base + one), (5, (base - 2 * one, base - one), base + one)):
             for k in range(PAIR):
                 woven = laid_tile([P, P, PACK], BF16, "woven%d" % (m + 1 + k), offsets_of[k])
                 gpsimd_weave(m + 1 + k, 1, woven[:])
                 quantise_xm(m + 1 + k, 1, woven[:])
             vector_tile(m, columns_at)
-            scalar_tile(nc.scalar, m + 1, scalar_base + PAIR * staged)
+            scalar_tile(nc.sync if m == 3 else nc.scalar, m + 1, scalar_base + PAIR * staged)
         vector_tile(7, base + one)

@@ -104,24 +104,29 @@ def tile_attend_gsig_w_kernel(tc, xT, w_words, w_scales, y, wt, xm, offs, out):
         nc.sync.dma_start(after_scales[:, PAIR * R :], y_rows[:, 0, :])
         move_plane(1)
         x_raw = [[x_first[:, places, :] for places in pairs], [x_third[:], x_last]]
-        picked_words = tile([P, N], U32, "picked_words")
+        head = 16 * 1024
+        picked_words = laid_tile([P, N], U32, "picked_words", head)
         nc.vector.tensor_copy(picked_words[:], table_words[:].bitcast(U32).indirect(offsets[:]))
         w_codes = tile([P, PASSES, N], U16, "w_codes")
         word_pairs = picked_words[:].bitcast(U16).rearrange("p (n o) -> p o n", o=PASSES)
-        nc.vector.tensor_copy(w_codes[:, 0, :], word_pairs[:, 0, :])
+        for o in range(PASSES):
+            nc.vector.tensor_copy(w_codes[:, o, :], word_pairs[:, o, :])
 
         y_rest = tile([P, PACK - 1, N], F32, "y_rest", "table_words")
         nc.sync.dma_start(y_rest[:, 0, :], y_rows[:, 1, :])
         nc.sync.dma_start(y_rest[:, 1:, :], y_rows[:, pairs[1], :])
         signs = [after_scales[:, PAIR * R :]] + [y_rest[:, j, :] for j in range(PACK - 1)]
 
-        x_codes = [tile([P, R], U32, "x_codes%d" % o) for o in range(PASSES)]
+        low_codes = tile([P, PAIR * P], U32, "low_codes")
+        high_codes = laid_tile([P, PAIR * P], U32, "high_codes", head + 1024)
+        last_codes = tile([P, R], U32, "last_codes")
+        x_codes = [[t[:, cols] for t in (low_codes, high_codes) for cols in quarters[:PAIR]], [last_codes[:, cols] for cols in quarters]]
         x_planes = [tile([P, R], U8, "x_plane%d" % o) for o in range(PASSES)]
         factor_words = [tile([P, PACK * HALF], F32, "factor_words%d" % h) for h in range(PAIR)]
         factors = [t[:].rearrange("p (j n) -> p j n", j=PACK) for t in factor_words]
-        x_woven = [[tile([P, PAIR, P, PACK], BF16, "x_woven0_%d" % e)[:] for e in range(PAIR)]]
+        x_woven = [[laid_tile([P, PAIR, P, PACK], BF16, "x_woven0_0", head - 1024)[:], tile([P, PAIR, P, PACK], BF16, "x_woven0_1")[:]]]
         last_share = factor_words[1][:, HALF : HALF + N].bitcast(BF16).rearrange("p (j s t) -> p j s t", j=PAIR, t=PACK)
-        x_woven.append([tile([P, PAIR, P, PACK], BF16, "x_woven1_0")[:], last_share])
+        x_woven.append([laid_tile([P, PAIR, P, PACK], BF16, "x_woven1_0", head - 1024)[:], last_share])
 
         def weave_x(copy, o, e, places, raw):
             copy(
@@ -129,22 +134,21 @@ def tile_attend_gsig_w_kernel(tc, xT, w_words, w_scales, y, wt, xm, offs, out):
                 raw.rearrange("p t (s j) -> p s t j", j=PACK)[:, :, :, pairs[e]],
             )
 
-        def quantise_x(o, first, count):
+        def quantise_x(codes, o, first, count):
             cols = slice(first * P, (first + count) * P)
             woven = x_woven[o][first // PAIR][:, first % PAIR : first % PAIR + count, :, :]
-            nc.vector.quantize_mx(x_codes[o][:, cols].bitcast(E4M3), x_planes[o][:, cols], woven.rearrange("p j s t -> p (j s t)"))
+            nc.vector.quantize_mx(codes.bitcast(E4M3), x_planes[o][:, cols], woven.rearrange("p j s t -> p (j s t)"))
 
-        weave_x(nc.scalar.copy, 0, 0, pairs[0], x_raw[0][0])
-        weave_x(nc.vector.tensor_copy, 0, 0, pairs[1], x_raw[0][1])
-        weave_x(nc.scalar.copy, 0, 1, slice(0, PACK), x_first[:])
-        nc.vector.tensor_copy(w_codes[:, 1, :], word_pairs[:, 1, :])
-        for e in range(PAIR):
-            quantise_x(0, e * PAIR, PAIR)
+        for places in range(PAIR):
+            weave_x(nc.scalar.copy, 0, 1, pairs[places], x_raw[0][places])
+        weave_x(nc.vector.tensor_copy, 0, 0, slice(0, PACK), x_first[:])
+        quantise_x(high_codes[:], 0, PAIR, PAIR)
+        quantise_x(low_codes[:], 0, 0, PAIR)
         for places in range(PAIR):
             weave_x(nc.vector.tensor_copy, 1, 0, pairs[places], x_raw[1][places])
             weave_x(nc.scalar.copy, 1, 1, pairs[places], x_raw[1][places])
         for j in range(PACK):
-            quantise_x(1, j, 1)
+            quantise_x(x_codes[1][j], 1, j, 1)
 
         xm_rows = xm[0].rearrange("(p t) c -> p t c", t=PACK)
         xm_first = tile([P, PACK, PAIR * P], F32, "xm_first", "x_first")
@@ -162,7 +166,7 @@ def tile_attend_gsig_w_kernel(tc, xT, w_words, w_scales, y, wt, xm, offs, out):
             for j, h in pieces:
                 nc.tensor.matmul_mx(
                     scores[j, h][:],
-                    lhsT=x_codes[o][:, quarters[j]].bitcast(E4M3),
+                    lhsT=x_codes[o][j].bitcast(E4M3),
                     lhsT_scale=x_planes[o][:, quarters[j]],
                     rhs=w_codes[:, o, halves[h]].bitcast(E2M1),
                     rhs_scale=w_planes[o][:, halves[h]],

@@ -174,17 +174,21 @@ def tile_attend_gsig_w_kernel(tc, xT, w_words, w_scales, y, wt, xm, offs, out):
                     stop=(o == PASSES - 1),
                 )
 
-        for b, (j, h) in enumerate(pieces):
-            if b < SCALAR_FACTORS:
-                nc.scalar.activation(factors[h][:, j, :], signs[j][:, halves[h]], COPY, scale=negated[:, j : j + 1])
-            else:
-                nc.gpsimd.tensor_scalar(factors[h][:, j, :], signs[j][:, halves[h]], negated[:, j : j + 1], 0.0, MULT, ADD)
+        def scalar_factors(j, h):
+            nc.scalar.activation(factors[h][:, j, :], signs[j][:, halves[h]], COPY, scale=negated[:, j : j + 1])
+
+        for j, h in pieces[:SCALAR_FACTORS]:
+            scalar_factors(j, h)
+        for j, h in pieces[PACK:]:
+            nc.gpsimd.tensor_scalar(factors[h][:, j, :], signs[j][:, halves[h]], negated[:, j : j + 1], 0.0, MULT, ADD)
         margin_words = tile([P, PACK * N], F32, "margin_words")
         margins = {piece: margin_words[:, b * HALF : (b + 1) * HALF] for b, piece in enumerate(pieces)}
+        margins[PAIR, 1] = factor_words[1][:, HALF : PAIR * HALF]
         sigmoids = [tile([P, PACK, HALF], F32, "sigmoids%d" % h) for h in range(PAIR)]
         for j, h in pieces:
             nc.vector.tensor_tensor(margins[j, h], scores[j, h][:], signs[j][:, halves[h]], MULT)
             nc.scalar.activation(sigmoids[h][:, j, :], margins[j, h], SIGMOID, scale=-1.0)
+        scalar_factors(1, 1)
 
         g_codes = tile([P, N], U32, "g_codes")
         g_plane = tile([P, N], U8, "g_plane")

@@ -57,11 +57,12 @@ def tile_attend_gsig_w_kernel(tc, xT, w_words, w_scales, y, wt, xm, offs, out):
         nc.scalar.dma_start(weights[:], wt[0].rearrange("(p j) o -> p (j o)", j=PACK))
         table_words = tile([P, T], I32, "table_words")
         words = w_words[0].rearrange("p t b -> p (t b)").bitcast(I32)
-        nc.sync.dma_start(table_words[:, : T // 2], words[:, : T // 2])
-        nc.sync.dma_start(offsets[:], offs)
         table_scales = tile([P, T], U8, "table_scales")
-        nc.vector.memset(table_scales[:].bitcast(I32), 0)
-        nc.sync.dma_start(table_scales[0:P:PACK, :].bitcast(I32), w_scales.rearrange("o f t -> (o f) t").bitcast(I32))
+        scale_rows = P - QUADRANT
+        nc.gpsimd.memset(table_scales[:scale_rows, :].bitcast(I32), 0)
+        nc.sync.dma_start(table_scales[scale_rows:, :].bitcast(I32), w_scales.rearrange("o f t -> (o f) t").bitcast(I32))
+        nc.sync.dma_start(offsets[:], offs)
+        nc.sync.dma_start(table_words[:, : T // 2], words[:, : T // 2])
         nc.sync.dma_start(table_words[:, T // 2 :], words[:, T // 2 :])
         x_first = tile([P, PACK, R], F32, "x_first")
         x_third = tile([P, PAIR, R], F32, "x_third")
@@ -71,7 +72,7 @@ def tile_attend_gsig_w_kernel(tc, xT, w_words, w_scales, y, wt, xm, offs, out):
         nc.sync.dma_start(x_third[:], x_rows[1][:, pairs[0], :])
 
         planes = tile([P, PASSES * N], U8, "planes")
-        nc.gpsimd.memset(planes[:].bitcast(I32), 0)
+        nc.vector.memset(planes[:].bitcast(I32), 0)
         w_planes = [planes[:, o * N : (o + 1) * N] for o in range(PASSES)]
         warm = keep.tile([P, 1], F32, name="warm")
         nc.scalar.activation(warm[:], weights[:, 0:1], SIGMOID)
@@ -92,8 +93,8 @@ def tile_attend_gsig_w_kernel(tc, xT, w_words, w_scales, y, wt, xm, offs, out):
 
         def move_plane(o):
             for r in range(PACK):
-                first = P // PASSES * o + PACK * r
-                rows = picked_scales[first : P // PASSES * (o + 1) : HALF_QUADRANT, :]
+                first = scale_rows + HALF_QUADRANT * o
+                rows = picked_scales[first + r : first + HALF_QUADRANT : PACK, :]
                 nc.sync.dma_start(w_planes[o][r:P:QUADRANT, :].bitcast(I32), rows.bitcast(I32))
 
         move_plane(0)

@@ -44,7 +44,7 @@ def tile_attend_gsig_w_kernel(tc, xT, w_words, w_scales, y, wt, xm, offs, out):
         whole = slice(0, N)
 
         def tile(shape, dtype, name, tag=None):
-            return keep.tile(shape, dtype, name=name, tag=tag or name, align_bytes=64)
+            return keep.tile(shape, dtype, name=name, tag=tag or name, align_bytes=256)
 
         def laid_tile(shape, dtype, name, offset):
             return laid.tile(shape, dtype, name=name, align_bytes=64, offset=offset)

@@ -74,8 +74,12 @@ def tile_attend_gsig_w_kernel(tc, xT, w_words, w_scales, y, wt, xm, offs, out):
         planes = tile([P, PASSES * N], U8, "planes")
         nc.vector.memset(planes[:].bitcast(I32), 0)
         w_planes = [planes[:, o * N : (o + 1) * N] for o in range(PASSES)]
+        warm_in = keep.tile([P, 1], F32, name="warm_in")
         warm = keep.tile([P, 1], F32, name="warm")
-        nc.scalar.activation(warm[:], weights[:, 0:1], SIGMOID)
+        ones = keep.tile([P, 1], F32, name="ones")
+        nc.gpsimd.memset(warm_in[:], 0.0)
+        nc.gpsimd.memset(ones[:], 1.0)
+        nc.scalar.activation(warm[:], warm_in[:], SIGMOID)
 
         def zeroed_window(engine, tag):
             window = tile([P, T], F32, "window", tag)
@@ -105,7 +109,7 @@ def tile_attend_gsig_w_kernel(tc, xT, w_words, w_scales, y, wt, xm, offs, out):
         nc.sync.dma_start(after_scales[:, PAIR * R :], y_rows[:, 0, :])
         move_plane(1)
         x_raw = [[x_first[:, places, :] for places in pairs], [x_third[:], x_last]]
-        head = 16 * 1024
+        head = 20 * 1024
         picked_words = laid_tile([P, N], U32, "picked_words", head)
         nc.vector.tensor_copy(picked_words[:], table_words[:].bitcast(U32).indirect(offsets[:]))
         w_codes = tile([P, PASSES, N], U16, "w_codes")
@@ -222,11 +226,8 @@ def tile_attend_gsig_w_kernel(tc, xT, w_words, w_scales, y, wt, xm, offs, out):
             cols = slice(first * P, (first + count) * P)
             nc.vector.quantize_mx(xm_codes[:, cols].bitcast(E4M3), xm_plane[:, cols], woven.rearrange("p c t -> p (c t)"))
 
-        passes_done = []
-
-        def multiply(m, slots):
-            bank = psum.tile([P, slots.stop - slots.start], F32, name="grad", tag="bank%d" % (len(passes_done) % len(pieces)))
-            passes_done.append(m)
+        def multiply(m, slots, b):
+            bank = psum.tile([P, slots.stop - slots.start], F32, name="grad", tag="bank%d" % b)
             cols = slice(m * P, (m + 1) * P)
             nc.tensor.matmul_mx(
                 bank[:],
@@ -267,44 +268,44 @@ def tile_attend_gsig_w_kernel(tc, xT, w_words, w_scales, y, wt, xm, offs, out):
             for c in range(PAIR):
                 quantise_g(quarters[PAIR * h + c], g_woven[c][:])
             copy = nc.scalar.copy if h == 0 else nc.vector.tensor_copy
-            for slots in quarters[PAIR * h : PAIR * (h + 1)]:
-                copy(first_staged[:, slots], multiply(0, slots)[:])
+            for c in range(PAIR * h, PAIR * (h + 1)):
+                copy(first_staged[:, quarters[c]], multiply(0, quarters[c], c)[:])
             if h == 1:
                 first_columns = laid_tile([P, N], F32, "first_columns", base + one - line)
-                nc.scalar.copy(first_columns[:, halves[0]], multiply(1, halves[0])[:])
+                nc.scalar.copy(first_columns[:, halves[0]], multiply(1, halves[0], 4)[:])
             scalar_half(0, h, first_staged)
         store(nc.sync, 0)
 
-        def scalar_tile(queue, m, offset):
-            columns = laid_tile([P, N], F32, "columns%d" % m, offset)
-            bank = multiply(m, whole)
-            for slots in halves:
-                nc.scalar.copy(columns[:, slots], bank[:, slots])
-            for h in range(PAIR):
-                scalar_half(m, h, columns)
+        def scalar_scatter(queue, m, columns):
+            nc.scalar.activation(listed(m, whole), columns[:], COPY, scale=ones[:])
             store(queue, m)
 
         def vector_scatter(m, columns):
             nc.vector.tensor_copy(listed(m, whole), columns[:])
             store(nc.sync, m)
 
-        def vector_tile(m, offset):
-            columns = laid_tile([P, N], F32, "columns%d" % m, offset)
-            nc.vector.tensor_copy(columns[:], multiply(m, whole)[:])
-            vector_scatter(m, columns)
+        def staging(m, offset):
+            return laid_tile([P, N], F32, "columns%d" % m, offset)
 
         for m, offset in ((2, base - one + line), (3, base - 2 * one)):
             woven = laid_tile([P, P, PACK], BF16, "woven%d" % m, offset)
             nc.vector.tensor_copy(*weave_views(m, woven[:]))
             quantise_xm(m, 1, woven[:])
-        nc.vector.tensor_copy(first_columns[:, halves[1]], multiply(1, halves[1])[:])
+        nc.vector.tensor_copy(first_columns[:, halves[1]], multiply(1, halves[1], 5)[:])
         vector_scatter(1, first_columns)
-        scalar_tile(nc.sync, 2, scalar_base + staged)
-        for m, offsets_of, columns_at in ((3, (base - 5 * one // 2, base - 3 * one // 2), base + one), (5, (base - 2 * one, base - one), base + one)):
+        for m, places, banks in ((2, (base - 5 * one // 2, base - 3 * one // 2), (6, 7)), (4, (base - 2 * one, base - one), (0, 1))):
+            even, odd = staging(m, (8 + m) * one), staging(m + 1, (12 + m) * one)
+            nc.scalar.copy(even[:], multiply(m, whole, banks[0])[:])
+            nc.scalar.copy(odd[:, halves[0]], multiply(m + 1, halves[0], banks[1])[:])
+            scalar_scatter(nc.sync, m, even)
             for k in range(PAIR):
-                woven = laid_tile([P, P, PACK], BF16, "woven%d" % (m + 1 + k), offsets_of[k])
-                gpsimd_weave(m + 1 + k, 1, woven[:])
-                quantise_xm(m + 1 + k, 1, woven[:])
-            vector_tile(m, columns_at)
-            scalar_tile(nc.sync if m == 3 else nc.scalar, m + 1, scalar_base + PAIR * staged)
-        vector_tile(7, base + one)
+                woven = laid_tile([P, P, PACK], BF16, "woven%d" % (m + 2 + k), places[k])
+                gpsimd_weave(m + 2 + k, 1, woven[:])
+                quantise_xm(m + 2 + k, 1, woven[:])
+            nc.vector.tensor_copy(odd[:, halves[1]], multiply(m + 1, halves[1], banks[0])[:])
+            vector_scatter(m + 1, odd)
+        even, odd = staging(6, 10 * one + line), staging(7, 14 * one - line)
+        nc.scalar.copy(even[:], multiply(6, whole, 2)[:])
+        nc.scalar.copy(odd[:], multiply(7, whole, 3)[:])
+        scalar_scatter(nc.scalar, 6, even)
+        vector_scatter(7, odd)

@@ -21,7 +21,6 @@ SIGMOID = mybir.ActivationFunctionType.Sigmoid
 
 P = 128
 QUADRANT = 32
-HALF_QUADRANT = 16
 PACK = 4
 PAIR = 2
 K_PASS = P * PACK
@@ -29,7 +28,6 @@ PASSES = D // K_PASS
 D_TILES = D // P
 PER_COLUMN = 16
 HALF = N // 2
-SCALAR_FACTORS = 3
 
 
 def tile_attend_gsig_w_kernel(tc, xT, w_words, w_scales, y, wt, xm, offs, out):
@@ -59,8 +57,7 @@ def tile_attend_gsig_w_kernel(tc, xT, w_words, w_scales, y, wt, xm, offs, out):
         words = w_words[0].rearrange("p t b -> p (t b)").bitcast(I32)
         table_scales = tile([P, T], U8, "table_scales")
         scale_rows = P - QUADRANT
-        nc.gpsimd.memset(table_scales[:scale_rows, :].bitcast(I32), 0)
-        nc.sync.dma_start(table_scales[scale_rows:, :].bitcast(I32), w_scales.rearrange("o f t -> (o f) t").bitcast(I32))
+        nc.sync.dma_start(table_scales[scale_rows:, :].bitcast(I32), w_scales.rearrange("o f t -> f o t").bitcast(I32))
         nc.sync.dma_start(offsets[:], offs)
         nc.sync.dma_start(table_words[:, : T // 2], words[:, : T // 2])
         nc.sync.dma_start(table_words[:, T // 2 :], words[:, T // 2 :])
@@ -71,14 +68,15 @@ def tile_attend_gsig_w_kernel(tc, xT, w_words, w_scales, y, wt, xm, offs, out):
             nc.sync.dma_start(x_first[:, places, :], x_rows[0][:, places, :])
         nc.sync.dma_start(x_third[:], x_rows[1][:, pairs[0], :])
 
-        planes = tile([P, PASSES * N], U8, "planes")
-        nc.vector.memset(planes[:].bitcast(I32), 0)
-        w_planes = [planes[:, o * N : (o + 1) * N] for o in range(PASSES)]
         warm_in = keep.tile([P, 1], F32, name="warm_in")
         warm = keep.tile([P, 1], F32, name="warm")
         ones = keep.tile([P, 1], F32, name="ones")
-        nc.gpsimd.memset(warm_in[:], 0.0)
-        nc.gpsimd.memset(ones[:], 1.0)
+        nc.vector.memset(warm_in[:], 0.0)
+        nc.vector.memset(ones[:], 1.0)
+        nc.vector.memset(table_scales[:scale_rows, :].bitcast(I32), 0)
+        planes = tile([P, PASSES * N], U8, "planes")
+        nc.vector.memset(planes[:].bitcast(I32), 0)
+        w_planes = [planes[:, o * N : (o + 1) * N] for o in range(PASSES)]
         nc.scalar.activation(warm[:], warm_in[:], SIGMOID)
 
         def zeroed_window(engine, tag):
@@ -95,19 +93,18 @@ def tile_attend_gsig_w_kernel(tc, xT, w_words, w_scales, y, wt, xm, offs, out):
         picked_scales = tile([P, N], U8, "picked_scales")
         nc.vector.tensor_copy(picked_scales[:], table_scales[:].indirect(offsets[:]))
 
-        def move_plane(o):
-            for r in range(PACK):
-                first = scale_rows + HALF_QUADRANT * o
-                rows = picked_scales[first + r : first + HALF_QUADRANT : PACK, :]
-                nc.sync.dma_start(w_planes[o][r:P:QUADRANT, :].bitcast(I32), rows.bitcast(I32))
-
-        move_plane(0)
+        rows_a_quadrant = PACK * PASSES
+        for q in range(P // QUADRANT):
+            first = scale_rows + q * rows_a_quadrant
+            nc.sync.dma_start(
+                planes[q * QUADRANT : q * QUADRANT + PACK, :].bitcast(I32),
+                picked_scales[first : first + rows_a_quadrant, :].bitcast(I32),
+            )
         y_rows = y[0].rearrange("(p j) n -> p j n", j=PACK)
         after_scales = tile([P, PAIR * R + N], F32, "after_scales", "table_scales")
         x_last = after_scales[:, : PAIR * R].rearrange("p (t c) -> p t c", t=PAIR)
         nc.sync.dma_start(x_last, x_rows[1][:, pairs[1], :])
         nc.sync.dma_start(after_scales[:, PAIR * R :], y_rows[:, 0, :])
-        move_plane(1)
         x_raw = [[x_first[:, places, :] for places in pairs], [x_third[:], x_last]]
         head = 20 * 1024
         picked_words = laid_tile([P, N], U32, "picked_words", head)
@@ -127,10 +124,8 @@ def tile_attend_gsig_w_kernel(tc, xT, w_words, w_scales, y, wt, xm, offs, out):
         last_codes = tile([P, R], U32, "last_codes")
         x_codes = [[t[:, cols] for t in (low_codes, high_codes) for cols in quarters[:PAIR]], [last_codes[:, cols] for cols in quarters]]
         x_planes = [tile([P, R], U8, "x_plane%d" % o) for o in range(PASSES)]
-        factor_words = [tile([P, PACK * HALF], F32, "factor_words%d" % h) for h in range(PAIR)]
-        factors = [t[:].rearrange("p (j n) -> p j n", j=PACK) for t in factor_words]
         x_woven = [[laid_tile([P, PAIR, P, PACK], BF16, "x_woven0_0", head - 1024)[:], tile([P, PAIR, P, PACK], BF16, "x_woven0_1")[:]]]
-        last_share = factor_words[1][:, HALF : HALF + N].bitcast(BF16).rearrange("p (j s t) -> p j s t", j=PAIR, t=PACK)
+        last_share = tile([P, PAIR, P, PACK], BF16, "x_woven1_1")[:]
         x_woven.append([laid_tile([P, PAIR, P, PACK], BF16, "x_woven1_0", head - 1024)[:], last_share])
 
         def weave_x(copy, o, e, places, raw):
@@ -179,21 +174,17 @@ def tile_attend_gsig_w_kernel(tc, xT, w_words, w_scales, y, wt, xm, offs, out):
                     stop=(o == PASSES - 1),
                 )
 
-        def scalar_factors(j, h):
-            nc.scalar.activation(factors[h][:, j, :], signs[j][:, halves[h]], COPY, scale=negated[:, j : j + 1])
-
-        for j, h in pieces[:SCALAR_FACTORS]:
-            scalar_factors(j, h)
-        for j, h in pieces[PACK:]:
-            nc.gpsimd.tensor_scalar(factors[h][:, j, :], signs[j][:, halves[h]], negated[:, j : j + 1], 0.0, MULT, ADD)
+        factors = tile([P, PACK, N], F32, "factors")
+        for j in range(PAIR):
+            nc.scalar.activation(factors[:, j, :], signs[j], COPY, scale=negated[:, j : j + 1])
+        for j in range(PAIR, PACK):
+            nc.gpsimd.tensor_scalar(factors[:, j, :], signs[j], negated[:, j : j + 1], 0.0, MULT, ADD)
         margin_words = tile([P, PACK * N], F32, "margin_words")
         margins = {piece: margin_words[:, b * HALF : (b + 1) * HALF] for b, piece in enumerate(pieces)}
-        margins[PAIR, 1] = factor_words[1][:, HALF : PAIR * HALF]
         sigmoids = [tile([P, PACK, HALF], F32, "sigmoids%d" % h) for h in range(PAIR)]
         for j, h in pieces:
             nc.vector.tensor_tensor(margins[j, h], scores[j, h][:], signs[j][:, halves[h]], MULT)
             nc.scalar.activation(sigmoids[h][:, j, :], margins[j, h], SIGMOID, scale=-1.0)
-        scalar_factors(1, 1)
 
         g_codes = tile([P, N], U32, "g_codes")
         g_plane = tile([P, N], U8, "g_plane")
@@ -204,7 +195,7 @@ def tile_attend_gsig_w_kernel(tc, xT, w_words, w_scales, y, wt, xm, offs, out):
             nc.vector.tensor_tensor(
                 woven.rearrange("p (c i) j -> p c j i", i=PAIR),
                 sigmoids[h][:, :, slots].rearrange("p j (c i) -> p c j i", i=PAIR),
-                factors[h][:, :, slots].rearrange("p j (c i) -> p c j i", i=PAIR),
+                factors[:, :, halves[h]][:, :, slots].rearrange("p j (c i) -> p c j i", i=PAIR),
                 MULT,
             )
 

@@ -115,17 +115,16 @@ def tile_attend_gsig_w_kernel(tc, xT, w_words, w_scales, y, wt, xm, offs, out):
             nc.vector.tensor_copy(w_codes[:, o, :], word_pairs[:, o, :])
 
         y_rest = tile([P, PACK - 1, N], F32, "y_rest", "table_words")
-        nc.sync.dma_start(y_rest[:, 0, :], y_rows[:, 1, :])
-        nc.sync.dma_start(y_rest[:, 1:, :], y_rows[:, pairs[1], :])
+        for j in range(1, PACK):
+            nc.sync.dma_start(y_rest[:, j - 1, :], y_rows[:, j, :])
         signs = [after_scales[:, PAIR * R :]] + [y_rest[:, j, :] for j in range(PACK - 1)]
 
         low_codes = tile([P, PAIR * P], U32, "low_codes")
-        high_codes = laid_tile([P, PAIR * P], U32, "high_codes", head + 1024)
+        third_codes = laid_tile([P, P], U32, "third_codes", head + 1024)
         last_codes = tile([P, R], U32, "last_codes")
-        x_codes = [[t[:, cols] for t in (low_codes, high_codes) for cols in quarters[:PAIR]], [last_codes[:, cols] for cols in quarters]]
         x_planes = [tile([P, R], U8, "x_plane%d" % o) for o in range(PASSES)]
         x_woven = [[laid_tile([P, PAIR, P, PACK], BF16, "x_woven0_0", head - 1024)[:], tile([P, PAIR, P, PACK], BF16, "x_woven0_1")[:]]]
-        last_share = tile([P, PAIR, P, PACK], BF16, "x_woven1_1")[:]
+        last_share = laid_tile([P, PAIR, P, PACK], BF16, "x_woven1_1", head + 2048)[:]
         x_woven.append([laid_tile([P, PAIR, P, PACK], BF16, "x_woven1_0", head - 1024)[:], last_share])
 
         def weave_x(copy, o, e, places, raw):
@@ -142,13 +141,17 @@ def tile_attend_gsig_w_kernel(tc, xT, w_words, w_scales, y, wt, xm, offs, out):
         for places in range(PAIR):
             weave_x(nc.scalar.copy, 0, 1, pairs[places], x_raw[0][places])
         weave_x(nc.vector.tensor_copy, 0, 0, slice(0, PACK), x_first[:])
-        quantise_x(high_codes[:], 0, PAIR, PAIR)
+        quantise_x(third_codes[:], 0, PAIR, 1)
         quantise_x(low_codes[:], 0, 0, PAIR)
         for places in range(PAIR):
             weave_x(nc.vector.tensor_copy, 1, 0, pairs[places], x_raw[1][places])
             weave_x(nc.scalar.copy, 1, 1, pairs[places], x_raw[1][places])
         for j in range(PACK):
-            quantise_x(x_codes[1][j], 1, j, 1)
+            quantise_x(last_codes[:, quarters[j]], 1, j, 1)
+        fourth_codes = laid_tile([P, P], U32, "fourth_codes", head + 2048)
+        quantise_x(fourth_codes[:], 0, PACK - 1, 1)
+        first_pass = [low_codes[:, cols] for cols in quarters[:PAIR]] + [third_codes[:], fourth_codes[:]]
+        x_codes = [first_pass, [last_codes[:, cols] for cols in quarters]]
 
         xm_rows = xm[0].rearrange("(p t) c -> p t c", t=PACK)
         xm_first = tile([P, PACK, PAIR * P], F32, "xm_first", "x_first")
@@ -160,7 +163,7 @@ def tile_attend_gsig_w_kernel(tc, xT, w_words, w_scales, y, wt, xm, offs, out):
             nc.sync.dma_start(pair[:], xm_rows[:, :, k * PAIR * P : (k + 1) * PAIR * P])
             xm_raw.extend(pair[:, :, cols] for cols in quarters[:PAIR])
 
-        pieces = [(0, 0), (0, 1), (1, 0), (1, 1), (2, 0), (3, 0), (2, 1), (3, 1)]
+        pieces = [(j, h) for j in range(PACK) for h in range(PAIR)]
         scores = {piece: psum.tile([P, HALF], F32, name="scores", tag="bank%d" % b) for b, piece in enumerate(pieces)}
         for o in range(PASSES):
             for j, h in pieces:
@@ -181,8 +184,9 @@ def tile_attend_gsig_w_kernel(tc, xT, w_words, w_scales, y, wt, xm, offs, out):
             nc.gpsimd.tensor_scalar(factors[:, j, :], signs[j], negated[:, j : j + 1], 0.0, MULT, ADD)
         margin_words = tile([P, PACK * N], F32, "margin_words")
         margins = {piece: margin_words[:, b * HALF : (b + 1) * HALF] for b, piece in enumerate(pieces)}
+        margins[PAIR, 1] = margins[1, 1]
         sigmoids = [tile([P, PACK, HALF], F32, "sigmoids%d" % h) for h in range(PAIR)]
-        for j, h in pieces:
+        for j, h in pieces[:5] + [(3, 0), (3, 1), (2, 1)]:
             nc.vector.tensor_tensor(margins[j, h], scores[j, h][:], signs[j][:, halves[h]], MULT)
             nc.scalar.activation(sigmoids[h][:, j, :], margins[j, h], SIGMOID, scale=-1.0)
 

@@ -192,7 +192,8 @@ def tile_attend_gsig_w_kernel(tc, xT, w_words, w_scales, y, wt, xm, offs, out):
 
         g_codes = tile([P, N], U32, "g_codes")
         g_plane = tile([P, N], U8, "g_plane")
-        xm_codes = tile([P, D], U32, "xm_codes")
+        xm_words = tile([P, D], U32, "xm_words")
+        xm_codes = [xm_words[:, m * P : (m + 1) * P] for m in range(D_TILES)]
         xm_plane = tile([P, D], U8, "xm_plane")
 
         def form_g(woven, h, slots):
@@ -219,14 +220,14 @@ def tile_attend_gsig_w_kernel(tc, xT, w_words, w_scales, y, wt, xm, offs, out):
 
         def quantise_xm(first, count, woven):
             cols = slice(first * P, (first + count) * P)
-            nc.vector.quantize_mx(xm_codes[:, cols].bitcast(E4M3), xm_plane[:, cols], woven.rearrange("p c t -> p (c t)"))
+            nc.vector.quantize_mx(xm_codes[first].bitcast(E4M3), xm_plane[:, cols], woven.rearrange("p c t -> p (c t)"))
 
         def multiply(m, slots, b):
             bank = psum.tile([P, slots.stop - slots.start], F32, name="grad", tag="bank%d" % b)
             cols = slice(m * P, (m + 1) * P)
             nc.tensor.matmul_mx(
                 bank[:],
-                lhsT=xm_codes[:, cols].bitcast(E4M3),
+                lhsT=xm_codes[m].bitcast(E4M3),
                 lhsT_scale=xm_plane[:, cols],
                 rhs=g_codes[:, slots].bitcast(E5M2),
                 rhs_scale=g_plane[:, slots],
@@ -252,8 +253,8 @@ def tile_attend_gsig_w_kernel(tc, xT, w_words, w_scales, y, wt, xm, offs, out):
 
         one, line = P * PACK * 2, 64
         base = 3 * one
-        low_woven = [woven_view(margins[PACK - 1, h]) for h in range(PAIR)]
-        for m in range(PAIR):
+        low_woven = [woven_view(margins[piece]) for piece in ((3, 0), (3, 1), (2, 1))]
+        for m in range(len(low_woven)):
             nc.scalar.copy(*weave_views(m, low_woven[m]))
         for h in range(PAIR):
             g_woven = [laid_tile([P, P, PACK], BF16, "g_even%d" % h, base), laid_tile([P, P, PACK], BF16, "g_odd%d" % h, base - 2 * one)]
@@ -282,13 +283,14 @@ def tile_attend_gsig_w_kernel(tc, xT, w_words, w_scales, y, wt, xm, offs, out):
         def staging(m, offset):
             return laid_tile([P, N], F32, "columns%d" % m, offset)
 
-        for m, offset in ((2, base - one + line), (3, base - 2 * one)):
-            woven = laid_tile([P, P, PACK], BF16, "woven%d" % m, offset)
-            nc.vector.tensor_copy(*weave_views(m, woven[:]))
-            quantise_xm(m, 1, woven[:])
+        xm_codes[2] = laid_tile([P, P], U32, "held_codes", base - 2 * one)[:]
+        quantise_xm(2, 1, low_woven[2])
+        woven = laid_tile([P, P, PACK], BF16, "woven3", base - one - line)
+        nc.vector.tensor_copy(*weave_views(3, woven[:]))
+        quantise_xm(3, 1, woven[:])
         nc.vector.tensor_copy(first_columns[:, halves[1]], multiply(1, halves[1], 5)[:])
         vector_scatter(1, first_columns)
-        for m, places, banks in ((2, (base - 5 * one // 2, base - 3 * one // 2), (6, 7)), (4, (base - 2 * one, base - one), (0, 1))):
+        for m, places, banks in ((2, (base - 3 * one // 2, base - one // 2), (3, 7)), (4, (base - one, base), (0, 1))):
             even, odd = staging(m, (8 + m) * one), staging(m + 1, (12 + m) * one)
             nc.scalar.copy(even[:], multiply(m, whole, banks[0])[:])
             nc.scalar.copy(odd[:, halves[0]], multiply(m + 1, halves[0], banks[1])[:])
@@ -299,8 +301,10 @@ def tile_attend_gsig_w_kernel(tc, xT, w_words, w_scales, y, wt, xm, offs, out):
                 quantise_xm(m + 2 + k, 1, woven[:])
             nc.vector.tensor_copy(odd[:, halves[1]], multiply(m + 1, halves[1], banks[0])[:])
             vector_scatter(m + 1, odd)
-        even, odd = staging(6, 10 * one + line), staging(7, 14 * one - line)
-        nc.scalar.copy(even[:], multiply(6, whole, 2)[:])
-        nc.scalar.copy(odd[:], multiply(7, whole, 3)[:])
+        even, odd = staging(6, 12 * one), staging(7, 16 * one)
+        bank = multiply(6, whole, 2)
+        for slots in halves:
+            nc.scalar.copy(even[:, slots], bank[:, slots])
         scalar_scatter(nc.scalar, 6, even)
+        nc.vector.tensor_copy(odd[:], multiply(7, whole, 4)[:])
         vector_scatter(7, odd)

from contextlib import ExitStack

import concourse.mybir as mybir

N, T, D, R = 512, 2048, 1024, 512
FLOPS = 2 * 2 * N * D * R

F32 = mybir.dt.float32
BF16 = mybir.dt.bfloat16
I32 = mybir.dt.int32
U32 = mybir.dt.uint32
U16 = mybir.dt.uint16
U8 = mybir.dt.uint8
E4M3 = mybir.dt.float8_e4m3fn_x4
E5M2 = mybir.dt.float8_e5m2_x4
E2M1 = mybir.dt.float4_e2m1fn_x4
MULT = mybir.AluOpType.mult
ADD = mybir.AluOpType.add
COPY = mybir.ActivationFunctionType.Copy
SIGMOID = mybir.ActivationFunctionType.Sigmoid

P = 128
QUADRANT = 32
PACK = 4
PAIR = 2
K_PASS = P * PACK
PASSES = D // K_PASS
D_TILES = D // P
PER_COLUMN = 16
HALF = N // 2


def tile_attend_gsig_w_kernel(tc, xT, w_words, w_scales, y, wt, xm, offs, out):
    nc = tc.nc
    with ExitStack() as ctx:
        keep = ctx.enter_context(tc.tile_pool(name="keep", bufs=1))
        laid = ctx.enter_context(tc.tile_pool(name="laid", bufs=1))
        psum = ctx.enter_context(tc.psum_pool(name="psum", bufs=1))
        halves = [slice(0, HALF), slice(HALF, N)]
        quarters = [slice(c * P, (c + 1) * P) for c in range(N // P)]
        pairs = [slice(0, PAIR), slice(PAIR, PACK)]
        whole = slice(0, N)

        def tile(shape, dtype, name, tag=None):
            return keep.tile(shape, dtype, name=name, tag=tag or name, align_bytes=256)

        def laid_tile(shape, dtype, name, offset):
            return laid.tile(shape, dtype, name=name, align_bytes=64, offset=offset)

        def woven_view(words):
            return words.bitcast(BF16).rearrange("p (n j) -> p n j", j=PACK)

        offsets = keep.tile([P, N // PER_COLUMN], U16, name="offsets")
        weights = tile([P, PACK], F32, "weights")
        nc.scalar.dma_start(weights[:], wt[0].rearrange("(p j) o -> p (j o)", j=PACK))
        table_words = tile([P, T], I32, "table_words")
        words = w_words[0].rearrange("p t b -> p (t b)").bitcast(I32)
        table_scales = tile([P, T], U8, "table_scales")
        scale_rows = P - QUADRANT
        nc.sync.dma_start(table_scales[scale_rows:, :].bitcast(I32), w_scales.rearrange("o f t -> f o t").bitcast(I32))
        nc.sync.dma_start(offsets[:], offs)
        nc.sync.dma_start(table_words[:, : T // 2], words[:, : T // 2])
        nc.sync.dma_start(table_words[:, T // 2 :], words[:, T // 2 :])
        x_first = tile([P, PACK, R], F32, "x_first")
        x_third = tile([P, PAIR, R], F32, "x_third")
        x_rows = [xT[0, o * K_PASS : (o + 1) * K_PASS, :].rearrange("(p t) c -> p t c", t=PACK) for o in range(PASSES)]
        for places in pairs:
            nc.sync.dma_start(x_first[:, places, :], x_rows[0][:, places, :])
        nc.sync.dma_start(x_third[:], x_rows[1][:, pairs[0], :])

        warm_in = keep.tile([P, 1], F32, name="warm_in")
        warm = keep.tile([P, 1], F32, name="warm")
        ones = keep.tile([P, 1], F32, name="ones")
        nc.vector.memset(warm_in[:], 0.0)
        nc.vector.memset(ones[:], 1.0)
        nc.vector.memset(table_scales[:scale_rows, :].bitcast(I32), 0)
        planes = tile([P, PASSES * N], U8, "planes")
        nc.vector.memset(planes[:].bitcast(I32), 0)
        w_planes = [planes[:, o * N : (o + 1) * N] for o in range(PASSES)]
        nc.scalar.activation(warm[:], warm_in[:], SIGMOID)

        def zeroed_window(engine, tag):
            window = tile([P, T], F32, "window", tag)
            engine.memset(window[:].bitcast(I32), 0)
            return window

        windows = [zeroed_window(nc.vector, "window%d" % m) for m in range(PAIR)]
        negated = keep.tile([P, PACK], F32, name="negated")
        nc.vector.tensor_scalar(negated[:], weights[:], -1.0, 0.0, MULT, ADD)
        windows.append(zeroed_window(nc.vector, "window2"))
        windows.append(zeroed_window(nc.gpsimd, "weights"))

        picked_scales = tile([P, N], U8, "picked_scales")
        nc.vector.tensor_copy(picked_scales[:], table_scales[:].indirect(offsets[:]))

        rows_a_quadrant = PACK * PASSES
        for q in range(P // QUADRANT):
            first = scale_rows + q * rows_a_quadrant
            nc.sync.dma_start(
                planes[q * QUADRANT : q * QUADRANT + PACK, :].bitcast(I32),
                picked_scales[first : first + rows_a_quadrant, :].bitcast(I32),
            )
        y_rows = y[0].rearrange("(p j) n -> p j n", j=PACK)
        after_scales = tile([P, PAIR * R + N], F32, "after_scales", "table_scales")
        x_last = after_scales[:, : PAIR * R].rearrange("p (t c) -> p t c", t=PAIR)
        nc.sync.dma_start(x_last, x_rows[1][:, pairs[1], :])
        nc.sync.dma_start(after_scales[:, PAIR * R :], y_rows[:, 0, :])
        x_raw = [[x_first[:, places, :] for places in pairs], [x_third[:], x_last]]
        head = 20 * 1024
        picked_words = laid_tile([P, N], U32, "picked_words", head)
        nc.vector.tensor_copy(picked_words[:], table_words[:].bitcast(U32).indirect(offsets[:]))
        w_codes = tile([P, PASSES, N], U16, "w_codes")
        word_pairs = picked_words[:].bitcast(U16).rearrange("p (n o) -> p o n", o=PASSES)
        for o in range(PASSES):
            nc.vector.tensor_copy(w_codes[:, o, :], word_pairs[:, o, :])

        y_rest = tile([P, PACK - 1, N], F32, "y_rest", "table_words")
        for j in range(1, PACK):
            nc.sync.dma_start(y_rest[:, j - 1, :], y_rows[:, j, :])
        signs = [after_scales[:, PAIR * R :]] + [y_rest[:, j, :] for j in range(PACK - 1)]

        low_codes = tile([P, PAIR * P], U32, "low_codes")
        third_codes = laid_tile([P, P], U32, "third_codes", head + 1024)
        last_codes = tile([P, R], U32, "last_codes")
        x_planes = [tile([P, R], U8, "x_plane%d" % o) for o in range(PASSES)]
        x_woven = [[laid_tile([P, PAIR, P, PACK], BF16, "x_woven0_0", head - 1024)[:], tile([P, PAIR, P, PACK], BF16, "x_woven0_1")[:]]]
        last_share = laid_tile([P, PAIR, P, PACK], BF16, "x_woven1_1", head + 2048)[:]
        x_woven.append([laid_tile([P, PAIR, P, PACK], BF16, "x_woven1_0", head - 1024)[:], last_share])

        def weave_x(copy, o, e, places, raw):
            copy(
                x_woven[o][e].rearrange("p j s t -> p s t j")[:, :, places, :],
                raw.rearrange("p t (s j) -> p s t j", j=PACK)[:, :, :, pairs[e]],
            )

        def quantise_x(codes, o, first, count):
            cols = slice(first * P, (first + count) * P)
            woven = x_woven[o][first // PAIR][:, first % PAIR : first % PAIR + count, :, :]
            nc.vector.quantize_mx(codes.bitcast(E4M3), x_planes[o][:, cols], woven.rearrange("p j s t -> p (j s t)"))

        for places in range(PAIR):
            weave_x(nc.scalar.copy, 0, 1, pairs[places], x_raw[0][places])
        weave_x(nc.vector.tensor_copy, 0, 0, slice(0, PACK), x_first[:])
        quantise_x(third_codes[:], 0, PAIR, 1)
        quantise_x(low_codes[:], 0, 0, PAIR)
        for places in range(PAIR):
            weave_x(nc.vector.tensor_copy, 1, 0, pairs[places], x_raw[1][places])
            weave_x(nc.scalar.copy, 1, 1, pairs[places], x_raw[1][places])
        for j in range(PACK):
            quantise_x(last_codes[:, quarters[j]], 1, j, 1)
        fourth_codes = laid_tile([P, P], U32, "fourth_codes", head + 2048)
        quantise_x(fourth_codes[:], 0, PACK - 1, 1)
        first_pass = [low_codes[:, cols] for cols in quarters[:PAIR]] + [third_codes[:], fourth_codes[:]]
        x_codes = [first_pass, [last_codes[:, cols] for cols in quarters]]

        xm_rows = xm[0].rearrange("(p t) c -> p t c", t=PACK)
        xm_first = tile([P, PACK, PAIR * P], F32, "xm_first", "x_first")
        xm_second = tile([P, PACK, PAIR * P], F32, "xm_second", "x_third")
        xm_third = tile([P, PACK, PAIR * P], F32, "xm_third", "table_scales")
        xm_fourth = tile([P, PACK, PAIR * P], F32, "xm_fourth", "table_words")
        xm_raw = []
        for k, pair in enumerate((xm_first, xm_second, xm_third, xm_fourth)):
            nc.sync.dma_start(pair[:], xm_rows[:, :, k * PAIR * P : (k + 1) * PAIR * P])
            xm_raw.extend(pair[:, :, cols] for cols in quarters[:PAIR])

        pieces = [(j, h) for j in range(PACK) for h in range(PAIR)]
        scores = {piece: psum.tile([P, HALF], F32, name="scores", tag="bank%d" % b) for b, piece in enumerate(pieces)}
        for o in range(PASSES):
            for j, h in pieces:
                nc.tensor.matmul_mx(
                    scores[j, h][:],
                    lhsT=x_codes[o][j].bitcast(E4M3),
                    lhsT_scale=x_planes[o][:, quarters[j]],
                    rhs=w_codes[:, o, halves[h]].bitcast(E2M1),
                    rhs_scale=w_planes[o][:, halves[h]],
                    start=(o == 0),
                    stop=(o == PASSES - 1),
                )

        factors = tile([P, PACK, N], F32, "factors")
        for j in range(PAIR):
            nc.scalar.activation(factors[:, j, :], signs[j], COPY, scale=negated[:, j : j + 1])
        for j in range(PAIR, PACK):
            nc.gpsimd.tensor_scalar(factors[:, j, :], signs[j], negated[:, j : j + 1], 0.0, MULT, ADD)
        margin_words = tile([P, PACK * N], F32, "margin_words")
        margins = {piece: margin_words[:, b * HALF : (b + 1) * HALF] for b, piece in enumerate(pieces)}
        margins[PAIR, 1] = margins[1, 1]
        sigmoids = [tile([P, PACK, HALF], F32, "sigmoids%d" % h) for h in range(PAIR)]
        for j, h in pieces[:5] + [(3, 0), (3, 1), (2, 1)]:
            nc.vector.tensor_tensor(margins[j, h], scores[j, h][:], signs[j][:, halves[h]], MULT)
            nc.scalar.activation(sigmoids[h][:, j, :], margins[j, h], SIGMOID, scale=-1.0)

        g_codes = tile([P, N], U32, "g_codes")
        g_plane = tile([P, N], U8, "g_plane")
        xm_words = tile([P, D], U32, "xm_words")
        xm_codes = [xm_words[:, m * P : (m + 1) * P] for m in range(D_TILES)]
        xm_plane = tile([P, D], U8, "xm_plane")

        def form_g(woven, h, slots):
            nc.vector.tensor_tensor(
                woven.rearrange("p (c i) j -> p c j i", i=PAIR),
                sigmoids[h][:, :, slots].rearrange("p j (c i) -> p c j i", i=PAIR),
                factors[:, :, halves[h]][:, :, slots].rearrange("p j (c i) -> p c j i", i=PAIR),
                MULT,
            )

        def quantise_g(slots, woven):
            nc.vector.quantize_mx(g_codes[:, slots].bitcast(E5M2), g_plane[:, slots], woven.rearrange("p n j -> p (n j)"))

        def weave_views(m, woven):
            return (
                woven.rearrange("p (c i) t -> p c t i", i=PACK),
                xm_raw[m].rearrange("p t (c i) -> p c t i", i=PACK),
            )

        def gpsimd_weave(first, count, woven):
            for k in range(count):
                raw = xm_raw[first + k].rearrange("p t c -> p c t")
                nc.gpsimd.tensor_scalar(woven[:, quarters[k], :], raw, 1.0, 0.0, MULT, ADD)

        def quantise_xm(first, count, woven):
            cols = slice(first * P, (first + count) * P)
            nc.vector.quantize_mx(xm_codes[first].bitcast(E4M3), xm_plane[:, cols], woven.rearrange("p c t -> p (c t)"))

        def multiply(m, slots, b):
            bank = psum.tile([P, slots.stop - slots.start], F32, name="grad", tag="bank%d" % b)
            cols = slice(m * P, (m + 1) * P)
            nc.tensor.matmul_mx(
                bank[:],
                lhsT=xm_codes[m].bitcast(E4M3),
                lhsT_scale=xm_plane[:, cols],
                rhs=g_codes[:, slots].bitcast(E5M2),
                rhs_scale=g_plane[:, slots],
                start=True,
                stop=True,
            )
            return bank

        window_of = [m % len(windows) for m in range(D_TILES)]

        def listed(m, slots):
            return windows[window_of[m]][:].indirect(offsets[:, slots.start // PER_COLUMN : slots.stop // PER_COLUMN])

        def store(queue, m):
            queue.dma_start(out[m * P : (m + 1) * P, :], windows[window_of[m]][:])

        staged = 4 * N
        scalar_base = 4 * staged
        first_staged = laid_tile([P, N], F32, "first_staged", scalar_base)

        def scalar_half(m, h, columns):
            nc.scalar.activation(listed(m, halves[h]), columns[:, halves[h]], COPY)

        one, line = P * PACK * 2, 64
        base = 3 * one
        low_woven = [woven_view(margins[piece]) for piece in ((3, 0), (3, 1), (2, 1))]
        for m in range(len(low_woven)):
            nc.scalar.copy(*weave_views(m, low_woven[m]))
        for h in range(PAIR):
            g_woven = [laid_tile([P, P, PACK], BF16, "g_even%d" % h, base), laid_tile([P, P, PACK], BF16, "g_odd%d" % h, base - 2 * one)]
            for c in range(PAIR):
                form_g(g_woven[c][:], h, quarters[c])
            quantise_xm(h, 1, low_woven[h])
            for c in range(PAIR):
                quantise_g(quarters[PAIR * h + c], g_woven[c][:])
            copy = nc.scalar.copy if h == 0 else nc.vector.tensor_copy
            for c in range(PAIR * h, PAIR * (h + 1)):
                copy(first_staged[:, quarters[c]], multiply(0, quarters[c], c)[:])
            if h == 1:
                first_columns = laid_tile([P, N], F32, "first_columns", base + one - line)
                nc.scalar.copy(first_columns[:, halves[0]], multiply(1, halves[0], 4)[:])
            scalar_half(0, h, first_staged)
        store(nc.sync, 0)

        def scalar_scatter(queue, m, columns):
            nc.scalar.activation(listed(m, whole), columns[:], COPY, scale=ones[:])
            store(queue, m)

        def vector_scatter(m, columns):
            nc.vector.tensor_copy(listed(m, whole), columns[:])
            store(nc.sync, m)

        def staging(m, offset):
            return laid_tile([P, N], F32, "columns%d" % m, offset)

        xm_codes[2] = laid_tile([P, P], U32, "held_codes", base - 2 * one)[:]
        quantise_xm(2, 1, low_woven[2])
        woven = laid_tile([P, P, PACK], BF16, "woven3", base - one - line)
        nc.vector.tensor_copy(*weave_views(3, woven[:]))
        quantise_xm(3, 1, woven[:])
        nc.vector.tensor_copy(first_columns[:, halves[1]], multiply(1, halves[1], 5)[:])
        vector_scatter(1, first_columns)
        for m, places, banks in ((2, (base - 3 * one // 2, base - one // 2), (3, 7)), (4, (base - one, base), (0, 1))):
            even, odd = staging(m, (8 + m) * one), staging(m + 1, (12 + m) * one)
            nc.scalar.copy(even[:], multiply(m, whole, banks[0])[:])
            nc.scalar.copy(odd[:, halves[0]], multiply(m + 1, halves[0], banks[1])[:])
            scalar_scatter(nc.sync, m, even)
            for k in range(PAIR):
                woven = laid_tile([P, P, PACK], BF16, "woven%d" % (m + 2 + k), places[k])
                gpsimd_weave(m + 2 + k, 1, woven[:])
                quantise_xm(m + 2 + k, 1, woven[:])
            nc.vector.tensor_copy(odd[:, halves[1]], multiply(m + 1, halves[1], banks[0])[:])
            vector_scatter(m + 1, odd)
        even, odd = staging(6, 12 * one), staging(7, 16 * one)
        bank = multiply(6, whole, 2)
        for slots in halves:
            nc.scalar.copy(even[:, slots], bank[:, slots])
        scalar_scatter(nc.scalar, 6, even)
        nc.vector.tensor_copy(odd[:], multiply(7, whole, 4)[:])
        vector_scatter(7, odd)
